import numpy as np
import ml_dtypes


def mxq(x, axis, fmt="e4m3"):
    dtype, down = {"e4m3": (ml_dtypes.float8_e4m3fn, 7), "e5m2": (ml_dtypes.float8_e5m2, 14)}[fmt]
    v = np.moveaxis(np.asarray(x, np.float32).astype(ml_dtypes.bfloat16).astype(np.float64), axis, -1)
    blocks = v.reshape(v.shape[:-1] + (-1, 32))
    amax = np.abs(blocks).max(-1, keepdims=True)
    byte = np.maximum(np.where(amax > 0, np.frexp(amax)[1] - 1 + 127, 0) - down, 1)
    scale = np.exp2(byte - 127.0)
    codes = (blocks / scale).astype(np.float32).astype(dtype).astype(np.float64)
    return np.moveaxis((codes * scale).reshape(v.shape), -1, axis)


WIDE = False


def mx_kscale(k):
    if not WIDE:
        return np.ones(k)
    levels = np.array([10, -10, 5, -5, 0])
    if k % 512:
        return np.exp2(np.random.permutation(np.resize(levels, k // 32))).repeat(32)
    a = np.empty((k // 512, 16))
    for p in range(k // 512):
        a[p, :8] = np.random.permutation(np.resize(levels, 8))
        for g in range(8):
            far = levels[np.abs(levels - a[p, g]) >= 10]
            a[p, g + 8] = far[np.random.randint(len(far))]
    return np.exp2(a.ravel()).repeat(32)


def f64(x):
    return np.asarray(x).astype(np.float64)


def striped(idx):
    return np.tile(np.asarray(idx).reshape(-1, 16).T, (8, 1)).astype(np.uint16)


def unstriped(offs):
    return offs[:16].T.reshape(-1).astype(np.int64)


E2M1 = np.array([0.0, 0.5, 1.0, 1.5, 2.0, 3.0, 4.0, 6.0, -0.0, -0.5, -1.0, -1.5, -2.0, -3.0, -4.0, -6.0])


def pack_weight(w, fmt):
    k, n = w.shape
    w = f64(np.asarray(w, np.float32).astype(ml_dtypes.bfloat16)).reshape(k // 32, 32, n)
    amax = np.abs(w).max(1)
    if fmt == "e4m3":
        byte = np.frexp(amax)[1] - 1 + 127 - 7
    else:
        mant, ex = np.frexp(amax / 6.0)
        byte = np.where(mant > 0.5, ex, ex - 1) + 127
    byte = np.clip(np.where(amax > 0, byte, 1), 1, 254)
    scaled = (w * np.exp2(127.0 - byte)[:, None, :]).reshape(k, n).astype(np.float32)
    by_word = np.ascontiguousarray(scaled.reshape(k // 512, 128, 4, n).transpose(0, 1, 3, 2))
    if fmt == "e4m3":
        words = by_word.astype(ml_dtypes.float8_e4m3fn).view(np.uint8)
    else:
        c = by_word.astype(ml_dtypes.float4_e2m1fn).view(np.uint8) & 0xF
        words = (c[..., 0::2] | (c[..., 1::2] << 4)).reshape(k // 512, 128, 2 * n)
    return np.ascontiguousarray(words), np.ascontiguousarray(byte.astype(np.uint8).reshape(k // 512, 16, n))


def unpack_weight(words, scales, fmt):
    g, _, n = scales.shape
    words = np.ascontiguousarray(words).reshape(g, 128, n, -1)
    if fmt == "e4m3":
        vals = words.view(ml_dtypes.float8_e4m3fn).astype(np.float64)
    else:
        nib = np.empty((g, 128, n, 4), np.uint8)
        nib[..., 0::2] = words & 0xF
        nib[..., 1::2] = words >> 4
        vals = E2M1[nib]
    vals = vals * np.repeat(np.exp2(scales.astype(np.float64) - 127.0), 8, axis=1)[..., None]
    return vals.transpose(0, 1, 3, 2).reshape(g * 512, n)


B, N, T, D, DV, NQ = 1, 1024, 2048, 1024, 128, 256
CAP = 2.0
DRAFT = 128


def setup_inputs():
    n = np.random.standard_normal
    idx = np.random.permutation(T)[:B * N]
    s = mx_kscale(D)[:, None]
    u = np.ones(T)
    u[idx] = mx_kscale(B * N)
    r = np.random.uniform(0.5, 2.0, T)
    qp = [pack_weight(x, "e4m3") for x in n((B, D, NQ)) * s * (1.00 / np.sqrt(D))]
    k = n((D, T)) / s
    v = n((DV, T)) / (u * r)
    kp = pack_weight(k, "e2m1")
    when = np.zeros(T)
    when[idx] = np.concatenate([np.concatenate([np.arange(N - DRAFT), N - DRAFT + np.random.randint(0, 16, DRAFT)]) for b in range(B)])
    return {
        "q_words": np.stack([x[0] for x in qp]),
        "q_scales": np.stack([x[1] for x in qp]),
        "k_words": np.ascontiguousarray(kp[0].reshape(D // 1024, 2, 128, T, 2).transpose(0, 2, 3, 1, 4)).reshape(D // 1024, 128, T, 4),
        "k_scales": kp[1],
        "vT": v.astype(np.float32),
        "vs": np.tile(u * r, (128, 1)).astype(np.float32),
        "pos": np.tile(when, (128, 1)).astype(np.float32),
        "qpos": np.random.randint(N - DRAFT, N - DRAFT + 16, (B, NQ, 1)).astype(np.float32),
        "offs": striped(idx),
    }


def reference(q_words, q_scales, k_words, k_scales, vT, vs, pos, qpos, offs):
    idx = unstriped(offs)
    k = unpack_weight(k_words.reshape(D // 1024, 128, T, 2, 2).transpose(0, 3, 1, 2, 4).reshape(D // 512, 128, 2 * T), k_scales, "e2m1")
    v = f64(vT)
    pick = lambda x: x[:, idx].reshape(x.shape[0], B, N).transpose(1, 0, 2)
    q = np.stack([unpack_weight(q_words[b], q_scales[b], "e4m3") for b in range(B)])
    score = q.transpose(0, 2, 1) @ pick(k)
    score = CAP * np.tanh(score / CAP)
    score = np.where(pick(f64(pos))[:, :1, :] <= f64(qpos), score, -30000.0)
    m = score.max(-1, keepdims=True)
    p = np.exp(score - m)
    total = p.sum(-1, keepdims=True)
    w = p * pick(f64(vs))[:, :1, :]
    y = mxq(w, 2, "e4m3") @ mxq(pick(v).transpose(0, 2, 1), 1, "e4m3")
    y = y / total
    return y

@@ -1,0 +1,176 @@
+from contextlib import ExitStack
+
+import concourse.mybir as mybir
+from concourse.masks import make_identity
+
+N, T, D, DV, NQ = 1024, 2048, 1024, 128, 256
+CAP = 2.0
+FLOPS = 2 * NQ * N * (D + DV)
+
+F32 = mybir.dt.float32
+BF16 = mybir.dt.bfloat16
+I32 = mybir.dt.int32
+U32 = mybir.dt.uint32
+U16 = mybir.dt.uint16
+U8 = mybir.dt.uint8
+FP8X4 = mybir.dt.float8_e4m3fn_x4
+FP4X4 = mybir.dt.float4_e2m1fn_x4
+ACT = mybir.ActivationFunctionType
+ALU = mybir.AluOpType
+
+P = 128
+PASS = 512
+FLOOR = 2.0**-100
+
+
+def tile_attend_soft_draft_cap_topkq256n1024t2048_kernel(tc, q_words, q_scales, k_words, k_scales, vT, vs, pos, qpos, offs, out):
+    nc = tc.nc
+    with ExitStack() as ctx:
+        sb = ctx.enter_context(tc.tile_pool(name="sb", bufs=1))
+        ps = ctx.enter_context(tc.psum_pool(name="ps", bufs=1))
+
+        offsets = sb.tile([P, N // 16], U16, name="offsets")
+        nc.sync.dma_start(offsets[:], offs)
+
+        ks_pool = sb.tile([P, T], U8, name="ks_pool", align_bytes=64)
+        nc.sync.dma_start(ks_pool[0:32, :].bitcast(I32), k_scales.rearrange("o f t -> f o t").bitcast(I32))
+        q_place = sb.tile([P, 2], F32, name="q_place")
+        with nc.allow_non_contiguous_dma(reason="one place a partition"):
+            nc.scalar.dma_start(q_place[:], qpos[0].rearrange("(j p) o -> p (j o)", p=P))
+        k_scale = sb.tile([P, 2, N], U8, name="k_scale", align_bytes=64)
+        q_scale = sb.tile([P, 2, NQ], U8, name="q_scale", align_bytes=64)
+        warm = sb.tile([P, 1], F32, name="warm")
+        warm_out = sb.tile([P, 1], F32, name="warm_out")
+        nc.vector.memset(warm[:], 0.0)
+        nc.vector.memset(ks_pool[32:64, :].bitcast(I32), 0)
+        nc.vector.memset(ks_pool[64:128, :].bitcast(I32), 0)
+        nc.gpsimd.memset(q_scale[:].bitcast(I32), 0)
+        nc.vector.memset(k_scale[:].bitcast(I32), 0)
+        nc.scalar.activation(warm_out[:], warm[:], ACT.Exp)
+
+        kw_pool = sb.tile([P, T], I32, name="kw_pool", align_bytes=64)
+        nc.sync.dma_start(kw_pool[:], k_words[0].rearrange("p t b -> p (t b)").bitcast(I32))
+        q_code = sb.tile([P, 2, NQ], I32, name="q_code", align_bytes=64)
+        nc.sync.dma_start(q_code[:], q_words[0].rearrange("o p q r -> p o (q r)").bitcast(I32))
+        v_pool = sb.tile([P, T], F32, name="v_pool")
+        nc.sync.dma_start(v_pool[:], vT)
+        pos_pool = sb.tile([P, T], F32, name="pos_pool")
+        nc.sync.dma_start(pos_pool[:], pos)
+        vs_pool = sb.tile([P, T], F32, name="vs_pool")
+        nc.sync.dma_start(vs_pool[:], vs)
+
+        for quad in range(4):
+            nc.gpsimd.dma_start(
+                q_scale[32 * quad : 32 * quad + 4, :, :].bitcast(I32),
+                q_scales[0, :, 4 * quad : 4 * quad + 4, :].rearrange("o f q -> f o q").bitcast(I32),
+            )
+        ident = sb.tile([P, P], F32, name="ident")
+        make_identity(nc, ident[:])
+
+        ks_slots = sb.tile([P, N], U8, name="ks_slots", align_bytes=64)
+        nc.vector.tensor_copy(ks_slots[:], ks_pool[:].indirect(offsets[:]))
+        for quad in range(4):
+            nc.scalar.dma_start(
+                k_scale[32 * quad : 32 * quad + 4, :, :].bitcast(I32),
+                ks_slots[8 * quad : 8 * quad + 8, :].bitcast(I32),
+            )
+        kw = sb.tile([P, N], U32, name="kw", align_bytes=64)
+        nc.vector.tensor_copy(kw[:], kw_pool[:].bitcast(U32).indirect(offsets[:]))
+        k_code = sb.tile([P, 2, N], U16, name="k_code", align_bytes=64)
+        nc.vector.tensor_copy(k_code[:], kw[:].bitcast(U16).rearrange("p (n o) -> p o n", o=2))
+
+        v_bf = sb.tile([P, T], BF16, name="v_bf", align_bytes=64)
+        nc.scalar.activation(v_bf[:], v_pool[:], ACT.Copy)
+
+        pos_slots = sb.tile([P, N], F32, name="pos_slots")
+        nc.vector.tensor_copy(pos_slots[:], pos_pool[:].indirect(offsets[:]))
+
+        grown = []
+        for j in range(2):
+            capped = sb.tile([P, N], F32, name=f"capped{j}", tag=f"capped{j}", align_bytes=64)
+            for h in range(2):
+                bank = ps.tile([P, PASS], F32, name=f"score{j}{h}", tag=f"score{j}{h}")
+                for o in range(2):
+                    nc.tensor.matmul_mx(
+                        out=bank[:],
+                        lhsT=q_code[:, o, j * P : (j + 1) * P].bitcast(FP8X4),
+                        lhsT_scale=q_scale[:, o, j * P : (j + 1) * P],
+                        rhs=k_code[:, o, h * PASS : (h + 1) * PASS].bitcast(FP4X4),
+                        rhs_scale=k_scale[:, o, h * PASS : (h + 1) * PASS],
+                        start=(o == 0),
+                        stop=(o == 1),
+                    )
+                nc.scalar.activation(capped[:, h * PASS : (h + 1) * PASS], bank[:], ACT.Tanh, scale=1.0 / CAP)
+            e = sb.tile([P, N], F32, name=f"grown{j}")
+            nc.scalar.activation(e[:], capped[:], ACT.Exp, scale=CAP)
+            grown.append(e)
+
+        v_slots = sb.tile([P, N], BF16, name="v_slots", tag="capped1", align_bytes=64)
+        nc.scalar.activation(v_slots[:], v_bf[:].indirect(offsets[:]), ACT.Copy)
+        vs_slots = sb.tile([P, N], F32, name="vs_slots")
+        nc.vector.tensor_copy(vs_slots[:], vs_pool[:].indirect(offsets[:]))
+
+        def turn(src, bank, dst):
+            words = src.bitcast(F32)
+            for u in range(2):
+                nc.tensor.transpose(bank[:, u, :], words[:, u::2], ident[:])
+            nc.scalar.copy(dst.bitcast(F32).rearrange("p (c u) -> p c u", u=2), bank.rearrange("p u c -> p c u"))
+
+        def quantise(src, name):
+            cols = src.shape[1] // 4
+            codes = sb.tile([P, cols], U32, name=name + "_code", align_bytes=64)
+            scales = sb.tile([P, cols], U8, name=name + "_scale", align_bytes=64)
+            nc.vector.quantize_mx(out=codes[:].bitcast(FP8X4), scales=scales[:], in_=src)
+            return codes, scales
+
+        v_turned = sb.tile([P, 2 * 4 * DV], BF16, name="v_turned", align_bytes=64)
+        for g in range(2):
+            v_bank = ps.tile([P, 2, DV], F32, name=f"v_bank{g}")
+            turn(v_slots[:, g * PASS : (g + 1) * PASS], v_bank[:], v_turned[:, g * PASS : (g + 1) * PASS])
+
+        weights = []
+        factors = []
+        for j in range(2):
+            seen = sb.tile([P, N], F32, name=f"seen{j}")
+            total = sb.tile([P, 1], F32, name=f"total{j}")
+            nc.vector.scalar_tensor_tensor(seen[:], pos_slots[:], q_place[:, j : j + 1], grown[j][:], ALU.is_le, ALU.mult, accum_out=total[:])
+            floored = sb.tile([P, N], F32, name=f"floored{j}")
+            top = sb.tile([P, 1], F32, name=f"top{j}")
+            nc.vector.tensor_scalar(floored[:], seen[:], FLOOR, None, ALU.max, ALU.max, accum_out=top[:])
+            inv_top = sb.tile([P, 1], F32, name=f"inv_top{j}")
+            nc.vector.reciprocal(inv_top[:], top[:])
+            total_f = sb.tile([P, 1], F32, name=f"total_f{j}")
+            nc.vector.tensor_scalar(total_f[:], total[:], N * FLOOR, None, ALU.add)
+            halves = []
+            for g in range(2):
+                w = sb.tile([P, PASS], BF16, name=f"w{j}{g}", align_bytes=64)
+                cols = slice(g * PASS, (g + 1) * PASS)
+                nc.vector.scalar_tensor_tensor(w[:], floored[:, cols], inv_top[:], vs_slots[:, cols], ALU.mult, ALU.mult)
+                bank = ps.tile([P, 2, P], F32, name=f"w_bank{j}{g}", tag=f"score{j}{g}")
+                turned = sb.tile([P, PASS], BF16, name=f"w_turned{j}{g}", align_bytes=64)
+                turn(w[:], bank[:], turned[:])
+                halves.append(turned)
+            inv_total = sb.tile([P, 1], F32, name=f"inv_total{j}")
+            nc.vector.reciprocal(inv_total[:], total_f[:])
+            factor = sb.tile([P, 1], F32, name=f"factor{j}")
+            nc.vector.tensor_tensor(factor[:], inv_total[:], top[:], ALU.mult)
+            weights.append(halves)
+            factors.append(factor)
+
+        v_code, v_scale = quantise(v_turned[:], "v")
+        for j in range(2):
+            acc = ps.tile([P, DV], F32, name=f"acc{j}")
+            for g in range(2):
+                w_code, w_scale = quantise(weights[j][g][:], f"wq{j}{g}")
+                nc.tensor.matmul_mx(
+                    out=acc[:],
+                    lhsT=w_code[:].bitcast(FP8X4),
+                    lhsT_scale=w_scale[:],
+                    rhs=v_code[:, g * DV : (g + 1) * DV].bitcast(FP8X4),
+                    rhs_scale=v_scale[:, g * DV : (g + 1) * DV],
+                    start=(g == 0),
+                    stop=(g == 1),
+                )
+            result = sb.tile([P, DV], F32, name=f"result{j}")
+            nc.scalar.activation(result[:], acc[:], ACT.Copy, scale=factors[j][:])
+            nc.sync.dma_start(out[0, j * P : (j + 1) * P, :], result[:])

@@ -32,56 +32,56 @@ def tile_attend_soft_draft_cap_topkq256n1024t2048_kernel(tc, q_words, q_scales, 
         offsets = sb.tile([P, N // 16], U16, name="offsets")
         nc.sync.dma_start(offsets[:], offs)
 
-        ks_pool = sb.tile([P, T], U8, name="ks_pool", align_bytes=64)
+        ks_pool = sb.tile([P, T], U8, name="ks_pool", tag="ks_then_pos", align_bytes=64)
         nc.sync.dma_start(ks_pool[0:32, :].bitcast(I32), k_scales.rearrange("o f t -> f o t").bitcast(I32))
+        kw_pool = sb.tile([P, T], I32, name="kw_pool", tag="kw_then_vs", align_bytes=64)
+        nc.sync.dma_start(kw_pool[:], k_words[0].rearrange("p t b -> p (t b)").bitcast(I32))
+
+        q_scale = sb.tile([P, 2, NQ], U8, name="q_scale", align_bytes=64)
+        nc.gpsimd.memset(q_scale[:].bitcast(I32), 0)
+        for quad in range(4):
+            nc.sync.dma_start(
+                q_scale[32 * quad : 32 * quad + 4, :, :].bitcast(I32),
+                q_scales[0, :, 4 * quad : 4 * quad + 4, :].rearrange("o f q -> f o q").bitcast(I32),
+            )
+        q_code = sb.tile([P, 2, NQ], I32, name="q_code", align_bytes=64)
+        nc.sync.dma_start(q_code[:], q_words[0].rearrange("o p q r -> p o (q r)").bitcast(I32))
+        v_pool = sb.tile([P, T], F32, name="v_pool")
+        nc.sync.dma_start(v_pool[:], vT)
         q_place = sb.tile([P, 2], F32, name="q_place")
         with nc.allow_non_contiguous_dma(reason="one place a partition"):
-            nc.scalar.dma_start(q_place[:], qpos[0].rearrange("(j p) o -> p (j o)", p=P))
+            nc.gpsimd.dma_start(q_place[:], qpos[0].rearrange("(j p) o -> p (j o)", p=P))
+        ident = sb.tile([P, P], F32, name="ident")
+        make_identity(nc, ident[:])
+
         k_scale = sb.tile([P, 2, N], U8, name="k_scale", align_bytes=64)
-        q_scale = sb.tile([P, 2, NQ], U8, name="q_scale", align_bytes=64)
         warm = sb.tile([P, 1], F32, name="warm")
         warm_out = sb.tile([P, 1], F32, name="warm_out")
         nc.vector.memset(warm[:], 0.0)
         nc.vector.memset(ks_pool[32:64, :].bitcast(I32), 0)
         nc.vector.memset(ks_pool[64:128, :].bitcast(I32), 0)
-        nc.gpsimd.memset(q_scale[:].bitcast(I32), 0)
         nc.vector.memset(k_scale[:].bitcast(I32), 0)
         nc.scalar.activation(warm_out[:], warm[:], ACT.Exp)
-
-        kw_pool = sb.tile([P, T], I32, name="kw_pool", align_bytes=64)
-        nc.sync.dma_start(kw_pool[:], k_words[0].rearrange("p t b -> p (t b)").bitcast(I32))
-        q_code = sb.tile([P, 2, NQ], I32, name="q_code", align_bytes=64)
-        nc.sync.dma_start(q_code[:], q_words[0].rearrange("o p q r -> p o (q r)").bitcast(I32))
-        v_pool = sb.tile([P, T], F32, name="v_pool")
-        nc.sync.dma_start(v_pool[:], vT)
-        pos_pool = sb.tile([P, T], F32, name="pos_pool")
-        nc.sync.dma_start(pos_pool[:], pos)
-        vs_pool = sb.tile([P, T], F32, name="vs_pool")
-        nc.sync.dma_start(vs_pool[:], vs)
-
-        for quad in range(4):
-            nc.gpsimd.dma_start(
-                q_scale[32 * quad : 32 * quad + 4, :, :].bitcast(I32),
-                q_scales[0, :, 4 * quad : 4 * quad + 4, :].rearrange("o f q -> f o q").bitcast(I32),
-            )
-        ident = sb.tile([P, P], F32, name="ident")
-        make_identity(nc, ident[:])
 
         ks_slots = sb.tile([P, N], U8, name="ks_slots", align_bytes=64)
         nc.vector.tensor_copy(ks_slots[:], ks_pool[:].indirect(offsets[:]))
         for quad in range(4):
-            nc.scalar.dma_start(
+            nc.sync.dma_start(
                 k_scale[32 * quad : 32 * quad + 4, :, :].bitcast(I32),
                 ks_slots[8 * quad : 8 * quad + 8, :].bitcast(I32),
             )
+        pos_pool = sb.tile([P, T], F32, name="pos_pool", tag="ks_then_pos", align_bytes=64)
+        nc.sync.dma_start(pos_pool[:], pos)
         kw = sb.tile([P, N], U32, name="kw", align_bytes=64)
         nc.vector.tensor_copy(kw[:], kw_pool[:].bitcast(U32).indirect(offsets[:]))
+        vs_pool = sb.tile([P, T], F32, name="vs_pool", tag="kw_then_vs", align_bytes=64)
+        nc.sync.dma_start(vs_pool[:], vs)
         k_code = sb.tile([P, 2, N], U16, name="k_code", align_bytes=64)
         nc.vector.tensor_copy(k_code[:], kw[:].bitcast(U16).rearrange("p (n o) -> p o n", o=2))
 
+
         v_bf = sb.tile([P, T], BF16, name="v_bf", align_bytes=64)
         nc.scalar.activation(v_bf[:], v_pool[:], ACT.Copy)
-
         pos_slots = sb.tile([P, N], F32, name="pos_slots")
         nc.vector.tensor_copy(pos_slots[:], pos_pool[:].indirect(offsets[:]))
 
@@ -116,11 +116,10 @@ def tile_attend_soft_draft_cap_topkq256n1024t2048_kernel(tc, q_words, q_scales, 
                 nc.tensor.transpose(bank[:, u, :], words[:, u::2], ident[:])
             nc.scalar.copy(dst.bitcast(F32).rearrange("p (c u) -> p c u", u=2), bank.rearrange("p u c -> p c u"))
 
-        def quantise(src, name):
+        def quantise(src, codes, name):
             cols = src.shape[1] // 4
-            codes = sb.tile([P, cols], U32, name=name + "_code", align_bytes=64)
             scales = sb.tile([P, cols], U8, name=name + "_scale", align_bytes=64)
-            nc.vector.quantize_mx(out=codes[:].bitcast(FP8X4), scales=scales[:], in_=src)
+            nc.vector.quantize_mx(out=codes.bitcast(FP8X4), scales=scales[:], in_=src)
             return codes, scales
 
         v_turned = sb.tile([P, 2 * 4 * DV], BF16, name="v_turned", align_bytes=64)
@@ -129,42 +128,41 @@ def tile_attend_soft_draft_cap_topkq256n1024t2048_kernel(tc, q_words, q_scales, 
             turn(v_slots[:, g * PASS : (g + 1) * PASS], v_bank[:], v_turned[:, g * PASS : (g + 1) * PASS])
 
         weights = []
-        factors = []
+        totals = sb.tile([P, 2], F32, name="totals")
+        inv_tops = sb.tile([P, 2], F32, name="inv_tops")
         for j in range(2):
-            seen = sb.tile([P, N], F32, name=f"seen{j}")
-            total = sb.tile([P, 1], F32, name=f"total{j}")
-            nc.vector.scalar_tensor_tensor(seen[:], pos_slots[:], q_place[:, j : j + 1], grown[j][:], ALU.is_le, ALU.mult, accum_out=total[:])
+            seen = sb.tile([P, N], F32, name=f"seen{j}", tag=["kw_then_vs", "seen1"][j], align_bytes=64)
+            nc.vector.scalar_tensor_tensor(seen[:], pos_slots[:], q_place[:, j : j + 1], grown[j][:], ALU.is_le, ALU.mult, accum_out=totals[:, j : j + 1])
             floored = sb.tile([P, N], F32, name=f"floored{j}")
             top = sb.tile([P, 1], F32, name=f"top{j}")
             nc.vector.tensor_scalar(floored[:], seen[:], FLOOR, None, ALU.max, ALU.max, accum_out=top[:])
-            inv_top = sb.tile([P, 1], F32, name=f"inv_top{j}")
-            nc.vector.reciprocal(inv_top[:], top[:])
-            total_f = sb.tile([P, 1], F32, name=f"total_f{j}")
-            nc.vector.tensor_scalar(total_f[:], total[:], N * FLOOR, None, ALU.add)
+            nc.vector.reciprocal(inv_tops[:, j : j + 1], top[:])
             halves = []
             for g in range(2):
                 w = sb.tile([P, PASS], BF16, name=f"w{j}{g}", align_bytes=64)
                 cols = slice(g * PASS, (g + 1) * PASS)
-                nc.vector.scalar_tensor_tensor(w[:], floored[:, cols], inv_top[:], vs_slots[:, cols], ALU.mult, ALU.mult)
+                nc.vector.scalar_tensor_tensor(w[:], floored[:, cols], inv_tops[:, j : j + 1], vs_slots[:, cols], ALU.mult, ALU.mult)
                 bank = ps.tile([P, 2, P], F32, name=f"w_bank{j}{g}", tag=f"score{j}{g}")
                 turned = sb.tile([P, PASS], BF16, name=f"w_turned{j}{g}", align_bytes=64)
                 turn(w[:], bank[:], turned[:])
                 halves.append(turned)
-            inv_total = sb.tile([P, 1], F32, name=f"inv_total{j}")
-            nc.vector.reciprocal(inv_total[:], total_f[:])
-            factor = sb.tile([P, 1], F32, name=f"factor{j}")
-            nc.vector.tensor_tensor(factor[:], inv_total[:], top[:], ALU.mult)
             weights.append(halves)
-            factors.append(factor)
+        sums = sb.tile([P, 2], F32, name="sums")
+        nc.vector.scalar_tensor_tensor(sums[:], totals[:], N * FLOOR, inv_tops[:], ALU.add, ALU.mult)
+        inv_sums = sb.tile([P, 2], F32, name="inv_sums")
+        nc.vector.reciprocal(inv_sums[:], sums[:])
 
-        v_code, v_scale = quantise(v_turned[:], "v")
+        early_codes = sb.tile([P, 4 * P], U32, name="early_codes", tag="seen1", align_bytes=64)
+        late_codes = sb.tile([P, 2 * P], U32, name="late_codes", align_bytes=64)
+        v_code, v_scale = quantise(v_turned[:], early_codes[:, 0 : 2 * P], "v")
+        w_codes = [early_codes[:, 2 * P : 4 * P], late_codes[:]]
         for j in range(2):
             acc = ps.tile([P, DV], F32, name=f"acc{j}")
             for g in range(2):
-                w_code, w_scale = quantise(weights[j][g][:], f"wq{j}{g}")
+                w_code, w_scale = quantise(weights[j][g][:], w_codes[j][:, g * P : (g + 1) * P], f"wq{j}{g}")
                 nc.tensor.matmul_mx(
                     out=acc[:],
-                    lhsT=w_code[:].bitcast(FP8X4),
+                    lhsT=w_code.bitcast(FP8X4),
                     lhsT_scale=w_scale[:],
                     rhs=v_code[:, g * DV : (g + 1) * DV].bitcast(FP8X4),
                     rhs_scale=v_scale[:, g * DV : (g + 1) * DV],
@@ -172,5 +170,5 @@ def tile_attend_soft_draft_cap_topkq256n1024t2048_kernel(tc, q_words, q_scales, 
                     stop=(g == 1),
                 )
             result = sb.tile([P, DV], F32, name=f"result{j}")
-            nc.scalar.activation(result[:], acc[:], ACT.Copy, scale=factors[j][:])
+            nc.scalar.activation(result[:], acc[:], ACT.Copy, scale=inv_sums[:, j : j + 1])
             nc.sync.dma_start(out[0, j * P : (j + 1) * P, :], result[:])

@@ -5,6 +5,7 @@ from concourse.masks import make_identity
 
 N, T, D, DV, NQ = 1024, 2048, 1024, 128, 256
 CAP = 2.0
+LOG_FLOOR = -70.0
 FLOPS = 2 * NQ * N * (D + DV)
 
 F32 = mybir.dt.float32
@@ -20,7 +21,11 @@ ALU = mybir.AluOpType
 
 P = 128
 PASS = 512
-FLOOR = 2.0**-100
+QUAD = 32
+LIST_ROWS = 16
+D_PASSES = D // PASS
+SLOT_PASSES = N // PASS
+ROW_TILES = NQ // P
 
 
 def tile_attend_soft_draft_cap_topkq256n1024t2048_kernel(tc, q_words, q_scales, k_words, k_scales, vT, vs, pos, qpos, offs, out):
@@ -29,146 +34,159 @@ def tile_attend_soft_draft_cap_topkq256n1024t2048_kernel(tc, q_words, q_scales, 
         sb = ctx.enter_context(tc.tile_pool(name="sb", bufs=1))
         ps = ctx.enter_context(tc.psum_pool(name="ps", bufs=1))
 
-        offsets = sb.tile([P, N // 16], U16, name="offsets")
-        nc.sync.dma_start(offsets[:], offs)
 
-        ks_pool = sb.tile([P, T], U8, name="ks_pool", tag="ks_then_pos", align_bytes=64)
-        nc.sync.dma_start(ks_pool[0:32, :].bitcast(I32), k_scales.rearrange("o f t -> f o t").bitcast(I32))
-        kw_pool = sb.tile([P, T], I32, name="kw_pool", tag="kw_then_vs", align_bytes=64)
+        offsets = sb.tile([P, N // LIST_ROWS], U16, name="offsets")
+        nc.sync.dma_start(offsets[:], offs)
+        ks_pool = sb.tile([P, T], U8, name="ks_pool", tag="after_scale_gather", align_bytes=64)
+        nc.sync.dma_start(ks_pool[0:QUAD, :].bitcast(I32), k_scales.rearrange("o f t -> f o t").bitcast(I32))
+        kw_pool = sb.tile([P, T], I32, name="kw_pool", align_bytes=64)
         nc.sync.dma_start(kw_pool[:], k_words[0].rearrange("p t b -> p (t b)").bitcast(I32))
 
-        q_scale = sb.tile([P, 2, NQ], U8, name="q_scale", align_bytes=64)
+        q_scale = sb.tile([P, D_PASSES, NQ], U8, name="q_scale", align_bytes=64)
         nc.gpsimd.memset(q_scale[:].bitcast(I32), 0)
-        for quad in range(4):
+        for quad in range(P // QUAD):
             nc.sync.dma_start(
-                q_scale[32 * quad : 32 * quad + 4, :, :].bitcast(I32),
+                q_scale[QUAD * quad : QUAD * quad + 4, :, :].bitcast(I32),
                 q_scales[0, :, 4 * quad : 4 * quad + 4, :].rearrange("o f q -> f o q").bitcast(I32),
             )
-        q_code = sb.tile([P, 2, NQ], I32, name="q_code", align_bytes=64)
+        q_code = sb.tile([P, D_PASSES, NQ], I32, name="q_code", align_bytes=64)
         nc.sync.dma_start(q_code[:], q_words[0].rearrange("o p q r -> p o (q r)").bitcast(I32))
         v_pool = sb.tile([P, T], F32, name="v_pool")
         nc.sync.dma_start(v_pool[:], vT)
-        q_place = sb.tile([P, 2], F32, name="q_place")
-        with nc.allow_non_contiguous_dma(reason="one place a partition"):
+        v_bf = sb.tile([P, T], BF16, name="v_bf", align_bytes=64)
+        nc.scalar.activation(v_bf[:], v_pool[:], ACT.Copy)
+        q_place = sb.tile([P, ROW_TILES], F32, name="q_place")
+        with nc.allow_non_contiguous_dma(reason="one place for each query row"):
             nc.gpsimd.dma_start(q_place[:], qpos[0].rearrange("(j p) o -> p (j o)", p=P))
         ident = sb.tile([P, P], F32, name="ident")
         make_identity(nc, ident[:])
 
-        k_scale = sb.tile([P, 2, N], U8, name="k_scale", align_bytes=64)
-        warm = sb.tile([P, 1], F32, name="warm")
-        warm_out = sb.tile([P, 1], F32, name="warm_out")
-        nc.vector.memset(warm[:], 0.0)
-        nc.vector.memset(ks_pool[32:64, :].bitcast(I32), 0)
-        nc.vector.memset(ks_pool[64:128, :].bitcast(I32), 0)
+        k_scale = sb.tile([P, D_PASSES, N], U8, name="k_scale", align_bytes=64)
+        log_floor = sb.tile([P, 1], F32, name="log_floor")
+        nc.vector.memset(log_floor[:], LOG_FLOOR)
+        nc.vector.memset(ks_pool[QUAD : 2 * QUAD, :].bitcast(I32), 0)
+        nc.vector.memset(ks_pool[2 * QUAD : P, :].bitcast(I32), 0)
         nc.vector.memset(k_scale[:].bitcast(I32), 0)
-        nc.scalar.activation(warm_out[:], warm[:], ACT.Exp)
+        floor = sb.tile([P, 1], F32, name="floor")
+        nc.scalar.activation(floor[:], log_floor[:], ACT.Exp)
+        floor_sum = sb.tile([P, 1], F32, name="floor_sum")
+        nc.scalar.activation(floor_sum[:], floor[:], ACT.Copy, scale=float(N))
 
         ks_slots = sb.tile([P, N], U8, name="ks_slots", align_bytes=64)
         nc.vector.tensor_copy(ks_slots[:], ks_pool[:].indirect(offsets[:]))
-        for quad in range(4):
+        for quad in range(P // QUAD):
             nc.sync.dma_start(
-                k_scale[32 * quad : 32 * quad + 4, :, :].bitcast(I32),
+                k_scale[QUAD * quad : QUAD * quad + 4, :, :].bitcast(I32),
                 ks_slots[8 * quad : 8 * quad + 8, :].bitcast(I32),
             )
-        pos_pool = sb.tile([P, T], F32, name="pos_pool", tag="ks_then_pos", align_bytes=64)
+        pos_pool = sb.tile([P, T], F32, name="pos_pool", tag="after_scale_gather", align_bytes=64)
         nc.sync.dma_start(pos_pool[:], pos)
-        kw = sb.tile([P, N], U32, name="kw", align_bytes=64)
-        nc.vector.tensor_copy(kw[:], kw_pool[:].bitcast(U32).indirect(offsets[:]))
-        vs_pool = sb.tile([P, T], F32, name="vs_pool", tag="kw_then_vs", align_bytes=64)
+
+        k_code = []
+        for h in range(SLOT_PASSES):
+            kw_slots = sb.tile([P, PASS], U32, name=f"kw_slots{h}", tag=f"after_parting{h}", align_bytes=64)
+            entries = offsets[:, h * PASS // LIST_ROWS : (h + 1) * PASS // LIST_ROWS]
+            nc.vector.tensor_copy(kw_slots[:], kw_pool[:].bitcast(U32).indirect(entries))
+            parted = sb.tile([P, D_PASSES, PASS], U16, name=f"k_code{h}", align_bytes=64)
+            nc.vector.tensor_copy(parted[:], kw_slots[:].bitcast(U16).rearrange("p (n o) -> p o n", o=D_PASSES))
+            k_code.append(parted)
+        vs_pool = sb.tile([P, T], F32, name="vs_pool", tag="after_parting0", align_bytes=64)
         nc.sync.dma_start(vs_pool[:], vs)
-        k_code = sb.tile([P, 2, N], U16, name="k_code", align_bytes=64)
-        nc.vector.tensor_copy(k_code[:], kw[:].bitcast(U16).rearrange("p (n o) -> p o n", o=2))
 
-
-        v_bf = sb.tile([P, T], BF16, name="v_bf", align_bytes=64)
-        nc.scalar.activation(v_bf[:], v_pool[:], ACT.Copy)
         pos_slots = sb.tile([P, N], F32, name="pos_slots")
         nc.vector.tensor_copy(pos_slots[:], pos_pool[:].indirect(offsets[:]))
-
-        grown = []
-        for j in range(2):
-            capped = sb.tile([P, N], F32, name=f"capped{j}", tag=f"capped{j}", align_bytes=64)
-            for h in range(2):
-                bank = ps.tile([P, PASS], F32, name=f"score{j}{h}", tag=f"score{j}{h}")
-                for o in range(2):
-                    nc.tensor.matmul_mx(
-                        out=bank[:],
-                        lhsT=q_code[:, o, j * P : (j + 1) * P].bitcast(FP8X4),
-                        lhsT_scale=q_scale[:, o, j * P : (j + 1) * P],
-                        rhs=k_code[:, o, h * PASS : (h + 1) * PASS].bitcast(FP4X4),
-                        rhs_scale=k_scale[:, o, h * PASS : (h + 1) * PASS],
-                        start=(o == 0),
-                        stop=(o == 1),
-                    )
-                nc.scalar.activation(capped[:, h * PASS : (h + 1) * PASS], bank[:], ACT.Tanh, scale=1.0 / CAP)
-            e = sb.tile([P, N], F32, name=f"grown{j}")
-            nc.scalar.activation(e[:], capped[:], ACT.Exp, scale=CAP)
-            grown.append(e)
-
-        v_slots = sb.tile([P, N], BF16, name="v_slots", tag="capped1", align_bytes=64)
-        nc.scalar.activation(v_slots[:], v_bf[:].indirect(offsets[:]), ACT.Copy)
         vs_slots = sb.tile([P, N], F32, name="vs_slots")
         nc.vector.tensor_copy(vs_slots[:], vs_pool[:].indirect(offsets[:]))
 
-        def turn(src, bank, dst):
-            words = src.bitcast(F32)
-            for u in range(2):
-                nc.tensor.transpose(bank[:, u, :], words[:, u::2], ident[:])
-            nc.scalar.copy(dst.bitcast(F32).rearrange("p (c u) -> p c u", u=2), bank.rearrange("p u c -> p c u"))
+        e_all = []
+        for j in range(ROW_TILES):
+            capped = sb.tile([P, N], F32, name=f"capped{j}", tag=f"capped{j}", align_bytes=64)
+            for h in range(SLOT_PASSES):
+                slots = slice(h * PASS, (h + 1) * PASS)
+                score = ps.tile([P, PASS], F32, name=f"score{j}{h}", tag=f"bank{j}{h}")
+                for o in range(D_PASSES):
+                    nc.tensor.matmul_mx(
+                        out=score[:],
+                        lhsT=q_code[:, o, j * P : (j + 1) * P].bitcast(FP8X4),
+                        lhsT_scale=q_scale[:, o, j * P : (j + 1) * P],
+                        rhs=k_code[h][:, o, :].bitcast(FP4X4),
+                        rhs_scale=k_scale[:, o, slots],
+                        start=(o == 0),
+                        stop=(o == D_PASSES - 1),
+                    )
+                nc.scalar.activation(capped[:, slots], score[:], ACT.Tanh, scale=1.0 / CAP)
+            e = sb.tile([P, N], F32, name=f"e{j}")
+            nc.scalar.activation(e[:], capped[:], ACT.Exp, scale=CAP)
+            e_all.append(e)
 
-        def quantise(src, codes, name):
-            cols = src.shape[1] // 4
-            scales = sb.tile([P, cols], U8, name=name + "_scale", align_bytes=64)
-            nc.vector.quantize_mx(out=codes.bitcast(FP8X4), scales=scales[:], in_=src)
+        v_slots = sb.tile([P, N], BF16, name="v_slots", tag=f"capped{ROW_TILES - 1}", align_bytes=64)
+        nc.scalar.activation(v_slots[:], v_bf[:].indirect(offsets[:]), ACT.Copy)
+
+        def turn(src, bank, dst):
+            passes = src.shape[1] // PASS
+            words = src.bitcast(F32)
+            for g in range(passes):
+                for u in range(2):
+                    nc.tensor.transpose(bank[:, g, u, :], words[:, g * 2 * P + u : (g + 1) * 2 * P : 2], ident[:])
+            nc.scalar.copy(dst.bitcast(F32).rearrange("p (g c u) -> p g c u", g=passes, u=2), bank.rearrange("p g u c -> p g c u"))
+
+        def quantise(src, name, tag):
+            columns = src.shape[1] // 4
+            codes = sb.tile([P, columns], U32, name=name + "_code", tag=tag, align_bytes=64)
+            scales = sb.tile([P, columns], U8, name=name + "_scale", align_bytes=64)
+            nc.vector.quantize_mx(out=codes[:].bitcast(FP8X4), scales=scales[:], in_=src)
             return codes, scales
 
-        v_turned = sb.tile([P, 2 * 4 * DV], BF16, name="v_turned", align_bytes=64)
-        for g in range(2):
-            v_bank = ps.tile([P, 2, DV], F32, name=f"v_bank{g}")
-            turn(v_slots[:, g * PASS : (g + 1) * PASS], v_bank[:], v_turned[:, g * PASS : (g + 1) * PASS])
-
-        weights = []
-        totals = sb.tile([P, 2], F32, name="totals")
-        inv_tops = sb.tile([P, 2], F32, name="inv_tops")
-        for j in range(2):
-            seen = sb.tile([P, N], F32, name=f"seen{j}", tag=["kw_then_vs", "seen1"][j], align_bytes=64)
-            nc.vector.scalar_tensor_tensor(seen[:], pos_slots[:], q_place[:, j : j + 1], grown[j][:], ALU.is_le, ALU.mult, accum_out=totals[:, j : j + 1])
-            floored = sb.tile([P, N], F32, name=f"floored{j}")
+        e_sum = sb.tile([P, ROW_TILES], F32, name="e_sum")
+        inv_top = sb.tile([P, ROW_TILES], F32, name="inv_top")
+        masked_tags = ["after_parting0", "after_maxima"]
+        lifted_all = []
+        top_all = []
+        for j in range(ROW_TILES):
+            masked = sb.tile([P, N], F32, name=f"masked{j}", tag=masked_tags[j], align_bytes=64)
+            nc.vector.scalar_tensor_tensor(masked[:], pos_slots[:], q_place[:, j : j + 1], e_all[j][:], ALU.is_le, ALU.mult, accum_out=e_sum[:, j : j + 1])
+            lifted = sb.tile([P, N], F32, name=f"lifted{j}", tag=f"lifted{j}", align_bytes=64)
             top = sb.tile([P, 1], F32, name=f"top{j}")
-            nc.vector.tensor_scalar(floored[:], seen[:], FLOOR, None, ALU.max, ALU.max, accum_out=top[:])
-            nc.vector.reciprocal(inv_tops[:, j : j + 1], top[:])
-            halves = []
-            for g in range(2):
-                w = sb.tile([P, PASS], BF16, name=f"w{j}{g}", align_bytes=64)
-                cols = slice(g * PASS, (g + 1) * PASS)
-                nc.vector.scalar_tensor_tensor(w[:], floored[:, cols], inv_tops[:, j : j + 1], vs_slots[:, cols], ALU.mult, ALU.mult)
-                bank = ps.tile([P, 2, P], F32, name=f"w_bank{j}{g}", tag=f"score{j}{g}")
-                turned = sb.tile([P, PASS], BF16, name=f"w_turned{j}{g}", align_bytes=64)
-                turn(w[:], bank[:], turned[:])
-                halves.append(turned)
-            weights.append(halves)
-        sums = sb.tile([P, 2], F32, name="sums")
-        nc.vector.scalar_tensor_tensor(sums[:], totals[:], N * FLOOR, inv_tops[:], ALU.add, ALU.mult)
-        inv_sums = sb.tile([P, 2], F32, name="inv_sums")
-        nc.vector.reciprocal(inv_sums[:], sums[:])
+            nc.vector.tensor_scalar(lifted[:], masked[:], floor[:], None, ALU.max, ALU.max, accum_out=top[:])
+            lifted_all.append(lifted)
+            top_all.append(top)
+        for j in range(ROW_TILES):
+            nc.vector.reciprocal(inv_top[:, j : j + 1], top_all[j][:])
 
-        early_codes = sb.tile([P, 4 * P], U32, name="early_codes", tag="seen1", align_bytes=64)
-        late_codes = sb.tile([P, 2 * P], U32, name="late_codes", align_bytes=64)
-        v_code, v_scale = quantise(v_turned[:], early_codes[:, 0 : 2 * P], "v")
-        w_codes = [early_codes[:, 2 * P : 4 * P], late_codes[:]]
-        for j in range(2):
+        v_turned = sb.tile([P, N], BF16, name="v_turned", align_bytes=64)
+        v_bank = ps.tile([P, SLOT_PASSES, 2, DV], F32, name="v_bank")
+        turn(v_slots[:], v_bank[:], v_turned[:])
+
+        w = sb.tile([P, ROW_TILES * N], BF16, name="w", tag="after_maxima", align_bytes=64)
+        w_turned = {}
+        for j in range(ROW_TILES):
+            for g in range(SLOT_PASSES):
+                slots = slice(g * PASS, (g + 1) * PASS)
+                piece = w[:, j * N + g * PASS : j * N + (g + 1) * PASS]
+                nc.vector.scalar_tensor_tensor(piece, lifted_all[j][:, slots], inv_top[:, j : j + 1], vs_slots[:, slots], ALU.mult, ALU.mult)
+                w_bank = ps.tile([P, 1, 2, P], F32, name=f"w_bank{j}{g}", tag=f"bank{j}{g}")
+                w_turned[j, g] = sb.tile([P, PASS], BF16, name=f"w_turned{j}{g}", align_bytes=64)
+                turn(piece, w_bank[:], w_turned[j, g][:])
+
+        row_sum = sb.tile([P, ROW_TILES], F32, name="row_sum")
+        nc.vector.scalar_tensor_tensor(row_sum[:], e_sum[:], floor_sum[:], inv_top[:], ALU.add, ALU.mult)
+        inv_row_sum = sb.tile([P, ROW_TILES], F32, name="inv_row_sum")
+        nc.vector.reciprocal(inv_row_sum[:], row_sum[:])
+
+        v_code, v_scale = quantise(v_turned[:], "v", "lifted0")
+        for j in range(ROW_TILES):
             acc = ps.tile([P, DV], F32, name=f"acc{j}")
-            for g in range(2):
-                w_code, w_scale = quantise(weights[j][g][:], w_codes[j][:, g * P : (g + 1) * P], f"wq{j}{g}")
+            for g in range(SLOT_PASSES):
+                w_code, w_scale = quantise(w_turned[j, g][:], f"w{j}{g}", f"w_code{j}{g}")
                 nc.tensor.matmul_mx(
                     out=acc[:],
-                    lhsT=w_code.bitcast(FP8X4),
+                    lhsT=w_code[:].bitcast(FP8X4),
                     lhsT_scale=w_scale[:],
                     rhs=v_code[:, g * DV : (g + 1) * DV].bitcast(FP8X4),
                     rhs_scale=v_scale[:, g * DV : (g + 1) * DV],
                     start=(g == 0),
-                    stop=(g == 1),
+                    stop=(g == SLOT_PASSES - 1),
                 )
             result = sb.tile([P, DV], F32, name=f"result{j}")
-            nc.scalar.activation(result[:], acc[:], ACT.Copy, scale=inv_sums[:, j : j + 1])
+            nc.scalar.activation(result[:], acc[:], ACT.Copy, scale=inv_row_sum[:, j : j + 1])
             nc.sync.dma_start(out[0, j * P : (j + 1) * P, :], result[:])

@@ -39,7 +39,7 @@ def tile_attend_soft_draft_cap_topkq256n1024t2048_kernel(tc, q_words, q_scales, 
         nc.sync.dma_start(offsets[:], offs)
         ks_pool = sb.tile([P, T], U8, name="ks_pool", tag="after_scale_gather", align_bytes=64)
         nc.sync.dma_start(ks_pool[0:QUAD, :].bitcast(I32), k_scales.rearrange("o f t -> f o t").bitcast(I32))
-        kw_pool = sb.tile([P, T], I32, name="kw_pool", align_bytes=64)
+        kw_pool = sb.tile([P, T], I32, name="kw_pool", tag="after_word_gathers", align_bytes=64)
         nc.sync.dma_start(kw_pool[:], k_words[0].rearrange("p t b -> p (t b)").bitcast(I32))
 
         q_scale = sb.tile([P, D_PASSES, NQ], U8, name="q_scale", align_bytes=64)
@@ -51,10 +51,8 @@ def tile_attend_soft_draft_cap_topkq256n1024t2048_kernel(tc, q_words, q_scales, 
             )
         q_code = sb.tile([P, D_PASSES, NQ], I32, name="q_code", align_bytes=64)
         nc.sync.dma_start(q_code[:], q_words[0].rearrange("o p q r -> p o (q r)").bitcast(I32))
-        v_pool = sb.tile([P, T], F32, name="v_pool")
-        nc.sync.dma_start(v_pool[:], vT)
-        v_bf = sb.tile([P, T], BF16, name="v_bf", align_bytes=64)
-        nc.scalar.activation(v_bf[:], v_pool[:], ACT.Copy)
+        pos_pool = sb.tile([P, T], F32, name="pos_pool")
+        nc.sync.dma_start(pos_pool[:], pos)
         q_place = sb.tile([P, ROW_TILES], F32, name="q_place")
         with nc.allow_non_contiguous_dma(reason="one place for each query row"):
             nc.gpsimd.dma_start(q_place[:], qpos[0].rearrange("(j p) o -> p (j o)", p=P))
@@ -79,19 +77,19 @@ def tile_attend_soft_draft_cap_topkq256n1024t2048_kernel(tc, q_words, q_scales, 
                 k_scale[QUAD * quad : QUAD * quad + 4, :, :].bitcast(I32),
                 ks_slots[8 * quad : 8 * quad + 8, :].bitcast(I32),
             )
-        pos_pool = sb.tile([P, T], F32, name="pos_pool", tag="after_scale_gather", align_bytes=64)
-        nc.sync.dma_start(pos_pool[:], pos)
+        vs_pool = sb.tile([P, T], F32, name="vs_pool", tag="after_scale_gather", align_bytes=64)
+        nc.sync.dma_start(vs_pool[:], vs)
 
         k_code = []
         for h in range(SLOT_PASSES):
-            kw_slots = sb.tile([P, PASS], U32, name=f"kw_slots{h}", tag=f"after_parting{h}", align_bytes=64)
+            kw_slots = sb.tile([P, PASS], U32, name=f"kw_slots{h}", align_bytes=64)
             entries = offsets[:, h * PASS // LIST_ROWS : (h + 1) * PASS // LIST_ROWS]
             nc.vector.tensor_copy(kw_slots[:], kw_pool[:].bitcast(U32).indirect(entries))
             parted = sb.tile([P, D_PASSES, PASS], U16, name=f"k_code{h}", align_bytes=64)
             nc.vector.tensor_copy(parted[:], kw_slots[:].bitcast(U16).rearrange("p (n o) -> p o n", o=D_PASSES))
             k_code.append(parted)
-        vs_pool = sb.tile([P, T], F32, name="vs_pool", tag="after_parting0", align_bytes=64)
-        nc.sync.dma_start(vs_pool[:], vs)
+        v_pool = sb.tile([P, T], F32, name="v_pool", tag="after_word_gathers", align_bytes=64)
+        nc.sync.dma_start(v_pool[:], vT)
 
         pos_slots = sb.tile([P, N], F32, name="pos_slots")
         nc.vector.tensor_copy(pos_slots[:], pos_pool[:].indirect(offsets[:]))
@@ -119,7 +117,9 @@ def tile_attend_soft_draft_cap_topkq256n1024t2048_kernel(tc, q_words, q_scales, 
             nc.scalar.activation(e[:], capped[:], ACT.Exp, scale=CAP)
             e_all.append(e)
 
-        v_slots = sb.tile([P, N], BF16, name="v_slots", tag=f"capped{ROW_TILES - 1}", align_bytes=64)
+        v_bf = sb.tile([P, T], BF16, name="v_bf", tag=f"capped{ROW_TILES - 1}", align_bytes=64)
+        nc.scalar.activation(v_bf[:], v_pool[:], ACT.Copy)
+        v_slots = sb.tile([P, N], BF16, name="v_slots", align_bytes=64)
         nc.scalar.activation(v_slots[:], v_bf[:].indirect(offsets[:]), ACT.Copy)
 
         def turn(src, bank, dst):
@@ -130,22 +130,22 @@ def tile_attend_soft_draft_cap_topkq256n1024t2048_kernel(tc, q_words, q_scales, 
                     nc.tensor.transpose(bank[:, g, u, :], words[:, g * 2 * P + u : (g + 1) * 2 * P : 2], ident[:])
             nc.scalar.copy(dst.bitcast(F32).rearrange("p (g c u) -> p g c u", g=passes, u=2), bank.rearrange("p g u c -> p g c u"))
 
-        def quantise(src, name, tag):
+        def quantise(src, name):
             columns = src.shape[1] // 4
-            codes = sb.tile([P, columns], U32, name=name + "_code", tag=tag, align_bytes=64)
+            codes = sb.tile([P, columns], U32, name=name + "_code", align_bytes=64)
             scales = sb.tile([P, columns], U8, name=name + "_scale", align_bytes=64)
             nc.vector.quantize_mx(out=codes[:].bitcast(FP8X4), scales=scales[:], in_=src)
             return codes, scales
 
         e_sum = sb.tile([P, ROW_TILES], F32, name="e_sum")
         inv_top = sb.tile([P, ROW_TILES], F32, name="inv_top")
-        masked_tags = ["after_parting0", "after_maxima"]
+        masked_tags = ["after_scale_gather", "after_maxima"]
         lifted_all = []
         top_all = []
         for j in range(ROW_TILES):
             masked = sb.tile([P, N], F32, name=f"masked{j}", tag=masked_tags[j], align_bytes=64)
             nc.vector.scalar_tensor_tensor(masked[:], pos_slots[:], q_place[:, j : j + 1], e_all[j][:], ALU.is_le, ALU.mult, accum_out=e_sum[:, j : j + 1])
-            lifted = sb.tile([P, N], F32, name=f"lifted{j}", tag=f"lifted{j}", align_bytes=64)
+            lifted = sb.tile([P, N], F32, name=f"lifted{j}")
             top = sb.tile([P, 1], F32, name=f"top{j}")
             nc.vector.tensor_scalar(lifted[:], masked[:], floor[:], None, ALU.max, ALU.max, accum_out=top[:])
             lifted_all.append(lifted)
@@ -173,11 +173,11 @@ def tile_attend_soft_draft_cap_topkq256n1024t2048_kernel(tc, q_words, q_scales, 
         inv_row_sum = sb.tile([P, ROW_TILES], F32, name="inv_row_sum")
         nc.vector.reciprocal(inv_row_sum[:], row_sum[:])
 
-        v_code, v_scale = quantise(v_turned[:], "v", "lifted0")
+        v_code, v_scale = quantise(v_turned[:], "v")
         for j in range(ROW_TILES):
             acc = ps.tile([P, DV], F32, name=f"acc{j}")
             for g in range(SLOT_PASSES):
-                w_code, w_scale = quantise(w_turned[j, g][:], f"w{j}{g}", f"w_code{j}{g}")
+                w_code, w_scale = quantise(w_turned[j, g][:], f"w{j}{g}")
                 nc.tensor.matmul_mx(
                     out=acc[:],
                     lhsT=w_code[:].bitcast(FP8X4),

@@ -39,9 +39,12 @@ def tile_attend_soft_draft_cap_topkq256n1024t2048_kernel(tc, q_words, q_scales, 
         nc.sync.dma_start(offsets[:], offs)
         ks_pool = sb.tile([P, T], U8, name="ks_pool", tag="after_scale_gather", align_bytes=64)
         nc.sync.dma_start(ks_pool[0:QUAD, :].bitcast(I32), k_scales.rearrange("o f t -> f o t").bitcast(I32))
-        kw_pool = sb.tile([P, T], I32, name="kw_pool", tag="after_word_gathers", align_bytes=64)
+        nc.vector.memset(ks_pool[QUAD : 2 * QUAD, :].bitcast(I32), 0)
+        nc.vector.memset(ks_pool[2 * QUAD : P, :].bitcast(I32), 0)
+        kw_pool = sb.tile([P, T], I32, name="kw_pool", align_bytes=64)
         nc.sync.dma_start(kw_pool[:], k_words[0].rearrange("p t b -> p (t b)").bitcast(I32))
-
+        q_code = sb.tile([P, D_PASSES, NQ], I32, name="q_code", align_bytes=64)
+        nc.sync.dma_start(q_code[:], q_words[0].rearrange("o p q r -> p o (q r)").bitcast(I32))
         q_scale = sb.tile([P, D_PASSES, NQ], U8, name="q_scale", align_bytes=64)
         nc.gpsimd.memset(q_scale[:].bitcast(I32), 0)
         for quad in range(P // QUAD):
@@ -49,24 +52,25 @@ def tile_attend_soft_draft_cap_topkq256n1024t2048_kernel(tc, q_words, q_scales, 
                 q_scale[QUAD * quad : QUAD * quad + 4, :, :].bitcast(I32),
                 q_scales[0, :, 4 * quad : 4 * quad + 4, :].rearrange("o f q -> f o q").bitcast(I32),
             )
-        q_code = sb.tile([P, D_PASSES, NQ], I32, name="q_code", align_bytes=64)
-        nc.sync.dma_start(q_code[:], q_words[0].rearrange("o p q r -> p o (q r)").bitcast(I32))
+
         pos_pool = sb.tile([P, T], F32, name="pos_pool")
-        nc.sync.dma_start(pos_pool[:], pos)
+        nc.gpsimd.memset(pos_pool[:], 0.0)
+        nc.sync.dma_start(pos_pool[0:1, :], pos[0:1, :])
+
+        log_floor = sb.tile([P, 1], F32, name="log_floor", tag="after_floor", align_bytes=64)
+        nc.vector.memset(log_floor[:], LOG_FLOOR)
+        floor = sb.tile([P, 1], F32, name="floor")
+        nc.scalar.activation(floor[:], log_floor[:], ACT.Exp)
+        v_pool = sb.tile([P, T], F32, name="v_pool", tag="after_floor", align_bytes=64)
+        nc.sync.dma_start(v_pool[:], vT)
+
         q_place = sb.tile([P, ROW_TILES], F32, name="q_place")
         with nc.allow_non_contiguous_dma(reason="one place for each query row"):
             nc.gpsimd.dma_start(q_place[:], qpos[0].rearrange("(j p) o -> p (j o)", p=P))
+        k_scale = sb.tile([P, D_PASSES, N], U8, name="k_scale", align_bytes=64)
+        nc.vector.memset(k_scale[:].bitcast(I32), 0)
         ident = sb.tile([P, P], F32, name="ident")
         make_identity(nc, ident[:])
-
-        k_scale = sb.tile([P, D_PASSES, N], U8, name="k_scale", align_bytes=64)
-        log_floor = sb.tile([P, 1], F32, name="log_floor")
-        nc.vector.memset(log_floor[:], LOG_FLOOR)
-        nc.vector.memset(ks_pool[QUAD : 2 * QUAD, :].bitcast(I32), 0)
-        nc.vector.memset(ks_pool[2 * QUAD : P, :].bitcast(I32), 0)
-        nc.vector.memset(k_scale[:].bitcast(I32), 0)
-        floor = sb.tile([P, 1], F32, name="floor")
-        nc.scalar.activation(floor[:], log_floor[:], ACT.Exp)
         floor_sum = sb.tile([P, 1], F32, name="floor_sum")
         nc.scalar.activation(floor_sum[:], floor[:], ACT.Copy, scale=float(N))
 
@@ -77,30 +81,53 @@ def tile_attend_soft_draft_cap_topkq256n1024t2048_kernel(tc, q_words, q_scales, 
                 k_scale[QUAD * quad : QUAD * quad + 4, :, :].bitcast(I32),
                 ks_slots[8 * quad : 8 * quad + 8, :].bitcast(I32),
             )
+
         vs_pool = sb.tile([P, T], F32, name="vs_pool", tag="after_scale_gather", align_bytes=64)
         nc.sync.dma_start(vs_pool[:], vs)
 
+        v_bf = sb.tile([P, T], BF16, name="v_bf", align_bytes=64)
+        nc.scalar.activation(v_bf[:], v_pool[:], ACT.Copy)
+
         k_code = []
+        pos_cols = []
         for h in range(SLOT_PASSES):
             kw_slots = sb.tile([P, PASS], U32, name=f"kw_slots{h}", align_bytes=64)
             entries = offsets[:, h * PASS // LIST_ROWS : (h + 1) * PASS // LIST_ROWS]
             nc.vector.tensor_copy(kw_slots[:], kw_pool[:].bitcast(U32).indirect(entries))
+            pos_slots = sb.tile([P, PASS], F32, name=f"pos_slots{h}")
+            nc.vector.tensor_copy(pos_slots[:], pos_pool[:].indirect(entries))
+            cols = sb.tile([P, 4], F32, name=f"pos_cols{h}")
+            nc.sync.dma_start(cols[:], pos_slots[0:1, :])
+            pos_cols.append(cols)
             parted = sb.tile([P, D_PASSES, PASS], U16, name=f"k_code{h}", align_bytes=64)
             nc.vector.tensor_copy(parted[:], kw_slots[:].bitcast(U16).rearrange("p (n o) -> p o n", o=D_PASSES))
             k_code.append(parted)
-        v_pool = sb.tile([P, T], F32, name="v_pool", tag="after_word_gathers", align_bytes=64)
-        nc.sync.dma_start(v_pool[:], vT)
-
-        pos_slots = sb.tile([P, N], F32, name="pos_slots")
-        nc.vector.tensor_copy(pos_slots[:], pos_pool[:].indirect(offsets[:]))
         vs_slots = sb.tile([P, N], F32, name="vs_slots")
         nc.vector.tensor_copy(vs_slots[:], vs_pool[:].indirect(offsets[:]))
 
-        e_all = []
-        for j in range(ROW_TILES):
-            capped = sb.tile([P, N], F32, name=f"capped{j}", tag=f"capped{j}", align_bytes=64)
-            for h in range(SLOT_PASSES):
-                slots = slice(h * PASS, (h + 1) * PASS)
+        def turn(src, bank, dst):
+            passes = src.shape[1] // PASS
+            words = src.bitcast(F32)
+            for g in range(passes):
+                for u in range(2):
+                    nc.tensor.transpose(bank[:, g, u, :], words[:, g * 2 * P + u : (g + 1) * 2 * P : 2], ident[:])
+            nc.scalar.copy(dst.bitcast(F32).rearrange("p (g c u) -> p g c u", g=passes, u=2), bank.rearrange("p g u c -> p g c u"))
+
+        def quantise(src, name, tag):
+            columns = src.shape[1] // 4
+            codes = sb.tile([P, columns], U32, name=name + "_code", tag=tag, align_bytes=64)
+            scales = sb.tile([P, columns], U8, name=name + "_scale", align_bytes=64)
+            nc.vector.quantize_mx(out=codes[:].bitcast(FP8X4), scales=scales[:], in_=src)
+            return codes, scales
+
+
+        e_sum = sb.tile([P, SLOT_PASSES, ROW_TILES], F32, name="e_sum")
+        masked_tags = ["after_scale_gather", "masked1"]
+        masked_all = [sb.tile([P, N], F32, name=f"masked{j}", tag=masked_tags[j], align_bytes=64) for j in range(ROW_TILES)]
+        for h in range(SLOT_PASSES):
+            slots = slice(h * PASS, (h + 1) * PASS)
+            e_half = []
+            for j in range(ROW_TILES):
                 score = ps.tile([P, PASS], F32, name=f"score{j}{h}", tag=f"bank{j}{h}")
                 for o in range(D_PASSES):
                     nc.tensor.matmul_mx(
@@ -112,72 +139,67 @@ def tile_attend_soft_draft_cap_topkq256n1024t2048_kernel(tc, q_words, q_scales, 
                         start=(o == 0),
                         stop=(o == D_PASSES - 1),
                     )
-                nc.scalar.activation(capped[:, slots], score[:], ACT.Tanh, scale=1.0 / CAP)
-            e = sb.tile([P, N], F32, name=f"e{j}")
-            nc.scalar.activation(e[:], capped[:], ACT.Exp, scale=CAP)
-            e_all.append(e)
+                capped = sb.tile([P, PASS], F32, name=f"capped{j}{h}", tag=f"capped{j}{h}", align_bytes=64)
+                nc.scalar.activation(capped[:], score[:], ACT.Tanh, scale=1.0 / CAP)
+                e = sb.tile([P, PASS], F32, name=f"e{j}{h}")
+                nc.scalar.activation(e[:], capped[:], ACT.Exp, scale=CAP)
+                e_half.append(e)
+            place_bank = ps.tile([P, 4, P], F32, name=f"place_bank{h}", tag=f"bank{h}0")
+            for c in range(4):
+                nc.tensor.transpose(place_bank[:, c, :], pos_cols[h][:, c : c + 1].to_broadcast([P, P]), ident[:])
+            for j in range(ROW_TILES):
+                nc.vector.scalar_tensor_tensor(
+                    masked_all[j][:, slots].rearrange("p (k c) -> p k c", c=4),
+                    place_bank[:].rearrange("p c k -> p k c"),
+                    q_place[:, j : j + 1],
+                    e_half[j][:].rearrange("p (k c) -> p k c", c=4),
+                    ALU.is_le,
+                    ALU.mult,
+                    accum_out=e_sum[:, h, j : j + 1],
+                )
 
-        v_bf = sb.tile([P, T], BF16, name="v_bf", tag=f"capped{ROW_TILES - 1}", align_bytes=64)
-        nc.scalar.activation(v_bf[:], v_pool[:], ACT.Copy)
-        v_slots = sb.tile([P, N], BF16, name="v_slots", align_bytes=64)
+        v_slots = sb.tile([P, N], BF16, name="v_slots", tag="capped11", align_bytes=64)
         nc.scalar.activation(v_slots[:], v_bf[:].indirect(offsets[:]), ACT.Copy)
+        v_turned = sb.tile([P, N], BF16, name="v_turned", align_bytes=64)
+        v_bank = ps.tile([P, SLOT_PASSES, 2, DV], F32, name="v_bank", tag="bank11")
+        turn(v_slots[:], v_bank[:], v_turned[:])
 
-        def turn(src, bank, dst):
-            passes = src.shape[1] // PASS
-            words = src.bitcast(F32)
-            for g in range(passes):
-                for u in range(2):
-                    nc.tensor.transpose(bank[:, g, u, :], words[:, g * 2 * P + u : (g + 1) * 2 * P : 2], ident[:])
-            nc.scalar.copy(dst.bitcast(F32).rearrange("p (g c u) -> p g c u", g=passes, u=2), bank.rearrange("p g u c -> p g c u"))
-
-        def quantise(src, name):
-            columns = src.shape[1] // 4
-            codes = sb.tile([P, columns], U32, name=name + "_code", align_bytes=64)
-            scales = sb.tile([P, columns], U8, name=name + "_scale", align_bytes=64)
-            nc.vector.quantize_mx(out=codes[:].bitcast(FP8X4), scales=scales[:], in_=src)
-            return codes, scales
-
-        e_sum = sb.tile([P, ROW_TILES], F32, name="e_sum")
         inv_top = sb.tile([P, ROW_TILES], F32, name="inv_top")
-        masked_tags = ["after_scale_gather", "after_maxima"]
         lifted_all = []
         top_all = []
         for j in range(ROW_TILES):
-            masked = sb.tile([P, N], F32, name=f"masked{j}", tag=masked_tags[j], align_bytes=64)
-            nc.vector.scalar_tensor_tensor(masked[:], pos_slots[:], q_place[:, j : j + 1], e_all[j][:], ALU.is_le, ALU.mult, accum_out=e_sum[:, j : j + 1])
-            lifted = sb.tile([P, N], F32, name=f"lifted{j}")
+            lifted = sb.tile([P, N], F32, name=f"lifted{j}", tag=f"lifted{j}", align_bytes=64)
             top = sb.tile([P, 1], F32, name=f"top{j}")
-            nc.vector.tensor_scalar(lifted[:], masked[:], floor[:], None, ALU.max, ALU.max, accum_out=top[:])
+            nc.vector.tensor_scalar(lifted[:], masked_all[j][:], floor[:], None, ALU.max, ALU.max, accum_out=top[:])
             lifted_all.append(lifted)
             top_all.append(top)
         for j in range(ROW_TILES):
             nc.vector.reciprocal(inv_top[:, j : j + 1], top_all[j][:])
 
-        v_turned = sb.tile([P, N], BF16, name="v_turned", align_bytes=64)
-        v_bank = ps.tile([P, SLOT_PASSES, 2, DV], F32, name="v_bank")
-        turn(v_slots[:], v_bank[:], v_turned[:])
-
-        w = sb.tile([P, ROW_TILES * N], BF16, name="w", tag="after_maxima", align_bytes=64)
+        w = sb.tile([P, ROW_TILES * N], BF16, name="w", align_bytes=64)
         w_turned = {}
         for j in range(ROW_TILES):
             for g in range(SLOT_PASSES):
                 slots = slice(g * PASS, (g + 1) * PASS)
                 piece = w[:, j * N + g * PASS : j * N + (g + 1) * PASS]
                 nc.vector.scalar_tensor_tensor(piece, lifted_all[j][:, slots], inv_top[:, j : j + 1], vs_slots[:, slots], ALU.mult, ALU.mult)
-                w_bank = ps.tile([P, 1, 2, P], F32, name=f"w_bank{j}{g}", tag=f"bank{j}{g}")
+                w_bank = ps.tile([P, 1, 2, P], F32, name=f"w_bank{j}{g}")
                 w_turned[j, g] = sb.tile([P, PASS], BF16, name=f"w_turned{j}{g}", align_bytes=64)
                 turn(piece, w_bank[:], w_turned[j, g][:])
 
+        e_total = sb.tile([P, ROW_TILES], F32, name="e_total")
+        nc.vector.scalar_tensor_tensor(e_total[:], e_sum[:, 0, :], floor_sum[:], e_sum[:, 1, :], ALU.add, ALU.add)
         row_sum = sb.tile([P, ROW_TILES], F32, name="row_sum")
-        nc.vector.scalar_tensor_tensor(row_sum[:], e_sum[:], floor_sum[:], inv_top[:], ALU.add, ALU.mult)
+        nc.vector.tensor_tensor(row_sum[:], e_total[:], inv_top[:], ALU.mult)
         inv_row_sum = sb.tile([P, ROW_TILES], F32, name="inv_row_sum")
         nc.vector.reciprocal(inv_row_sum[:], row_sum[:])
 
-        v_code, v_scale = quantise(v_turned[:], "v")
+        v_code, v_scale = quantise(v_turned[:], "v", "lifted0")
+        acc_tags = ["bank00", "bank10"]
         for j in range(ROW_TILES):
-            acc = ps.tile([P, DV], F32, name=f"acc{j}")
+            acc = ps.tile([P, DV], F32, name=f"acc{j}", tag=acc_tags[j])
             for g in range(SLOT_PASSES):
-                w_code, w_scale = quantise(w_turned[j, g][:], f"w{j}{g}")
+                w_code, w_scale = quantise(w_turned[j, g][:], f"w{j}{g}", f"w{j}{g}_code")
                 nc.tensor.matmul_mx(
                     out=acc[:],
                     lhsT=w_code[:].bitcast(FP8X4),

@@ -39,8 +39,9 @@ def tile_attend_soft_draft_cap_topkq256n1024t2048_kernel(tc, q_words, q_scales, 
         nc.sync.dma_start(offsets[:], offs)
         ks_pool = sb.tile([P, T], U8, name="ks_pool", tag="after_scale_gather", align_bytes=64)
         nc.sync.dma_start(ks_pool[0:QUAD, :].bitcast(I32), k_scales.rearrange("o f t -> f o t").bitcast(I32))
-        nc.vector.memset(ks_pool[QUAD : 2 * QUAD, :].bitcast(I32), 0)
-        nc.vector.memset(ks_pool[2 * QUAD : P, :].bitcast(I32), 0)
+        for rows in (slice(QUAD, 2 * QUAD), slice(2 * QUAD, P)):
+            for cols in (slice(0, T - 4), slice(T - 4, T)):
+                nc.vector.memset(ks_pool[rows, cols].bitcast(I32), 0)
         kw_pool = sb.tile([P, T], I32, name="kw_pool", align_bytes=64)
         nc.sync.dma_start(kw_pool[:], k_words[0].rearrange("p t b -> p (t b)").bitcast(I32))
         q_code = sb.tile([P, D_PASSES, NQ], I32, name="q_code", align_bytes=64)
@@ -58,19 +59,19 @@ def tile_attend_soft_draft_cap_topkq256n1024t2048_kernel(tc, q_words, q_scales, 
         nc.sync.dma_start(pos_pool[0:1, :], pos[0:1, :])
 
         log_floor = sb.tile([P, 1], F32, name="log_floor", tag="after_floor", align_bytes=64)
-        nc.vector.memset(log_floor[:], LOG_FLOOR)
+        nc.gpsimd.memset(log_floor[:], LOG_FLOOR)
         floor = sb.tile([P, 1], F32, name="floor")
         nc.scalar.activation(floor[:], log_floor[:], ACT.Exp)
         v_pool = sb.tile([P, T], F32, name="v_pool", tag="after_floor", align_bytes=64)
         nc.sync.dma_start(v_pool[:], vT)
 
+        k_scale = sb.tile([P, D_PASSES, N], U8, name="k_scale", align_bytes=64)
+        nc.gpsimd.memset(k_scale[:].bitcast(I32), 0)
+        ident = sb.tile([P, P], F32, name="ident")
+        make_identity(nc, ident[:])
         q_place = sb.tile([P, ROW_TILES], F32, name="q_place")
         with nc.allow_non_contiguous_dma(reason="one place for each query row"):
             nc.gpsimd.dma_start(q_place[:], qpos[0].rearrange("(j p) o -> p (j o)", p=P))
-        k_scale = sb.tile([P, D_PASSES, N], U8, name="k_scale", align_bytes=64)
-        nc.vector.memset(k_scale[:].bitcast(I32), 0)
-        ident = sb.tile([P, P], F32, name="ident")
-        make_identity(nc, ident[:])
         floor_sum = sb.tile([P, 1], F32, name="floor_sum")
         nc.scalar.activation(floor_sum[:], floor[:], ACT.Copy, scale=float(N))
 
@@ -144,15 +145,15 @@ def tile_attend_soft_draft_cap_topkq256n1024t2048_kernel(tc, q_words, q_scales, 
                 e = sb.tile([P, PASS], F32, name=f"e{j}{h}")
                 nc.scalar.activation(e[:], capped[:], ACT.Exp, scale=CAP)
                 e_half.append(e)
-            place_bank = ps.tile([P, 4, P], F32, name=f"place_bank{h}", tag=f"bank{h}0")
+            place_bank = ps.tile([P, P, 4], F32, name=f"place_bank{h}", tag=f"bank{h}0")
             for c in range(4):
-                nc.tensor.transpose(place_bank[:, c, :], pos_cols[h][:, c : c + 1].to_broadcast([P, P]), ident[:])
+                nc.tensor.transpose(place_bank[:, :, c], pos_cols[h][:, c : c + 1].to_broadcast([P, P]), ident[:])
             for j in range(ROW_TILES):
                 nc.vector.scalar_tensor_tensor(
-                    masked_all[j][:, slots].rearrange("p (k c) -> p k c", c=4),
-                    place_bank[:].rearrange("p c k -> p k c"),
+                    masked_all[j][:, slots],
+                    place_bank[:].rearrange("p k c -> p (k c)"),
                     q_place[:, j : j + 1],
-                    e_half[j][:].rearrange("p (k c) -> p k c", c=4),
+                    e_half[j][:],
                     ALU.is_le,
                     ALU.mult,
                     accum_out=e_sum[:, h, j : j + 1],
@@ -183,7 +184,7 @@ def tile_attend_soft_draft_cap_topkq256n1024t2048_kernel(tc, q_words, q_scales, 
                 slots = slice(g * PASS, (g + 1) * PASS)
                 piece = w[:, j * N + g * PASS : j * N + (g + 1) * PASS]
                 nc.vector.scalar_tensor_tensor(piece, lifted_all[j][:, slots], inv_top[:, j : j + 1], vs_slots[:, slots], ALU.mult, ALU.mult)
-                w_bank = ps.tile([P, 1, 2, P], F32, name=f"w_bank{j}{g}")
+                w_bank = ps.tile([P, 1, 2, P], F32, name=f"w_bank{j}{g}", tag=f"w_bank{2 * j + g}")
                 w_turned[j, g] = sb.tile([P, PASS], BF16, name=f"w_turned{j}{g}", align_bytes=64)
                 turn(piece, w_bank[:], w_turned[j, g][:])
 

@@ -32,6 +32,7 @@ def tile_attend_soft_draft_cap_topkq256n1024t2048_kernel(tc, q_words, q_scales, 
     nc = tc.nc
     with ExitStack() as ctx:
         sb = ctx.enter_context(tc.tile_pool(name="sb", bufs=1))
+        late = ctx.enter_context(tc.tile_pool(name="late", bufs=1))
         ps = ctx.enter_context(tc.psum_pool(name="ps", bufs=1))
 
 
@@ -54,24 +55,26 @@ def tile_attend_soft_draft_cap_topkq256n1024t2048_kernel(tc, q_words, q_scales, 
                 q_scales[0, :, 4 * quad : 4 * quad + 4, :].rearrange("o f q -> f o q").bitcast(I32),
             )
 
-        pos_pool = sb.tile([P, T], F32, name="pos_pool")
-        nc.gpsimd.memset(pos_pool[:], 0.0)
-        nc.sync.dma_start(pos_pool[0:1, :], pos[0:1, :])
-
-        log_floor = sb.tile([P, 1], F32, name="log_floor", tag="after_floor", align_bytes=64)
-        nc.gpsimd.memset(log_floor[:], LOG_FLOOR)
-        floor = sb.tile([P, 1], F32, name="floor")
-        nc.scalar.activation(floor[:], log_floor[:], ACT.Exp)
-        v_pool = sb.tile([P, T], F32, name="v_pool", tag="after_floor", align_bytes=64)
+        v_pool = sb.tile([P, T], F32, name="v_pool")
         nc.sync.dma_start(v_pool[:], vT)
 
-        k_scale = sb.tile([P, D_PASSES, N], U8, name="k_scale", align_bytes=64)
-        nc.gpsimd.memset(k_scale[:].bitcast(I32), 0)
+        k_scale = sb.tile([P, D_PASSES * N], U8, name="k_scale", align_bytes=64)
+        for cols in (slice(0, D_PASSES * N - 4), slice(D_PASSES * N - 4, D_PASSES * N)):
+            nc.vector.memset(k_scale[:, cols].bitcast(I32), 0)
         ident = sb.tile([P, P], F32, name="ident")
         make_identity(nc, ident[:])
         q_place = sb.tile([P, ROW_TILES], F32, name="q_place")
         with nc.allow_non_contiguous_dma(reason="one place for each query row"):
-            nc.gpsimd.dma_start(q_place[:], qpos[0].rearrange("(j p) o -> p (j o)", p=P))
+            nc.sync.dma_start(q_place[:], qpos[0].rearrange("(j p) o -> p (j o)", p=P))
+
+        pos_pool = sb.tile([P, T], F32, name="pos_pool")
+        nc.gpsimd.memset(pos_pool[:], 0.0)
+        nc.sync.dma_start(pos_pool[0:1, :], pos[0:1, :])
+
+        log_floor = sb.tile([P, 1], F32, name="log_floor")
+        nc.vector.memset(log_floor[:], LOG_FLOOR)
+        floor = sb.tile([P, 1], F32, name="floor")
+        nc.scalar.activation(floor[:], log_floor[:], ACT.Exp)
         floor_sum = sb.tile([P, 1], F32, name="floor_sum")
         nc.scalar.activation(floor_sum[:], floor[:], ACT.Copy, scale=float(N))
 
@@ -79,7 +82,7 @@ def tile_attend_soft_draft_cap_topkq256n1024t2048_kernel(tc, q_words, q_scales, 
         nc.vector.tensor_copy(ks_slots[:], ks_pool[:].indirect(offsets[:]))
         for quad in range(P // QUAD):
             nc.sync.dma_start(
-                k_scale[QUAD * quad : QUAD * quad + 4, :, :].bitcast(I32),
+                k_scale[QUAD * quad : QUAD * quad + 4, :].bitcast(I32),
                 ks_slots[8 * quad : 8 * quad + 8, :].bitcast(I32),
             )
 
@@ -103,20 +106,22 @@ def tile_attend_soft_draft_cap_topkq256n1024t2048_kernel(tc, q_words, q_scales, 
             parted = sb.tile([P, D_PASSES, PASS], U16, name=f"k_code{h}", align_bytes=64)
             nc.vector.tensor_copy(parted[:], kw_slots[:].bitcast(U16).rearrange("p (n o) -> p o n", o=D_PASSES))
             k_code.append(parted)
+        def dealt(ap):
+            return ap.rearrange("p (u gb i) -> p gb u i", u=2, i=16)
+
         vs_slots = sb.tile([P, N], F32, name="vs_slots")
-        nc.vector.tensor_copy(vs_slots[:], vs_pool[:].indirect(offsets[:]))
+        nc.vector.tensor_copy(dealt(vs_slots[:].bitcast(U32)), vs_pool[:].bitcast(U32).indirect(offsets[:]))
 
         def turn(src, bank, dst):
-            passes = src.shape[1] // PASS
             words = src.bitcast(F32)
+            passes = src.shape[1] // PASS
             for g in range(passes):
                 for u in range(2):
-                    nc.tensor.transpose(bank[:, g, u, :], words[:, g * 2 * P + u : (g + 1) * 2 * P : 2], ident[:])
+                    nc.tensor.transpose(bank[:, g, u, :], words[:, (u * passes + g) * P : (u * passes + g + 1) * P], ident[:])
             nc.scalar.copy(dst.bitcast(F32).rearrange("p (g c u) -> p g c u", g=passes, u=2), bank.rearrange("p g u c -> p g c u"))
 
-        def quantise(src, name, tag):
+        def quantise(src, name, codes):
             columns = src.shape[1] // 4
-            codes = sb.tile([P, columns], U32, name=name + "_code", tag=tag, align_bytes=64)
             scales = sb.tile([P, columns], U8, name=name + "_scale", align_bytes=64)
             nc.vector.quantize_mx(out=codes[:].bitcast(FP8X4), scales=scales[:], in_=src)
             return codes, scales
@@ -136,7 +141,7 @@ def tile_attend_soft_draft_cap_topkq256n1024t2048_kernel(tc, q_words, q_scales, 
                         lhsT=q_code[:, o, j * P : (j + 1) * P].bitcast(FP8X4),
                         lhsT_scale=q_scale[:, o, j * P : (j + 1) * P],
                         rhs=k_code[h][:, o, :].bitcast(FP4X4),
-                        rhs_scale=k_scale[:, o, slots],
+                        rhs_scale=k_scale[:, o * N + h * PASS : o * N + (h + 1) * PASS],
                         start=(o == 0),
                         stop=(o == D_PASSES - 1),
                     )
@@ -160,7 +165,7 @@ def tile_attend_soft_draft_cap_topkq256n1024t2048_kernel(tc, q_words, q_scales, 
                 )
 
         v_slots = sb.tile([P, N], BF16, name="v_slots", tag="capped11", align_bytes=64)
-        nc.scalar.activation(v_slots[:], v_bf[:].indirect(offsets[:]), ACT.Copy)
+        nc.scalar.activation(dealt(v_slots[:]), v_bf[:].indirect(offsets[:]), ACT.Copy)
         v_turned = sb.tile([P, N], BF16, name="v_turned", align_bytes=64)
         v_bank = ps.tile([P, SLOT_PASSES, 2, DV], F32, name="v_bank", tag="bank11")
         turn(v_slots[:], v_bank[:], v_turned[:])
@@ -169,38 +174,49 @@ def tile_attend_soft_draft_cap_topkq256n1024t2048_kernel(tc, q_words, q_scales, 
         lifted_all = []
         top_all = []
         for j in range(ROW_TILES):
-            lifted = sb.tile([P, N], F32, name=f"lifted{j}", tag=f"lifted{j}", align_bytes=64)
+            lifted = late.tile([P, N], F32, name=f"lifted{j}", offset=4 * N * j, align_bytes=64)
             top = sb.tile([P, 1], F32, name=f"top{j}")
-            nc.vector.tensor_scalar(lifted[:], masked_all[j][:], floor[:], None, ALU.max, ALU.max, accum_out=top[:])
+            nc.vector.tensor_scalar(dealt(lifted[:]), masked_all[j][:].rearrange("p (gb u i) -> p gb u i", u=2, i=16), floor[:], None, ALU.max, ALU.max, accum_out=top[:])
             lifted_all.append(lifted)
             top_all.append(top)
         for j in range(ROW_TILES):
             nc.vector.reciprocal(inv_top[:, j : j + 1], top_all[j][:])
 
-        w = sb.tile([P, ROW_TILES * N], BF16, name="w", align_bytes=64)
+        def of_pass(ap, g):
+            return ap.rearrange("p (u g x) -> p u g x", u=2, g=SLOT_PASSES)[:, :, g, :]
+
         w_turned = {}
         for j in range(ROW_TILES):
             for g in range(SLOT_PASSES):
-                slots = slice(g * PASS, (g + 1) * PASS)
-                piece = w[:, j * N + g * PASS : j * N + (g + 1) * PASS]
-                nc.vector.scalar_tensor_tensor(piece, lifted_all[j][:, slots], inv_top[:, j : j + 1], vs_slots[:, slots], ALU.mult, ALU.mult)
+                w = sb.tile([P, PASS], BF16, name=f"w{j}{g}", align_bytes=64)
+                last = (j, g) == (ROW_TILES - 1, SLOT_PASSES - 1)
+                for us in (slice(0, 1), slice(1, 2)) if last else (slice(0, 2),):
+                    nc.vector.scalar_tensor_tensor(
+                        w[:].rearrange("p (u x) -> p u x", u=2)[:, us, :],
+                        of_pass(lifted_all[j][:], g)[:, us, :],
+                        inv_top[:, j : j + 1],
+                        of_pass(vs_slots[:], g)[:, us, :],
+                        ALU.mult,
+                        ALU.mult,
+                    )
                 w_bank = ps.tile([P, 1, 2, P], F32, name=f"w_bank{j}{g}", tag=f"w_bank{2 * j + g}")
                 w_turned[j, g] = sb.tile([P, PASS], BF16, name=f"w_turned{j}{g}", align_bytes=64)
-                turn(piece, w_bank[:], w_turned[j, g][:])
+                turn(w[:], w_bank[:], w_turned[j, g][:])
 
-        e_total = sb.tile([P, ROW_TILES], F32, name="e_total")
+        e_total = late.tile([P, ROW_TILES], F32, name="e_total", offset=2 * N, align_bytes=64)
         nc.vector.scalar_tensor_tensor(e_total[:], e_sum[:, 0, :], floor_sum[:], e_sum[:, 1, :], ALU.add, ALU.add)
         row_sum = sb.tile([P, ROW_TILES], F32, name="row_sum")
         nc.vector.tensor_tensor(row_sum[:], e_total[:], inv_top[:], ALU.mult)
         inv_row_sum = sb.tile([P, ROW_TILES], F32, name="inv_row_sum")
         nc.vector.reciprocal(inv_row_sum[:], row_sum[:])
 
-        v_code, v_scale = quantise(v_turned[:], "v", "lifted0")
+        v_code, v_scale = quantise(v_turned[:], "v", late.tile([P, N // 4], U32, name="v_code", offset=0, align_bytes=64))
+        store_queues = [nc.sync, nc.scalar]
         acc_tags = ["bank00", "bank10"]
         for j in range(ROW_TILES):
             acc = ps.tile([P, DV], F32, name=f"acc{j}", tag=acc_tags[j])
             for g in range(SLOT_PASSES):
-                w_code, w_scale = quantise(w_turned[j, g][:], f"w{j}{g}", f"w{j}{g}_code")
+                w_code, w_scale = quantise(w_turned[j, g][:], f"w{j}{g}", sb.tile([P, PASS // 4], U32, name=f"w{j}{g}_code", align_bytes=64))
                 nc.tensor.matmul_mx(
                     out=acc[:],
                     lhsT=w_code[:].bitcast(FP8X4),
@@ -212,4 +228,4 @@ def tile_attend_soft_draft_cap_topkq256n1024t2048_kernel(tc, q_words, q_scales, 
                 )
             result = sb.tile([P, DV], F32, name=f"result{j}")
             nc.scalar.activation(result[:], acc[:], ACT.Copy, scale=inv_row_sum[:, j : j + 1])
-            nc.sync.dma_start(out[0, j * P : (j + 1) * P, :], result[:])
+            store_queues[j].dma_start(out[0, j * P : (j + 1) * P, :], result[:])

@@ -39,14 +39,12 @@ def tile_attend_soft_draft_cap_topkq256n1024t2048_kernel(tc, q_words, q_scales, 
         offsets = sb.tile([P, N // LIST_ROWS], U16, name="offsets")
         nc.sync.dma_start(offsets[:], offs)
         ks_pool = sb.tile([P, T], U8, name="ks_pool", tag="after_scale_gather", align_bytes=64)
-        nc.sync.dma_start(ks_pool[0:QUAD, :].bitcast(I32), k_scales.rearrange("o f t -> f o t").bitcast(I32))
+        nc.scalar.dma_start(ks_pool[0:QUAD, :].bitcast(I32), k_scales.rearrange("o f t -> f o t").bitcast(I32))
         for rows in (slice(QUAD, 2 * QUAD), slice(2 * QUAD, P)):
             for cols in (slice(0, T - 4), slice(T - 4, T)):
                 nc.vector.memset(ks_pool[rows, cols].bitcast(I32), 0)
         kw_pool = sb.tile([P, T], I32, name="kw_pool", align_bytes=64)
         nc.sync.dma_start(kw_pool[:], k_words[0].rearrange("p t b -> p (t b)").bitcast(I32))
-        q_code = sb.tile([P, D_PASSES, NQ], I32, name="q_code", align_bytes=64)
-        nc.sync.dma_start(q_code[:], q_words[0].rearrange("o p q r -> p o (q r)").bitcast(I32))
         q_scale = sb.tile([P, D_PASSES, NQ], U8, name="q_scale", align_bytes=64)
         nc.gpsimd.memset(q_scale[:].bitcast(I32), 0)
         for quad in range(P // QUAD):
@@ -55,8 +53,13 @@ def tile_attend_soft_draft_cap_topkq256n1024t2048_kernel(tc, q_words, q_scales, 
                 q_scales[0, :, 4 * quad : 4 * quad + 4, :].rearrange("o f q -> f o q").bitcast(I32),
             )
 
-        v_pool = sb.tile([P, T], F32, name="v_pool")
-        nc.sync.dma_start(v_pool[:], vT)
+        v_halves = []
+        for half in range(2):
+            v_pool = sb.tile([P, T // 2], F32, name=f"v_pool{half}")
+            nc.sync.dma_start(v_pool[:], vT[:, half * T // 2 : (half + 1) * T // 2])
+            v_halves.append(v_pool)
+        q_code = sb.tile([P, D_PASSES, NQ], I32, name="q_code", align_bytes=64)
+        nc.sync.dma_start(q_code[:], q_words[0].rearrange("o p q r -> p o (q r)").bitcast(I32))
 
         k_scale = sb.tile([P, D_PASSES * N], U8, name="k_scale", align_bytes=64)
         for cols in (slice(0, D_PASSES * N - 4), slice(D_PASSES * N - 4, D_PASSES * N)):
@@ -90,7 +93,8 @@ def tile_attend_soft_draft_cap_topkq256n1024t2048_kernel(tc, q_words, q_scales, 
         nc.sync.dma_start(vs_pool[:], vs)
 
         v_bf = sb.tile([P, T], BF16, name="v_bf", align_bytes=64)
-        nc.scalar.activation(v_bf[:], v_pool[:], ACT.Copy)
+        for half in range(2):
+            nc.scalar.activation(v_bf[:, half * T // 2 : (half + 1) * T // 2], v_halves[half][:], ACT.Copy)
 
         k_code = []
         pos_cols = []
@@ -112,13 +116,13 @@ def tile_attend_soft_draft_cap_topkq256n1024t2048_kernel(tc, q_words, q_scales, 
         vs_slots = sb.tile([P, N], F32, name="vs_slots")
         nc.vector.tensor_copy(dealt(vs_slots[:].bitcast(U32)), vs_pool[:].bitcast(U32).indirect(offsets[:]))
 
-        def turn(src, bank, dst):
+        def turn(src, bank):
             words = src.bitcast(F32)
-            passes = src.shape[1] // PASS
-            for g in range(passes):
-                for u in range(2):
-                    nc.tensor.transpose(bank[:, g, u, :], words[:, (u * passes + g) * P : (u * passes + g + 1) * P], ident[:])
-            nc.scalar.copy(dst.bitcast(F32).rearrange("p (g c u) -> p g c u", g=passes, u=2), bank.rearrange("p g u c -> p g c u"))
+            for u in range(2):
+                nc.tensor.transpose(bank[:, u, :], words[:, u * P : (u + 1) * P], ident[:])
+
+        def lay(bank, dst):
+            nc.scalar.copy(dst.bitcast(F32).rearrange("p (g c u) -> p g c u", g=bank.shape[1], u=2), bank.rearrange("p g u c -> p g c u"))
 
         def quantise(src, name, codes):
             columns = src.shape[1] // 4
@@ -127,12 +131,9 @@ def tile_attend_soft_draft_cap_topkq256n1024t2048_kernel(tc, q_words, q_scales, 
             return codes, scales
 
 
-        e_sum = sb.tile([P, SLOT_PASSES, ROW_TILES], F32, name="e_sum")
-        masked_tags = ["after_scale_gather", "masked1"]
-        masked_all = [sb.tile([P, N], F32, name=f"masked{j}", tag=masked_tags[j], align_bytes=64) for j in range(ROW_TILES)]
+        e_all = {}
+        place_banks = []
         for h in range(SLOT_PASSES):
-            slots = slice(h * PASS, (h + 1) * PASS)
-            e_half = []
             for j in range(ROW_TILES):
                 score = ps.tile([P, PASS], F32, name=f"score{j}{h}", tag=f"bank{j}{h}")
                 for o in range(D_PASSES):
@@ -147,63 +148,94 @@ def tile_attend_soft_draft_cap_topkq256n1024t2048_kernel(tc, q_words, q_scales, 
                     )
                 capped = sb.tile([P, PASS], F32, name=f"capped{j}{h}", tag=f"capped{j}{h}", align_bytes=64)
                 nc.scalar.activation(capped[:], score[:], ACT.Tanh, scale=1.0 / CAP)
-                e = sb.tile([P, PASS], F32, name=f"e{j}{h}")
-                nc.scalar.activation(e[:], capped[:], ACT.Exp, scale=CAP)
-                e_half.append(e)
+                e_all[j, h] = sb.tile([P, PASS], F32, name=f"e{j}{h}")
+                nc.scalar.activation(e_all[j, h][:], capped[:], ACT.Exp, scale=CAP)
             place_bank = ps.tile([P, P, 4], F32, name=f"place_bank{h}", tag=f"bank{h}0")
             for c in range(4):
                 nc.tensor.transpose(place_bank[:, :, c], pos_cols[h][:, c : c + 1].to_broadcast([P, P]), ident[:])
-            for j in range(ROW_TILES):
-                nc.vector.scalar_tensor_tensor(
-                    masked_all[j][:, slots],
-                    place_bank[:].rearrange("p k c -> p (k c)"),
-                    q_place[:, j : j + 1],
-                    e_half[j][:],
-                    ALU.is_le,
-                    ALU.mult,
-                    accum_out=e_sum[:, h, j : j + 1],
-                )
+            place_banks.append(place_bank)
 
-        v_slots = sb.tile([P, N], BF16, name="v_slots", tag="capped11", align_bytes=64)
-        nc.scalar.activation(dealt(v_slots[:]), v_bf[:].indirect(offsets[:]), ACT.Copy)
+        v_slot_tags = ["v_slots0", "capped11"]
         v_turned = sb.tile([P, N], BF16, name="v_turned", align_bytes=64)
         v_bank = ps.tile([P, SLOT_PASSES, 2, DV], F32, name="v_bank", tag="bank11")
-        turn(v_slots[:], v_bank[:], v_turned[:])
+        for g in range(SLOT_PASSES):
+            v_slots = sb.tile([P, PASS], BF16, name=f"v_slots{g}", tag=v_slot_tags[g], align_bytes=64)
+            entries = offsets[:, g * PASS // LIST_ROWS : (g + 1) * PASS // LIST_ROWS]
+            nc.scalar.activation(dealt(v_slots[:]), v_bf[:].indirect(entries), ACT.Copy)
+            turn(v_slots[:], v_bank[:, g])
+        lay(v_bank[:], v_turned[:])
 
+        e_sum = sb.tile([P, SLOT_PASSES, ROW_TILES], F32, name="e_sum")
         inv_top = sb.tile([P, ROW_TILES], F32, name="inv_top")
-        lifted_all = []
-        top_all = []
-        for j in range(ROW_TILES):
-            lifted = late.tile([P, N], F32, name=f"lifted{j}", offset=4 * N * j, align_bytes=64)
-            top = sb.tile([P, 1], F32, name=f"top{j}")
-            nc.vector.tensor_scalar(dealt(lifted[:]), masked_all[j][:].rearrange("p (gb u i) -> p gb u i", u=2, i=16), floor[:], None, ALU.max, ALU.max, accum_out=top[:])
-            lifted_all.append(lifted)
-            top_all.append(top)
-        for j in range(ROW_TILES):
-            nc.vector.reciprocal(inv_top[:, j : j + 1], top_all[j][:])
+        top_offsets = [N + 128, N - 64]
+        masked, lifted, top, scaled, w_turned = {}, {}, {}, {}, {}
 
-        def of_pass(ap, g):
-            return ap.rearrange("p (u g x) -> p u g x", u=2, g=SLOT_PASSES)[:, :, g, :]
+        def mask(j, h):
+            tag = "capped10" if (j, h) == (0, 0) else f"masked{j}{h}"
+            masked[j, h] = sb.tile([P, PASS], F32, name=f"masked{j}{h}", tag=tag, align_bytes=64)
+            nc.vector.scalar_tensor_tensor(
+                masked[j, h][:], place_banks[h][:].rearrange("p k c -> p (k c)"), q_place[:, j : j + 1], e_all[j, h][:], ALU.is_le, ALU.mult, accum_out=e_sum[:, h, j : j + 1]
+            )
 
-        w_turned = {}
-        for j in range(ROW_TILES):
-            for g in range(SLOT_PASSES):
-                w = sb.tile([P, PASS], BF16, name=f"w{j}{g}", align_bytes=64)
-                last = (j, g) == (ROW_TILES - 1, SLOT_PASSES - 1)
-                for us in (slice(0, 1), slice(1, 2)) if last else (slice(0, 2),):
-                    nc.vector.scalar_tensor_tensor(
-                        w[:].rearrange("p (u x) -> p u x", u=2)[:, us, :],
-                        of_pass(lifted_all[j][:], g)[:, us, :],
-                        inv_top[:, j : j + 1],
-                        of_pass(vs_slots[:], g)[:, us, :],
-                        ALU.mult,
-                        ALU.mult,
-                    )
-                w_bank = ps.tile([P, 1, 2, P], F32, name=f"w_bank{j}{g}", tag=f"w_bank{2 * j + g}")
-                w_turned[j, g] = sb.tile([P, PASS], BF16, name=f"w_turned{j}{g}", align_bytes=64)
-                turn(w[:], w_bank[:], w_turned[j, g][:])
+        def lift(j, h):
+            lifted[j, h] = sb.tile([P, PASS], F32, name=f"lifted{j}{h}")
+            if h == 0:
+                top[j, h] = sb.tile([P, 1], F32, name=f"top{j}{h}")
+            else:
+                top[j, h] = late.tile([P, 32], F32, name=f"top{j}{h}", offset=top_offsets[j], align_bytes=64)
+            nc.vector.tensor_scalar(
+                dealt(lifted[j, h][:]),
+                masked[j, h][:].rearrange("p (gb u i) -> p gb u i", u=2, i=16),
+                floor[:],
+                top[j, h - 1][:, 0:1] if h else None,
+                ALU.max,
+                ALU.max,
+                accum_out=top[j, h][:, 0:1],
+            )
 
-        e_total = late.tile([P, ROW_TILES], F32, name="e_total", offset=2 * N, align_bytes=64)
+        def invert(j):
+            nc.vector.reciprocal(inv_top[:, j : j + 1], top[j, SLOT_PASSES - 1][:, 0:1])
+
+        def halves(ap):
+            return ap.rearrange("p (u x) -> p u x", u=2)
+
+        def token_scales(g):
+            return vs_slots[:].rearrange("p (u g x) -> p u g x", u=2, g=SLOT_PASSES)[:, :, g, :]
+
+        def scale(j, g):
+            scaled[j, g] = sb.tile([P, PASS], F32, name=f"scaled{j}{g}")
+            nc.gpsimd.tensor_tensor(halves(scaled[j, g][:]), halves(lifted[j, g][:]), token_scales(g), ALU.mult)
+
+        def weigh(j, g, pieces):
+            w = sb.tile([P, PASS], BF16, name=f"w{j}{g}", align_bytes=64)
+            if (j, g) in scaled:
+                nc.scalar.activation(w[:], scaled[j, g][:], ACT.Copy, scale=inv_top[:, j : j + 1])
+            for us in pieces:
+                nc.vector.scalar_tensor_tensor(halves(w[:])[:, us, :], halves(lifted[j, g][:])[:, us, :], inv_top[:, j : j + 1], token_scales(g)[:, us, :], ALU.mult, ALU.mult)
+            w_bank = ps.tile([P, 1, 2, P], F32, name=f"w_bank{j}{g}", tag=f"w_bank{2 * j + g}")
+            w_turned[j, g] = sb.tile([P, PASS], BF16, name=f"w_turned{j}{g}", align_bytes=64)
+            turn(w[:], w_bank[:, 0])
+            lay(w_bank[:], w_turned[j, g][:])
+
+        whole = [slice(0, 2)]
+        mask(0, 0)
+        mask(1, 0)
+        lift(0, 0)
+        scale(0, 0)
+        mask(0, 1)
+        lift(1, 0)
+        scale(1, 0)
+        lift(0, 1)
+        mask(1, 1)
+        invert(0)
+        lift(1, 1)
+        weigh(0, 0, [])
+        weigh(0, 1, whole)
+        invert(1)
+        weigh(1, 0, [])
+        weigh(1, 1, [slice(0, 1), slice(1, 2)])
+
+        e_total = late.tile([P, ROW_TILES], F32, name="e_total", offset=N, align_bytes=64)
         nc.vector.scalar_tensor_tensor(e_total[:], e_sum[:, 0, :], floor_sum[:], e_sum[:, 1, :], ALU.add, ALU.add)
         row_sum = sb.tile([P, ROW_TILES], F32, name="row_sum")
         nc.vector.tensor_tensor(row_sum[:], e_total[:], inv_top[:], ALU.mult)

@@ -39,7 +39,7 @@ def tile_attend_soft_draft_cap_topkq256n1024t2048_kernel(tc, q_words, q_scales, 
         offsets = sb.tile([P, N // LIST_ROWS], U16, name="offsets")
         nc.sync.dma_start(offsets[:], offs)
         ks_pool = sb.tile([P, T], U8, name="ks_pool", tag="after_scale_gather", align_bytes=64)
-        nc.scalar.dma_start(ks_pool[0:QUAD, :].bitcast(I32), k_scales.rearrange("o f t -> f o t").bitcast(I32))
+        nc.sync.dma_start(ks_pool[0:QUAD, :].bitcast(I32), k_scales.rearrange("o f t -> f o t").bitcast(I32))
         for rows in (slice(QUAD, 2 * QUAD), slice(2 * QUAD, P)):
             for cols in (slice(0, T - 4), slice(T - 4, T)):
                 nc.vector.memset(ks_pool[rows, cols].bitcast(I32), 0)
@@ -150,7 +150,7 @@ def tile_attend_soft_draft_cap_topkq256n1024t2048_kernel(tc, q_words, q_scales, 
                 nc.scalar.activation(capped[:], score[:], ACT.Tanh, scale=1.0 / CAP)
                 e_all[j, h] = sb.tile([P, PASS], F32, name=f"e{j}{h}")
                 nc.scalar.activation(e_all[j, h][:], capped[:], ACT.Exp, scale=CAP)
-            place_bank = ps.tile([P, P, 4], F32, name=f"place_bank{h}", tag=f"bank{h}0")
+            place_bank = ps.tile([P, P, 4], F32, name=f"place_bank{h}", tag=f"bank{1 - h}{h}")
             for c in range(4):
                 nc.tensor.transpose(place_bank[:, :, c], pos_cols[h][:, c : c + 1].to_broadcast([P, P]), ident[:])
             place_banks.append(place_bank)

@@ -32,7 +32,6 @@ def tile_attend_soft_draft_cap_topkq256n1024t2048_kernel(tc, q_words, q_scales, 
     nc = tc.nc
     with ExitStack() as ctx:
         sb = ctx.enter_context(tc.tile_pool(name="sb", bufs=1))
-        late = ctx.enter_context(tc.tile_pool(name="late", bufs=1))
         ps = ctx.enter_context(tc.psum_pool(name="ps", bufs=1))
 
 
@@ -66,9 +65,6 @@ def tile_attend_soft_draft_cap_topkq256n1024t2048_kernel(tc, q_words, q_scales, 
             nc.vector.memset(k_scale[:, cols].bitcast(I32), 0)
         ident = sb.tile([P, P], F32, name="ident")
         make_identity(nc, ident[:])
-        q_place = sb.tile([P, ROW_TILES], F32, name="q_place")
-        with nc.allow_non_contiguous_dma(reason="one place for each query row"):
-            nc.sync.dma_start(q_place[:], qpos[0].rearrange("(j p) o -> p (j o)", p=P))
 
         pos_pool = sb.tile([P, T], F32, name="pos_pool")
         nc.gpsimd.memset(pos_pool[:], 0.0)
@@ -81,7 +77,7 @@ def tile_attend_soft_draft_cap_topkq256n1024t2048_kernel(tc, q_words, q_scales, 
         floor_sum = sb.tile([P, 1], F32, name="floor_sum")
         nc.scalar.activation(floor_sum[:], floor[:], ACT.Copy, scale=float(N))
 
-        ks_slots = sb.tile([P, N], U8, name="ks_slots", align_bytes=64)
+        ks_slots = sb.tile([P, N], U8, name="ks_slots", tag="after_scale_moves", align_bytes=64)
         nc.vector.tensor_copy(ks_slots[:], ks_pool[:].indirect(offsets[:]))
         for quad in range(P // QUAD):
             nc.sync.dma_start(
@@ -92,6 +88,9 @@ def tile_attend_soft_draft_cap_topkq256n1024t2048_kernel(tc, q_words, q_scales, 
         vs_pool = sb.tile([P, T], F32, name="vs_pool", tag="after_scale_gather", align_bytes=64)
         nc.sync.dma_start(vs_pool[:], vs)
 
+        q_place = sb.tile([P, ROW_TILES], F32, name="q_place", tag="after_scale_moves", align_bytes=64)
+        with nc.allow_non_contiguous_dma(reason="one place for each query row"):
+            nc.sync.dma_start(q_place[:], qpos[0].rearrange("(j p) o -> p (j o)", p=P))
         v_bf = sb.tile([P, T], BF16, name="v_bf", align_bytes=64)
         for half in range(2):
             nc.scalar.activation(v_bf[:, half * T // 2 : (half + 1) * T // 2], v_halves[half][:], ACT.Copy)
@@ -166,8 +165,9 @@ def tile_attend_soft_draft_cap_topkq256n1024t2048_kernel(tc, q_words, q_scales, 
         lay(v_bank[:], v_turned[:])
 
         e_sum = sb.tile([P, SLOT_PASSES, ROW_TILES], F32, name="e_sum")
-        inv_top = sb.tile([P, ROW_TILES], F32, name="inv_top")
-        top_offsets = [N + 128, N - 64]
+        stats = sb.tile([P, 2 * ROW_TILES], F32, name="stats")
+        inv_stats = sb.tile([P, 2 * ROW_TILES], F32, name="inv_stats")
+        inv_top = inv_stats[:, :ROW_TILES]
         masked, lifted, top, scaled, w_turned = {}, {}, {}, {}, {}
 
         def mask(j, h):
@@ -178,23 +178,20 @@ def tile_attend_soft_draft_cap_topkq256n1024t2048_kernel(tc, q_words, q_scales, 
             )
 
         def lift(j, h):
-            lifted[j, h] = sb.tile([P, PASS], F32, name=f"lifted{j}{h}")
-            if h == 0:
-                top[j, h] = sb.tile([P, 1], F32, name=f"top{j}{h}")
-            else:
-                top[j, h] = late.tile([P, 32], F32, name=f"top{j}{h}", offset=top_offsets[j], align_bytes=64)
+            lifted[j, h] = sb.tile([P, PASS], F32, name=f"lifted{j}{h}", tag=f"lifted{j}{h}", align_bytes=64)
+            top[j, h] = stats[:, j : j + 1] if h else sb.tile([P, 1], F32, name=f"top{j}")[:]
             nc.vector.tensor_scalar(
                 dealt(lifted[j, h][:]),
                 masked[j, h][:].rearrange("p (gb u i) -> p gb u i", u=2, i=16),
                 floor[:],
-                top[j, h - 1][:, 0:1] if h else None,
+                top[j, h - 1] if h else None,
                 ALU.max,
                 ALU.max,
-                accum_out=top[j, h][:, 0:1],
+                accum_out=top[j, h],
             )
 
-        def invert(j):
-            nc.vector.reciprocal(inv_top[:, j : j + 1], top[j, SLOT_PASSES - 1][:, 0:1])
+        def invert(cols):
+            nc.vector.reciprocal(inv_stats[:, cols], stats[:, cols])
 
         def halves(ap):
             return ap.rearrange("p (u x) -> p u x", u=2)
@@ -203,7 +200,7 @@ def tile_attend_soft_draft_cap_topkq256n1024t2048_kernel(tc, q_words, q_scales, 
             return vs_slots[:].rearrange("p (u g x) -> p u g x", u=2, g=SLOT_PASSES)[:, :, g, :]
 
         def scale(j, g):
-            scaled[j, g] = sb.tile([P, PASS], F32, name=f"scaled{j}{g}")
+            scaled[j, g] = sb.tile([P, PASS], F32, name=f"scaled{j}{g}", tag=f"scaled{j}{g}", align_bytes=64)
             nc.gpsimd.tensor_tensor(halves(scaled[j, g][:]), halves(lifted[j, g][:]), token_scales(g), ALU.mult)
 
         def weigh(j, g, pieces):
@@ -227,22 +224,19 @@ def tile_attend_soft_draft_cap_topkq256n1024t2048_kernel(tc, q_words, q_scales, 
         scale(1, 0)
         lift(0, 1)
         mask(1, 1)
-        invert(0)
+        invert(slice(0, 1))
+        nc.vector.scalar_tensor_tensor(stats[:, ROW_TILES:], e_sum[:, 0, :], floor_sum[:], e_sum[:, 1, :], ALU.add, ALU.add)
         lift(1, 1)
         weigh(0, 0, [])
         weigh(0, 1, whole)
-        invert(1)
+        invert(slice(1, 2 * ROW_TILES))
         weigh(1, 0, [])
         weigh(1, 1, [slice(0, 1), slice(1, 2)])
 
-        e_total = late.tile([P, ROW_TILES], F32, name="e_total", offset=N, align_bytes=64)
-        nc.vector.scalar_tensor_tensor(e_total[:], e_sum[:, 0, :], floor_sum[:], e_sum[:, 1, :], ALU.add, ALU.add)
-        row_sum = sb.tile([P, ROW_TILES], F32, name="row_sum")
-        nc.vector.tensor_tensor(row_sum[:], e_total[:], inv_top[:], ALU.mult)
         inv_row_sum = sb.tile([P, ROW_TILES], F32, name="inv_row_sum")
-        nc.vector.reciprocal(inv_row_sum[:], row_sum[:])
+        nc.gpsimd.tensor_tensor(inv_row_sum[:], inv_stats[:, ROW_TILES:], stats[:, :ROW_TILES], ALU.mult)
 
-        v_code, v_scale = quantise(v_turned[:], "v", late.tile([P, N // 4], U32, name="v_code", offset=0, align_bytes=64))
+        v_code, v_scale = quantise(v_turned[:], "v", sb.tile([P, N // 4], U32, name="v_code", tag="lifted11", align_bytes=64))
         store_queues = [nc.sync, nc.scalar]
         acc_tags = ["bank00", "bank10"]
         for j in range(ROW_TILES):

@@ -107,7 +107,9 @@ def tile_attend_soft_draft_cap_topkq256n1024t2048_kernel(tc, q_words, q_scales, 
             nc.sync.dma_start(cols[:], pos_slots[0:1, :])
             pos_cols.append(cols)
             parted = sb.tile([P, D_PASSES, PASS], U16, name=f"k_code{h}", align_bytes=64)
-            nc.vector.tensor_copy(parted[:], kw_slots[:].bitcast(U16).rearrange("p (n o) -> p o n", o=D_PASSES))
+            nc.vector.tensor_copy(
+                parted[:].rearrange("p o (a n) -> p a o n", a=2), kw_slots[:].bitcast(U16).rearrange("p (a n o) -> p a o n", a=2, o=D_PASSES)
+            )
             k_code.append(parted)
         def dealt(ap):
             return ap.rearrange("p (u gb i) -> p gb u i", u=2, i=16)

@@ -26,6 +26,8 @@ LIST_ROWS = 16
 D_PASSES = D // PASS
 SLOT_PASSES = N // PASS
 ROW_TILES = NQ // P
+CHUNKS = PASS // P
+LIVE = P - 1
 
 
 def tile_attend_soft_draft_cap_topkq256n1024t2048_kernel(tc, q_words, q_scales, k_words, k_scales, vT, vs, pos, qpos, offs, out):
@@ -34,96 +36,109 @@ def tile_attend_soft_draft_cap_topkq256n1024t2048_kernel(tc, q_words, q_scales, 
         sb = ctx.enter_context(tc.tile_pool(name="sb", bufs=1))
         ps = ctx.enter_context(tc.psum_pool(name="ps", bufs=1))
 
-
         offsets = sb.tile([P, N // LIST_ROWS], U16, name="offsets")
         nc.sync.dma_start(offsets[:], offs)
         ks_pool = sb.tile([P, T], U8, name="ks_pool", tag="after_scale_gather", align_bytes=64)
-        nc.sync.dma_start(ks_pool[0:QUAD, :].bitcast(I32), k_scales.rearrange("o f t -> f o t").bitcast(I32))
-        for rows in (slice(QUAD, 2 * QUAD), slice(2 * QUAD, P)):
-            for cols in (slice(0, T - 4), slice(T - 4, T)):
-                nc.vector.memset(ks_pool[rows, cols].bitcast(I32), 0)
+        nc.sync.dma_start(ks_pool[P - QUAD :, :].bitcast(I32), k_scales.rearrange("o f t -> f o t").bitcast(I32))
+        pos_pool = sb.tile([P, T], F32, name="pos_pool")
+        nc.sync.dma_start(pos_pool[LIVE:, :], pos[0:1, :])
+        vs_pool = sb.tile([P, T], F32, name="vs_pool")
+        nc.sync.dma_start(vs_pool[LIVE:, :], vs[0:1, :])
         kw_pool = sb.tile([P, T], I32, name="kw_pool", align_bytes=64)
         nc.sync.dma_start(kw_pool[:], k_words[0].rearrange("p t b -> p (t b)").bitcast(I32))
-        q_scale = sb.tile([P, D_PASSES, NQ], U8, name="q_scale", align_bytes=64)
-        nc.gpsimd.memset(q_scale[:].bitcast(I32), 0)
+        q_place = sb.tile([P, ROW_TILES], F32, name="q_place")
+        with nc.allow_non_contiguous_dma(reason="one place for each query row"):
+            nc.sync.dma_start(q_place[:], qpos[0].rearrange("(j p) o -> p (j o)", p=P))
+
+        def zero_words(words):
+            last = words.shape[1] - 1
+            nc.vector.memset(words[:, :last], 0)
+            nc.vector.memset(words[:, last:], 0)
+
+        q_scale = sb.tile([P, D_PASSES * NQ], U8, name="q_scale", align_bytes=64)
+        zero_words(q_scale[:].bitcast(I32))
+        log_floor = sb.tile([P, 1], F32, name="log_floor", tag="after_floor", align_bytes=64)
+        nc.vector.memset(log_floor[:], LOG_FLOOR)
+        zero_words(ks_pool[: P - QUAD, :].bitcast(I32))
+        k_scale = sb.tile([P, D_PASSES * N], U8, name="k_scale", align_bytes=64)
+        zero_words(k_scale[:].bitcast(I32))
         for quad in range(P // QUAD):
             nc.sync.dma_start(
-                q_scale[QUAD * quad : QUAD * quad + 4, :, :].bitcast(I32),
+                q_scale[QUAD * quad : QUAD * quad + 4, :].rearrange("p (o q) -> p o q", o=D_PASSES).bitcast(I32),
                 q_scales[0, :, 4 * quad : 4 * quad + 4, :].rearrange("o f q -> f o q").bitcast(I32),
             )
-
-        v_halves = []
-        for half in range(2):
-            v_pool = sb.tile([P, T // 2], F32, name=f"v_pool{half}")
-            nc.sync.dma_start(v_pool[:], vT[:, half * T // 2 : (half + 1) * T // 2])
-            v_halves.append(v_pool)
-        q_code = sb.tile([P, D_PASSES, NQ], I32, name="q_code", align_bytes=64)
-        nc.sync.dma_start(q_code[:], q_words[0].rearrange("o p q r -> p o (q r)").bitcast(I32))
-
-        k_scale = sb.tile([P, D_PASSES * N], U8, name="k_scale", align_bytes=64)
-        for cols in (slice(0, D_PASSES * N - 4), slice(D_PASSES * N - 4, D_PASSES * N)):
-            nc.vector.memset(k_scale[:, cols].bitcast(I32), 0)
         ident = sb.tile([P, P], F32, name="ident")
         make_identity(nc, ident[:])
+        nc.gpsimd.memset(pos_pool[:LIVE, :], 0.0)
+        nc.gpsimd.memset(vs_pool[:LIVE, :], 0.0)
 
-        pos_pool = sb.tile([P, T], F32, name="pos_pool")
-        nc.gpsimd.memset(pos_pool[:], 0.0)
-        nc.sync.dma_start(pos_pool[0:1, :], pos[0:1, :])
-
-        log_floor = sb.tile([P, 1], F32, name="log_floor")
-        nc.vector.memset(log_floor[:], LOG_FLOOR)
         floor = sb.tile([P, 1], F32, name="floor")
         nc.scalar.activation(floor[:], log_floor[:], ACT.Exp)
+        q_code = sb.tile([P, D_PASSES, NQ], I32, name="q_code", tag="after_floor", align_bytes=64)
+        nc.sync.dma_start(q_code[:], q_words[0].rearrange("o p q r -> p o (q r)").bitcast(I32))
         floor_sum = sb.tile([P, 1], F32, name="floor_sum")
         nc.scalar.activation(floor_sum[:], floor[:], ACT.Copy, scale=float(N))
+
+        def entries(h):
+            return offsets[:, h * PASS // LIST_ROWS : (h + 1) * PASS // LIST_ROWS]
 
         ks_slots = sb.tile([P, N], U8, name="ks_slots", tag="after_scale_moves", align_bytes=64)
         nc.vector.tensor_copy(ks_slots[:], ks_pool[:].indirect(offsets[:]))
         for quad in range(P // QUAD):
             nc.sync.dma_start(
                 k_scale[QUAD * quad : QUAD * quad + 4, :].bitcast(I32),
-                ks_slots[8 * quad : 8 * quad + 8, :].bitcast(I32),
+                ks_slots[P - QUAD + 8 * quad : P - QUAD + 8 * quad + 8, :].bitcast(I32),
             )
-
-        vs_pool = sb.tile([P, T], F32, name="vs_pool", tag="after_scale_gather", align_bytes=64)
-        nc.sync.dma_start(vs_pool[:], vs)
-
-        q_place = sb.tile([P, ROW_TILES], F32, name="q_place", tag="after_scale_moves", align_bytes=64)
-        with nc.allow_non_contiguous_dma(reason="one place for each query row"):
-            nc.sync.dma_start(q_place[:], qpos[0].rearrange("(j p) o -> p (j o)", p=P))
-        v_bf = sb.tile([P, T], BF16, name="v_bf", align_bytes=64)
-        for half in range(2):
-            nc.scalar.activation(v_bf[:, half * T // 2 : (half + 1) * T // 2], v_halves[half][:], ACT.Copy)
+        v_pool = sb.tile([P, T], F32, name="v_pool", tag="after_scale_gather", align_bytes=64)
+        nc.sync.dma_start(v_pool[:], vT)
 
         k_code = []
-        pos_cols = []
         for h in range(SLOT_PASSES):
-            kw_slots = sb.tile([P, PASS], U32, name=f"kw_slots{h}", align_bytes=64)
-            entries = offsets[:, h * PASS // LIST_ROWS : (h + 1) * PASS // LIST_ROWS]
-            nc.vector.tensor_copy(kw_slots[:], kw_pool[:].bitcast(U32).indirect(entries))
-            pos_slots = sb.tile([P, PASS], F32, name=f"pos_slots{h}")
-            nc.vector.tensor_copy(pos_slots[:], pos_pool[:].indirect(entries))
-            cols = sb.tile([P, 4], F32, name=f"pos_cols{h}")
-            nc.sync.dma_start(cols[:], pos_slots[0:1, :])
-            pos_cols.append(cols)
             parted = sb.tile([P, D_PASSES, PASS], U16, name=f"k_code{h}", align_bytes=64)
-            nc.vector.tensor_copy(
-                parted[:].rearrange("p o (a n) -> p a o n", a=2), kw_slots[:].bitcast(U16).rearrange("p (a n o) -> p a o n", a=2, o=D_PASSES)
-            )
+            gathered = []
+            for a in range(2):
+                kw_slots = sb.tile([P, PASS // 2], U32, name=f"kw_slots{h}{a}", tag=f"kw_slots{a}", align_bytes=64)
+                first = (2 * h + a) * PASS // 2 // LIST_ROWS
+                nc.vector.tensor_copy(kw_slots[:], kw_pool[:].bitcast(U32).indirect(offsets[:, first : first + PASS // 2 // LIST_ROWS]))
+                gathered.append(kw_slots)
+            for a in range(2):
+                nc.vector.tensor_copy(
+                    parted[:, :, a * PASS // 2 : (a + 1) * PASS // 2].rearrange("p o (b n) -> p b o n", b=2),
+                    gathered[a][:].bitcast(U16).rearrange("p (b n o) -> p b o n", b=2, o=D_PASSES),
+                )
             k_code.append(parted)
-        def dealt(ap):
-            return ap.rearrange("p (u gb i) -> p gb u i", u=2, i=16)
 
-        vs_slots = sb.tile([P, N], F32, name="vs_slots")
-        nc.vector.tensor_copy(dealt(vs_slots[:].bitcast(U32)), vs_pool[:].bitcast(U32).indirect(offsets[:]))
+        def gather_row(pool, h, name):
+            slots = sb.tile([P, PASS], F32, name=f"{name}_slots{h}")
+            nc.scalar.activation(slots[:], pool[:].indirect(entries(h)), ACT.Copy)
+            return slots
+
+        def to_columns(slots, name, tag):
+            bank = ps.tile([P, CHUNKS, P], F32, name=name + "_turned", tag=tag)
+            for c in range(CHUNKS):
+                nc.tensor.transpose(bank[:, c, :], slots[:, c * P : (c + 1) * P], ident[:])
+            cols = sb.tile([P, CHUNKS], F32, name=name + "_cols")
+            nc.scalar.copy(cols[:], bank[:, :, LIVE])
+            return cols
+
+        def spread(cols, name, tag):
+            bank = ps.tile([P, PASS], F32, name=name + "_bank", tag=tag)
+            for c in range(CHUNKS):
+                nc.tensor.transpose(bank[:, c * P : (c + 1) * P], cols[:, c : c + 1].to_broadcast([P, P]), ident[:])
+            return bank
+
+        pos_slots = [gather_row(pos_pool, h, "pos") for h in range(SLOT_PASSES)]
+        vs_slots = [gather_row(vs_pool, h, "vs") for h in range(SLOT_PASSES)]
+        pos_cols = [to_columns(pos_slots[h], f"pos{h}", f"score1{h}") for h in range(SLOT_PASSES)]
+        place_banks = [spread(pos_cols[h], f"pos{h}", f"place{h}") for h in range(SLOT_PASSES)]
 
         def turn(src, bank):
             words = src.bitcast(F32)
             for u in range(2):
-                nc.tensor.transpose(bank[:, u, :], words[:, u * P : (u + 1) * P], ident[:])
+                nc.tensor.transpose(bank[:, u, :], words[:, u::2], ident[:])
 
-        def lay(bank, dst):
-            nc.scalar.copy(dst.bitcast(F32).rearrange("p (g c u) -> p g c u", g=bank.shape[1], u=2), bank.rearrange("p g u c -> p g c u"))
+        def lay(bank, dst, move):
+            move(dst.bitcast(F32).rearrange("p (c u) -> p c u", u=2), bank.rearrange("p u c -> p c u"))
 
         def quantise(src, name, codes):
             columns = src.shape[1] // 4
@@ -131,17 +146,15 @@ def tile_attend_soft_draft_cap_topkq256n1024t2048_kernel(tc, q_words, q_scales, 
             nc.vector.quantize_mx(out=codes[:].bitcast(FP8X4), scales=scales[:], in_=src)
             return codes, scales
 
-
         e_all = {}
-        place_banks = []
-        for h in range(SLOT_PASSES):
-            for j in range(ROW_TILES):
-                score = ps.tile([P, PASS], F32, name=f"score{j}{h}", tag=f"bank{j}{h}")
+        for j in range(ROW_TILES):
+            for h in range(SLOT_PASSES):
+                score = ps.tile([P, PASS], F32, name=f"score{j}{h}", tag=f"score{j}{h}")
                 for o in range(D_PASSES):
                     nc.tensor.matmul_mx(
                         out=score[:],
                         lhsT=q_code[:, o, j * P : (j + 1) * P].bitcast(FP8X4),
-                        lhsT_scale=q_scale[:, o, j * P : (j + 1) * P],
+                        lhsT_scale=q_scale[:, o * NQ + j * P : o * NQ + (j + 1) * P],
                         rhs=k_code[h][:, o, :].bitcast(FP4X4),
                         rhs_scale=k_scale[:, o * N + h * PASS : o * N + (h + 1) * PASS],
                         start=(o == 0),
@@ -151,96 +164,77 @@ def tile_attend_soft_draft_cap_topkq256n1024t2048_kernel(tc, q_words, q_scales, 
                 nc.scalar.activation(capped[:], score[:], ACT.Tanh, scale=1.0 / CAP)
                 e_all[j, h] = sb.tile([P, PASS], F32, name=f"e{j}{h}")
                 nc.scalar.activation(e_all[j, h][:], capped[:], ACT.Exp, scale=CAP)
-            place_bank = ps.tile([P, P, 4], F32, name=f"place_bank{h}", tag=f"bank{1 - h}{h}")
-            for c in range(4):
-                nc.tensor.transpose(place_bank[:, :, c], pos_cols[h][:, c : c + 1].to_broadcast([P, P]), ident[:])
-            place_banks.append(place_bank)
 
-        v_slot_tags = ["v_slots0", "capped11"]
+        vs_turned = ps.tile([P, P + 2 * (N // P - 1)], F32, name="vs_turned", tag="score00")
+        for c in reversed(range(N // P)):
+            nc.tensor.transpose(vs_turned[:, 2 * c : 2 * c + P], vs_slots[c // CHUNKS][:, c % CHUNKS * P : (c % CHUNKS + 1) * P], ident[:])
+
         v_turned = sb.tile([P, N], BF16, name="v_turned", align_bytes=64)
-        v_bank = ps.tile([P, SLOT_PASSES, 2, DV], F32, name="v_bank", tag="bank11")
-        for g in range(SLOT_PASSES):
-            v_slots = sb.tile([P, PASS], BF16, name=f"v_slots{g}", tag=v_slot_tags[g], align_bytes=64)
-            entries = offsets[:, g * PASS // LIST_ROWS : (g + 1) * PASS // LIST_ROWS]
-            nc.scalar.activation(dealt(v_slots[:]), v_bf[:].indirect(entries), ACT.Copy)
-            turn(v_slots[:], v_bank[:, g])
-        lay(v_bank[:], v_turned[:])
+
+        def values(g, slots_tag, bank_tag):
+            v_slots = sb.tile([P, PASS], BF16, name=f"v_slots{g}", tag=slots_tag, align_bytes=64)
+            nc.scalar.activation(v_slots[:], v_pool[:].indirect(entries(g)), ACT.Copy)
+            v_bank = ps.tile([P, 2, DV], F32, name=f"v_bank{g}", tag=bank_tag)
+            turn(v_slots[:], v_bank[:])
+            lay(v_bank[:], v_turned[:, g * PASS : (g + 1) * PASS], nc.scalar.copy)
 
         e_sum = sb.tile([P, SLOT_PASSES, ROW_TILES], F32, name="e_sum")
         stats = sb.tile([P, 2 * ROW_TILES], F32, name="stats")
         inv_stats = sb.tile([P, 2 * ROW_TILES], F32, name="inv_stats")
         inv_top = inv_stats[:, :ROW_TILES]
-        masked, lifted, top, scaled, w_turned = {}, {}, {}, {}, {}
+        masked, lifted, top, w_turned = {}, {}, {}, {}
 
         def mask(j, h):
-            tag = "capped10" if (j, h) == (0, 0) else f"masked{j}{h}"
-            masked[j, h] = sb.tile([P, PASS], F32, name=f"masked{j}{h}", tag=tag, align_bytes=64)
+            masked[j, h] = sb.tile([P, PASS], F32, name=f"masked{j}{h}", tag=f"masked{j}{h}", align_bytes=64)
             nc.vector.scalar_tensor_tensor(
-                masked[j, h][:], place_banks[h][:].rearrange("p k c -> p (k c)"), q_place[:, j : j + 1], e_all[j, h][:], ALU.is_le, ALU.mult, accum_out=e_sum[:, h, j : j + 1]
+                masked[j, h][:], place_banks[h][:], q_place[:, j : j + 1], e_all[j, h][:], ALU.is_le, ALU.mult, accum_out=e_sum[:, h, j : j + 1]
             )
 
         def lift(j, h):
             lifted[j, h] = sb.tile([P, PASS], F32, name=f"lifted{j}{h}", tag=f"lifted{j}{h}", align_bytes=64)
             top[j, h] = stats[:, j : j + 1] if h else sb.tile([P, 1], F32, name=f"top{j}")[:]
-            nc.vector.tensor_scalar(
-                dealt(lifted[j, h][:]),
-                masked[j, h][:].rearrange("p (gb u i) -> p gb u i", u=2, i=16),
-                floor[:],
-                top[j, h - 1] if h else None,
-                ALU.max,
-                ALU.max,
-                accum_out=top[j, h],
-            )
+            nc.vector.tensor_scalar(lifted[j, h][:], masked[j, h][:], floor[:], top[j, h - 1] if h else None, ALU.max, ALU.max, accum_out=top[j, h])
 
         def invert(cols):
             nc.vector.reciprocal(inv_stats[:, cols], stats[:, cols])
 
-        def halves(ap):
-            return ap.rearrange("p (u x) -> p u x", u=2)
+        w_tags = {(0, 0): "score00", (0, 1): "score01", (1, 0): "score10", (1, 1): "place0"}
 
-        def token_scales(g):
-            return vs_slots[:].rearrange("p (u g x) -> p u g x", u=2, g=SLOT_PASSES)[:, :, g, :]
-
-        def scale(j, g):
-            scaled[j, g] = sb.tile([P, PASS], F32, name=f"scaled{j}{g}", tag=f"scaled{j}{g}", align_bytes=64)
-            nc.gpsimd.tensor_tensor(halves(scaled[j, g][:]), halves(lifted[j, g][:]), token_scales(g), ALU.mult)
-
-        def weigh(j, g, pieces):
+        def weigh(j, g, move):
             w = sb.tile([P, PASS], BF16, name=f"w{j}{g}", align_bytes=64)
-            if (j, g) in scaled:
-                nc.scalar.activation(w[:], scaled[j, g][:], ACT.Copy, scale=inv_top[:, j : j + 1])
-            for us in pieces:
-                nc.vector.scalar_tensor_tensor(halves(w[:])[:, us, :], halves(lifted[j, g][:])[:, us, :], inv_top[:, j : j + 1], token_scales(g)[:, us, :], ALU.mult, ALU.mult)
-            w_bank = ps.tile([P, 1, 2, P], F32, name=f"w_bank{j}{g}", tag=f"w_bank{2 * j + g}")
+            nc.vector.scalar_tensor_tensor(w[:], lifted[j, g][:], inv_top[:, j : j + 1], scale_banks[g][:], ALU.mult, ALU.mult)
+            w_bank = ps.tile([P, 2, P], F32, name=f"w_bank{j}{g}", tag=w_tags[j, g])
             w_turned[j, g] = sb.tile([P, PASS], BF16, name=f"w_turned{j}{g}", align_bytes=64)
-            turn(w[:], w_bank[:, 0])
-            lay(w_bank[:], w_turned[j, g][:])
+            turn(w[:], w_bank[:])
+            lay(w_bank[:], w_turned[j, g][:], move)
 
-        whole = [slice(0, 2)]
         mask(0, 0)
-        mask(1, 0)
         lift(0, 0)
-        scale(0, 0)
         mask(0, 1)
-        lift(1, 0)
-        scale(1, 0)
+        mask(1, 0)
         lift(0, 1)
-        mask(1, 1)
+        vs_cols = sb.tile([P, N // P], F32, name="vs_cols", tag="masked00", align_bytes=64)
+        nc.vector.tensor_copy(vs_cols[:], vs_turned[:, LIVE::2])
+        scale_banks = [spread(vs_cols[:, h * CHUNKS : (h + 1) * CHUNKS], f"vs{h}", f"scale{h}") for h in range(SLOT_PASSES)]
+        lift(1, 0)
         invert(slice(0, 1))
-        nc.vector.scalar_tensor_tensor(stats[:, ROW_TILES:], e_sum[:, 0, :], floor_sum[:], e_sum[:, 1, :], ALU.add, ALU.add)
+        mask(1, 1)
+        values(0, "capped11", "score11")
+        weigh(0, 0, nc.scalar.copy)
+        values(1, "masked10", "score00")
         lift(1, 1)
-        weigh(0, 0, [])
-        weigh(0, 1, whole)
+        nc.vector.scalar_tensor_tensor(stats[:, ROW_TILES:], e_sum[:, 0, :], floor_sum[:], e_sum[:, 1, :], ALU.add, ALU.add)
+        weigh(0, 1, nc.scalar.copy)
         invert(slice(1, 2 * ROW_TILES))
-        weigh(1, 0, [])
-        weigh(1, 1, [slice(0, 1), slice(1, 2)])
+        weigh(1, 0, nc.scalar.copy)
+        weigh(1, 1, nc.vector.tensor_copy)
 
         inv_row_sum = sb.tile([P, ROW_TILES], F32, name="inv_row_sum")
         nc.gpsimd.tensor_tensor(inv_row_sum[:], inv_stats[:, ROW_TILES:], stats[:, :ROW_TILES], ALU.mult)
 
         v_code, v_scale = quantise(v_turned[:], "v", sb.tile([P, N // 4], U32, name="v_code", tag="lifted11", align_bytes=64))
         store_queues = [nc.sync, nc.scalar]
-        acc_tags = ["bank00", "bank10"]
+        acc_tags = ["place1", "score01"]
         for j in range(ROW_TILES):
             acc = ps.tile([P, DV], F32, name=f"acc{j}", tag=acc_tags[j])
             for g in range(SLOT_PASSES):

@@ -36,37 +36,43 @@ def tile_attend_soft_draft_cap_topkq256n1024t2048_kernel(tc, q_words, q_scales, 
         sb = ctx.enter_context(tc.tile_pool(name="sb", bufs=1))
         ps = ctx.enter_context(tc.psum_pool(name="ps", bufs=1))
 
+        q_scale = sb.tile([P, D_PASSES * NQ], U8, name="q_scale", align_bytes=64)
+        nc.gpsimd.memset(q_scale[:].bitcast(I32), 0)
+
+        def load_query_scales(queue, quad):
+            queue.dma_start(
+                q_scale[QUAD * quad : QUAD * quad + 4, :].rearrange("p (o q) -> p o q", o=D_PASSES).bitcast(I32),
+                q_scales[0, :, 4 * quad : 4 * quad + 4, :].rearrange("o f q -> f o q").bitcast(I32),
+            )
+
         offsets = sb.tile([P, N // LIST_ROWS], U16, name="offsets")
         nc.sync.dma_start(offsets[:], offs)
-        ks_pool = sb.tile([P, T], U8, name="ks_pool", tag="after_scale_gather", align_bytes=64)
+        ks_pool = sb.tile([P, T], U8, name="ks_pool", align_bytes=64)
         nc.sync.dma_start(ks_pool[P - QUAD :, :].bitcast(I32), k_scales.rearrange("o f t -> f o t").bitcast(I32))
         pos_pool = sb.tile([P, T], F32, name="pos_pool")
         nc.sync.dma_start(pos_pool[LIVE:, :], pos[0:1, :])
         vs_pool = sb.tile([P, T], F32, name="vs_pool")
         nc.sync.dma_start(vs_pool[LIVE:, :], vs[0:1, :])
+        load_query_scales(nc.sync, 0)
+        load_query_scales(nc.sync, 1)
         kw_pool = sb.tile([P, T], I32, name="kw_pool", align_bytes=64)
         nc.sync.dma_start(kw_pool[:], k_words[0].rearrange("p t b -> p (t b)").bitcast(I32))
-        q_place = sb.tile([P, ROW_TILES], F32, name="q_place")
-        with nc.allow_non_contiguous_dma(reason="one place for each query row"):
-            nc.sync.dma_start(q_place[:], qpos[0].rearrange("(j p) o -> p (j o)", p=P))
+        q_code = sb.tile([P, D_PASSES, NQ], I32, name="q_code", align_bytes=64)
+        nc.sync.dma_start(q_code[:], q_words[0].rearrange("o p q r -> p o (q r)").bitcast(I32))
+        load_query_scales(nc.sync, 2)
+        load_query_scales(nc.sync, 3)
 
         def zero_words(words):
             last = words.shape[1] - 1
             nc.vector.memset(words[:, :last], 0)
             nc.vector.memset(words[:, last:], 0)
 
-        q_scale = sb.tile([P, D_PASSES * NQ], U8, name="q_scale", align_bytes=64)
-        zero_words(q_scale[:].bitcast(I32))
-        log_floor = sb.tile([P, 1], F32, name="log_floor", tag="after_floor", align_bytes=64)
+        log_floor = sb.tile([P, 1], F32, name="log_floor")
         nc.vector.memset(log_floor[:], LOG_FLOOR)
         zero_words(ks_pool[: P - QUAD, :].bitcast(I32))
-        k_scale = sb.tile([P, D_PASSES * N], U8, name="k_scale", align_bytes=64)
-        zero_words(k_scale[:].bitcast(I32))
-        for quad in range(P // QUAD):
-            nc.sync.dma_start(
-                q_scale[QUAD * quad : QUAD * quad + 4, :].rearrange("p (o q) -> p o q", o=D_PASSES).bitcast(I32),
-                q_scales[0, :, 4 * quad : 4 * quad + 4, :].rearrange("o f q -> f o q").bitcast(I32),
-            )
+        k_scale = [sb.tile([P, D_PASSES * PASS], U8, name=f"k_scale{h}", align_bytes=64) for h in range(SLOT_PASSES)]
+        for h in range(SLOT_PASSES):
+            zero_words(k_scale[h][:].bitcast(I32))
         ident = sb.tile([P, P], F32, name="ident")
         make_identity(nc, ident[:])
         nc.gpsimd.memset(pos_pool[:LIVE, :], 0.0)
@@ -74,22 +80,24 @@ def tile_attend_soft_draft_cap_topkq256n1024t2048_kernel(tc, q_words, q_scales, 
 
         floor = sb.tile([P, 1], F32, name="floor")
         nc.scalar.activation(floor[:], log_floor[:], ACT.Exp)
-        q_code = sb.tile([P, D_PASSES, NQ], I32, name="q_code", tag="after_floor", align_bytes=64)
-        nc.sync.dma_start(q_code[:], q_words[0].rearrange("o p q r -> p o (q r)").bitcast(I32))
         floor_sum = sb.tile([P, 1], F32, name="floor_sum")
         nc.scalar.activation(floor_sum[:], floor[:], ACT.Copy, scale=float(N))
 
         def entries(h):
             return offsets[:, h * PASS // LIST_ROWS : (h + 1) * PASS // LIST_ROWS]
 
-        ks_slots = sb.tile([P, N], U8, name="ks_slots", tag="after_scale_moves", align_bytes=64)
-        nc.vector.tensor_copy(ks_slots[:], ks_pool[:].indirect(offsets[:]))
-        for quad in range(P // QUAD):
-            nc.sync.dma_start(
-                k_scale[QUAD * quad : QUAD * quad + 4, :].bitcast(I32),
-                ks_slots[P - QUAD + 8 * quad : P - QUAD + 8 * quad + 8, :].bitcast(I32),
-            )
-        v_pool = sb.tile([P, T], F32, name="v_pool", tag="after_scale_gather", align_bytes=64)
+        for h in range(SLOT_PASSES):
+            ks_slots = sb.tile([P, PASS], U8, name=f"ks_slots{h}", tag=f"after_scale_moves{h}", align_bytes=64)
+            nc.vector.tensor_copy(ks_slots[:], ks_pool[:].indirect(entries(h)))
+            for quad in range(P // QUAD):
+                nc.sync.dma_start(
+                    k_scale[h][QUAD * quad : QUAD * quad + 4, :].bitcast(I32),
+                    ks_slots[P - QUAD + 8 * quad : P - QUAD + 8 * quad + 8, :].bitcast(I32),
+                )
+        q_place = sb.tile([P, ROW_TILES], F32, name="q_place", tag="after_scale_moves0", align_bytes=64)
+        with nc.allow_non_contiguous_dma(reason="one place for each query row"):
+            nc.sync.dma_start(q_place[:], qpos[0].rearrange("(j p) o -> p (j o)", p=P))
+        v_pool = sb.tile([P, T], F32, name="v_pool", tag="after_scale_moves1", align_bytes=64)
         nc.sync.dma_start(v_pool[:], vT)
 
         k_code = []
@@ -128,9 +136,10 @@ def tile_attend_soft_draft_cap_topkq256n1024t2048_kernel(tc, q_words, q_scales, 
             return bank
 
         pos_slots = [gather_row(pos_pool, h, "pos") for h in range(SLOT_PASSES)]
-        vs_slots = [gather_row(vs_pool, h, "vs") for h in range(SLOT_PASSES)]
-        pos_cols = [to_columns(pos_slots[h], f"pos{h}", f"score1{h}") for h in range(SLOT_PASSES)]
-        place_banks = [spread(pos_cols[h], f"pos{h}", f"place{h}") for h in range(SLOT_PASSES)]
+        vs_slots = [gather_row(vs_pool, 0, "vs"), sb.tile([P, PASS], F32, name="vs_slots1", tag="kw_slots1", align_bytes=64)]
+        nc.vector.tensor_copy(vs_slots[1][:], vs_pool[:].indirect(entries(1)))
+        pos_cols = [to_columns(pos_slots[h], f"pos{h}", f"score{h}1") for h in range(SLOT_PASSES)]
+        place_banks = [spread(pos_cols[0], "pos0", "place0")]
 
         def turn(src, bank):
             words = src.bitcast(F32)
@@ -147,8 +156,8 @@ def tile_attend_soft_draft_cap_topkq256n1024t2048_kernel(tc, q_words, q_scales, 
             return codes, scales
 
         e_all = {}
-        for j in range(ROW_TILES):
-            for h in range(SLOT_PASSES):
+        for h in range(SLOT_PASSES):
+            for j in range(ROW_TILES):
                 score = ps.tile([P, PASS], F32, name=f"score{j}{h}", tag=f"score{j}{h}")
                 for o in range(D_PASSES):
                     nc.tensor.matmul_mx(
@@ -156,16 +165,20 @@ def tile_attend_soft_draft_cap_topkq256n1024t2048_kernel(tc, q_words, q_scales, 
                         lhsT=q_code[:, o, j * P : (j + 1) * P].bitcast(FP8X4),
                         lhsT_scale=q_scale[:, o * NQ + j * P : o * NQ + (j + 1) * P],
                         rhs=k_code[h][:, o, :].bitcast(FP4X4),
-                        rhs_scale=k_scale[:, o * N + h * PASS : o * N + (h + 1) * PASS],
+                        rhs_scale=k_scale[h][:, o * PASS : (o + 1) * PASS],
                         start=(o == 0),
                         stop=(o == D_PASSES - 1),
                     )
                 capped = sb.tile([P, PASS], F32, name=f"capped{j}{h}", tag=f"capped{j}{h}", align_bytes=64)
-                nc.scalar.activation(capped[:], score[:], ACT.Tanh, scale=1.0 / CAP)
                 e_all[j, h] = sb.tile([P, PASS], F32, name=f"e{j}{h}")
-                nc.scalar.activation(e_all[j, h][:], capped[:], ACT.Exp, scale=CAP)
+                pieces = [slice(0, PASS // 2), slice(PASS // 2, PASS)] if (j, h) == (0, 0) else [slice(0, PASS)]
+                for cols in pieces:
+                    nc.scalar.activation(capped[:, cols], score[:, cols], ACT.Tanh, scale=1.0 / CAP)
+                for cols in pieces:
+                    nc.scalar.activation(e_all[j, h][:, cols], capped[:, cols], ACT.Exp, scale=CAP)
 
-        vs_turned = ps.tile([P, P + 2 * (N // P - 1)], F32, name="vs_turned", tag="score00")
+        place_banks.append(spread(pos_cols[1], "pos1", "score00"))
+        vs_turned = ps.tile([P, P + 2 * (N // P - 1)], F32, name="vs_turned", tag="score10")
         for c in reversed(range(N // P)):
             nc.tensor.transpose(vs_turned[:, 2 * c : 2 * c + P], vs_slots[c // CHUNKS][:, c % CHUNKS * P : (c % CHUNKS + 1) * P], ident[:])
 
@@ -179,8 +192,8 @@ def tile_attend_soft_draft_cap_topkq256n1024t2048_kernel(tc, q_words, q_scales, 
             lay(v_bank[:], v_turned[:, g * PASS : (g + 1) * PASS], nc.scalar.copy)
 
         e_sum = sb.tile([P, SLOT_PASSES, ROW_TILES], F32, name="e_sum")
-        stats = sb.tile([P, 2 * ROW_TILES], F32, name="stats")
-        inv_stats = sb.tile([P, 2 * ROW_TILES], F32, name="inv_stats")
+        stats = sb.tile([P, ROW_TILES], F32, name="stats")
+        inv_stats = sb.tile([P, ROW_TILES], F32, name="inv_stats")
         inv_top = inv_stats[:, :ROW_TILES]
         masked, lifted, top, w_turned = {}, {}, {}, {}
 
@@ -198,7 +211,7 @@ def tile_attend_soft_draft_cap_topkq256n1024t2048_kernel(tc, q_words, q_scales, 
         def invert(cols):
             nc.vector.reciprocal(inv_stats[:, cols], stats[:, cols])
 
-        w_tags = {(0, 0): "score00", (0, 1): "score01", (1, 0): "score10", (1, 1): "place0"}
+        w_tags = {(0, 0): "score10", (0, 1): "score01", (1, 0): "spare", (1, 1): "score11"}
 
         def weigh(j, g, move):
             w = sb.tile([P, PASS], BF16, name=f"w{j}{g}", align_bytes=64)
@@ -210,31 +223,36 @@ def tile_attend_soft_draft_cap_topkq256n1024t2048_kernel(tc, q_words, q_scales, 
 
         mask(0, 0)
         lift(0, 0)
-        mask(0, 1)
         mask(1, 0)
-        lift(0, 1)
+        mask(0, 1)
+        lift(1, 0)
         vs_cols = sb.tile([P, N // P], F32, name="vs_cols", tag="masked00", align_bytes=64)
         nc.vector.tensor_copy(vs_cols[:], vs_turned[:, LIVE::2])
         scale_banks = [spread(vs_cols[:, h * CHUNKS : (h + 1) * CHUNKS], f"vs{h}", f"scale{h}") for h in range(SLOT_PASSES)]
-        lift(1, 0)
-        invert(slice(0, 1))
+        lift(0, 1)
         mask(1, 1)
+        invert(slice(0, 1))
         values(0, "capped11", "score11")
-        weigh(0, 0, nc.scalar.copy)
-        values(1, "masked10", "score00")
         lift(1, 1)
-        nc.vector.scalar_tensor_tensor(stats[:, ROW_TILES:], e_sum[:, 0, :], floor_sum[:], e_sum[:, 1, :], ALU.add, ALU.add)
+        weigh(0, 0, nc.scalar.copy)
+        values(1, "masked01", "place0")
         weigh(0, 1, nc.scalar.copy)
-        invert(slice(1, 2 * ROW_TILES))
+        invert(slice(1, 2))
         weigh(1, 0, nc.scalar.copy)
-        weigh(1, 1, nc.vector.tensor_copy)
+        weigh(1, 1, nc.scalar.copy)
 
+        half_sum = sb.tile([P, ROW_TILES], F32, name="half_sum")
+        nc.gpsimd.tensor_scalar(half_sum[:], e_sum[:, 0, :], floor_sum[:], 1.0, ALU.add, ALU.mult)
+        row_sum = sb.tile([P, ROW_TILES], F32, name="row_sum")
+        nc.gpsimd.tensor_tensor(row_sum[:], half_sum[:], e_sum[:, 1, :], ALU.add)
+        inv_sum = sb.tile([P, ROW_TILES], F32, name="inv_sum", tag="lifted10", align_bytes=64)
+        nc.vector.reciprocal(inv_sum[:], row_sum[:])
         inv_row_sum = sb.tile([P, ROW_TILES], F32, name="inv_row_sum")
-        nc.gpsimd.tensor_tensor(inv_row_sum[:], inv_stats[:, ROW_TILES:], stats[:, :ROW_TILES], ALU.mult)
+        nc.gpsimd.tensor_tensor(inv_row_sum[:], inv_sum[:], stats[:], ALU.mult)
 
         v_code, v_scale = quantise(v_turned[:], "v", sb.tile([P, N // 4], U32, name="v_code", tag="lifted11", align_bytes=64))
         store_queues = [nc.sync, nc.scalar]
-        acc_tags = ["place1", "score01"]
+        acc_tags = ["score00", "score01"]
         for j in range(ROW_TILES):
             acc = ps.tile([P, DV], F32, name=f"acc{j}", tag=acc_tags[j])
             for g in range(SLOT_PASSES):

@@ -132,7 +132,7 @@ def tile_attend_soft_draft_cap_topkq256n1024t2048_kernel(tc, q_words, q_scales, 
         def spread(cols, name, tag):
             bank = ps.tile([P, PASS], F32, name=name + "_bank", tag=tag)
             for c in range(CHUNKS):
-                nc.tensor.transpose(bank[:, c * P : (c + 1) * P], cols[:, c : c + 1].to_broadcast([P, P]), ident[:])
+                nc.tensor.transpose(bank[:].rearrange("p (u c k e) -> p c k u e", u=2, c=CHUNKS, e=2)[:, c], cols[:, c : c + 1].to_broadcast([P, P]), ident[:])
             return bank
 
         pos_slots = [gather_row(pos_pool, h, "pos") for h in range(SLOT_PASSES)]
@@ -141,10 +141,8 @@ def tile_attend_soft_draft_cap_topkq256n1024t2048_kernel(tc, q_words, q_scales, 
         pos_cols = [to_columns(pos_slots[h], f"pos{h}", f"score{h}1") for h in range(SLOT_PASSES)]
         place_banks = [spread(pos_cols[0], "pos0", "place0")]
 
-        def turn(src, bank):
-            words = src.bitcast(F32)
-            for u in range(2):
-                nc.tensor.transpose(bank[:, u, :], words[:, u::2], ident[:])
+        def dealt(tile, cols):
+            return tile[:].rearrange("p (u x) -> p u x", u=2)[:, :, cols.start // 2 : cols.stop // 2]
 
         def lay(bank, dst, move):
             move(dst.bitcast(F32).rearrange("p (c u) -> p c u", u=2), bank.rearrange("p u c -> p c u"))
@@ -155,30 +153,40 @@ def tile_attend_soft_draft_cap_topkq256n1024t2048_kernel(tc, q_words, q_scales, 
             nc.vector.quantize_mx(out=codes[:].bitcast(FP8X4), scales=scales[:], in_=src)
             return codes, scales
 
+        def scores(j, h, cols, tag):
+            score = ps.tile([P, cols.stop - cols.start], F32, name=f"score{j}{h}_{cols.start}", tag=tag)
+            for o in range(D_PASSES):
+                nc.tensor.matmul_mx(
+                    out=score[:],
+                    lhsT=q_code[:, o, j * P : (j + 1) * P].bitcast(FP8X4),
+                    lhsT_scale=q_scale[:, o * NQ + j * P : o * NQ + (j + 1) * P],
+                    rhs=k_code[h][:, o, cols].bitcast(FP4X4),
+                    rhs_scale=k_scale[h][:, o * PASS + cols.start : o * PASS + cols.stop],
+                    start=(o == 0),
+                    stop=(o == D_PASSES - 1),
+                )
+            return score
+
         e_all = {}
         for h in range(SLOT_PASSES):
             for j in range(ROW_TILES):
-                score = ps.tile([P, PASS], F32, name=f"score{j}{h}", tag=f"score{j}{h}")
-                for o in range(D_PASSES):
-                    nc.tensor.matmul_mx(
-                        out=score[:],
-                        lhsT=q_code[:, o, j * P : (j + 1) * P].bitcast(FP8X4),
-                        lhsT_scale=q_scale[:, o * NQ + j * P : o * NQ + (j + 1) * P],
-                        rhs=k_code[h][:, o, :].bitcast(FP4X4),
-                        rhs_scale=k_scale[h][:, o * PASS : (o + 1) * PASS],
-                        start=(o == 0),
-                        stop=(o == D_PASSES - 1),
-                    )
-                capped = sb.tile([P, PASS], F32, name=f"capped{j}{h}", tag=f"capped{j}{h}", align_bytes=64)
+                pieces = [(slice(0, PASS), f"score{j}{h}")]
+                if (j, h) == (0, 0):
+                    pieces = [(slice(0, PASS // 2), "spare"), (slice(PASS // 2, PASS), "score00")]
+                capped = sb.tile([P, PASS], F32, name=f"capped{j}{h}", tag="capped10" if (j, h) == (0, 1) else f"capped{j}{h}", align_bytes=64)
                 e_all[j, h] = sb.tile([P, PASS], F32, name=f"e{j}{h}")
-                pieces = [slice(0, PASS // 2), slice(PASS // 2, PASS)] if (j, h) == (0, 0) else [slice(0, PASS)]
-                for cols in pieces:
-                    nc.scalar.activation(capped[:, cols], score[:, cols], ACT.Tanh, scale=1.0 / CAP)
-                for cols in pieces:
-                    nc.scalar.activation(e_all[j, h][:, cols], capped[:, cols], ACT.Exp, scale=CAP)
+                for cols, tag in pieces:
+                    nc.scalar.activation(
+                        dealt(capped, cols).rearrange("p u (k e) -> p u k e", e=2),
+                        scores(j, h, cols, tag)[:].rearrange("p (k u e) -> p u k e", u=2, e=2),
+                        ACT.Tanh,
+                        scale=1.0 / CAP,
+                    )
+                for cols, tag in pieces:
+                    nc.scalar.activation(dealt(e_all[j, h], cols), dealt(capped, cols), ACT.Exp, scale=CAP)
 
         place_banks.append(spread(pos_cols[1], "pos1", "score00"))
-        vs_turned = ps.tile([P, P + 2 * (N // P - 1)], F32, name="vs_turned", tag="score10")
+        vs_turned = ps.tile([P, P + 2 * (N // P - 1)], F32, name="vs_turned", tag="score01")
         for c in reversed(range(N // P)):
             nc.tensor.transpose(vs_turned[:, 2 * c : 2 * c + P], vs_slots[c // CHUNKS][:, c % CHUNKS * P : (c % CHUNKS + 1) * P], ident[:])
 
@@ -188,7 +196,8 @@ def tile_attend_soft_draft_cap_topkq256n1024t2048_kernel(tc, q_words, q_scales, 
             v_slots = sb.tile([P, PASS], BF16, name=f"v_slots{g}", tag=slots_tag, align_bytes=64)
             nc.scalar.activation(v_slots[:], v_pool[:].indirect(entries(g)), ACT.Copy)
             v_bank = ps.tile([P, 2, DV], F32, name=f"v_bank{g}", tag=bank_tag)
-            turn(v_slots[:], v_bank[:])
+            for u in range(2):
+                nc.tensor.transpose(v_bank[:, u, :], v_slots[:].bitcast(F32)[:, u::2], ident[:])
             lay(v_bank[:], v_turned[:, g * PASS : (g + 1) * PASS], nc.scalar.copy)
 
         e_sum = sb.tile([P, SLOT_PASSES, ROW_TILES], F32, name="e_sum")
@@ -211,16 +220,20 @@ def tile_attend_soft_draft_cap_topkq256n1024t2048_kernel(tc, q_words, q_scales, 
         def invert(cols):
             nc.vector.reciprocal(inv_stats[:, cols], stats[:, cols])
 
-        w_tags = {(0, 0): "score10", (0, 1): "score01", (1, 0): "spare", (1, 1): "score11"}
+        w_tags = {(0, 0): "score01", (0, 1): "score10", (1, 0): "spare", (1, 1): "score11"}
 
-        def weigh(j, g, move):
+        def weigh(j, g, pieces):
             w = sb.tile([P, PASS], BF16, name=f"w{j}{g}", align_bytes=64)
-            nc.vector.scalar_tensor_tensor(w[:], lifted[j, g][:], inv_top[:, j : j + 1], scale_banks[g][:], ALU.mult, ALU.mult)
+            for cols in pieces:
+                nc.vector.scalar_tensor_tensor(w[:, cols], lifted[j, g][:, cols], inv_top[:, j : j + 1], scale_banks[g][:, cols], ALU.mult, ALU.mult)
             w_bank = ps.tile([P, 2, P], F32, name=f"w_bank{j}{g}", tag=w_tags[j, g])
             w_turned[j, g] = sb.tile([P, PASS], BF16, name=f"w_turned{j}{g}", align_bytes=64)
-            turn(w[:], w_bank[:])
-            lay(w_bank[:], w_turned[j, g][:], move)
+            for u in range(2):
+                nc.tensor.transpose(w_bank[:, u, :], w[:].bitcast(F32)[:, u * P : (u + 1) * P], ident[:])
+            lay(w_bank[:], w_turned[j, g][:], nc.scalar.copy)
 
+        whole = [slice(0, PASS)]
+        halves = [slice(0, PASS // 2), slice(PASS // 2, PASS)]
         mask(0, 0)
         lift(0, 0)
         mask(1, 0)
@@ -234,25 +247,25 @@ def tile_attend_soft_draft_cap_topkq256n1024t2048_kernel(tc, q_words, q_scales, 
         invert(slice(0, 1))
         values(0, "capped11", "score11")
         lift(1, 1)
-        weigh(0, 0, nc.scalar.copy)
+        weigh(0, 0, whole)
         values(1, "masked01", "place0")
-        weigh(0, 1, nc.scalar.copy)
+        weigh(0, 1, whole)
         invert(slice(1, 2))
-        weigh(1, 0, nc.scalar.copy)
-        weigh(1, 1, nc.scalar.copy)
+        weigh(1, 0, whole)
+        weigh(1, 1, halves)
 
         half_sum = sb.tile([P, ROW_TILES], F32, name="half_sum")
         nc.gpsimd.tensor_scalar(half_sum[:], e_sum[:, 0, :], floor_sum[:], 1.0, ALU.add, ALU.mult)
         row_sum = sb.tile([P, ROW_TILES], F32, name="row_sum")
         nc.gpsimd.tensor_tensor(row_sum[:], half_sum[:], e_sum[:, 1, :], ALU.add)
-        inv_sum = sb.tile([P, ROW_TILES], F32, name="inv_sum", tag="lifted10", align_bytes=64)
+        inv_sum = sb.tile([P, ROW_TILES], F32, name="inv_sum")
         nc.vector.reciprocal(inv_sum[:], row_sum[:])
         inv_row_sum = sb.tile([P, ROW_TILES], F32, name="inv_row_sum")
         nc.gpsimd.tensor_tensor(inv_row_sum[:], inv_sum[:], stats[:], ALU.mult)
 
         v_code, v_scale = quantise(v_turned[:], "v", sb.tile([P, N // 4], U32, name="v_code", tag="lifted11", align_bytes=64))
         store_queues = [nc.sync, nc.scalar]
-        acc_tags = ["score00", "score01"]
+        acc_tags = ["score00", "score10"]
         for j in range(ROW_TILES):
             acc = ps.tile([P, DV], F32, name=f"acc{j}", tag=acc_tags[j])
             for g in range(SLOT_PASSES):

@@ -28,6 +28,7 @@ SLOT_PASSES = N // PASS
 ROW_TILES = NQ // P
 CHUNKS = PASS // P
 LIVE = P - 1
+VS_SPLIT = 768
 
 
 def tile_attend_soft_draft_cap_topkq256n1024t2048_kernel(tc, q_words, q_scales, k_words, k_scales, vT, vs, pos, qpos, offs, out):
@@ -121,12 +122,12 @@ def tile_attend_soft_draft_cap_topkq256n1024t2048_kernel(tc, q_words, q_scales, 
             nc.scalar.activation(slots[:], pool[:].indirect(entries(h)), ACT.Copy)
             return slots
 
-        def to_columns(slots, name, tag):
+        def to_columns(slots, name, tag, move):
             bank = ps.tile([P, CHUNKS, P], F32, name=name + "_turned", tag=tag)
             for c in range(CHUNKS):
                 nc.tensor.transpose(bank[:, c, :], slots[:, c * P : (c + 1) * P], ident[:])
             cols = sb.tile([P, CHUNKS], F32, name=name + "_cols")
-            nc.scalar.copy(cols[:], bank[:, :, LIVE])
+            move(cols[:], bank[:, :, LIVE])
             return cols
 
         def spread(cols, name, tag):
@@ -136,9 +137,12 @@ def tile_attend_soft_draft_cap_topkq256n1024t2048_kernel(tc, q_words, q_scales, 
             return bank
 
         pos_slots = [gather_row(pos_pool, h, "pos") for h in range(SLOT_PASSES)]
-        vs_slots = [gather_row(vs_pool, 0, "vs"), sb.tile([P, PASS], F32, name="vs_slots1", tag="kw_slots1", align_bytes=64)]
-        nc.vector.tensor_copy(vs_slots[1][:], vs_pool[:].indirect(entries(1)))
-        pos_cols = [to_columns(pos_slots[h], f"pos{h}", f"score{h}1") for h in range(SLOT_PASSES)]
+        vs_first = sb.tile([P, VS_SPLIT], F32, name="vs_first")
+        nc.scalar.activation(vs_first[:], vs_pool[:].indirect(offsets[:, : VS_SPLIT // LIST_ROWS]), ACT.Copy)
+        vs_last = sb.tile([P, N - VS_SPLIT], F32, name="vs_last", tag="kw_slots1", align_bytes=64)
+        nc.vector.tensor_copy(vs_last[:], vs_pool[:].indirect(offsets[:, VS_SPLIT // LIST_ROWS :]))
+        vs_chunks = [vs_first[:, c : c + P] for c in range(0, VS_SPLIT, P)] + [vs_last[:, c : c + P] for c in range(0, N - VS_SPLIT, P)]
+        pos_cols = [to_columns(pos_slots[h], f"pos{h}", f"score{h}1", move) for h, move in enumerate((nc.vector.tensor_copy, nc.scalar.copy))]
         place_banks = [spread(pos_cols[0], "pos0", "place0")]
 
         def dealt(tile, cols):
@@ -167,28 +171,32 @@ def tile_attend_soft_draft_cap_topkq256n1024t2048_kernel(tc, q_words, q_scales, 
                 )
             return score
 
+        whole = [slice(0, PASS)]
+        halves = [slice(0, PASS // 2), slice(PASS // 2, PASS)]
+        capped_tags = {(0, 0): ["capped_a", "capped_b"], (1, 0): ["capped_a", "capped_c"], (0, 1): ["capped_a"], (1, 1): ["capped11"]}
         e_all = {}
         for h in range(SLOT_PASSES):
             for j in range(ROW_TILES):
-                pieces = [(slice(0, PASS), f"score{j}{h}")]
+                pieces = whole if h else halves
                 if (j, h) == (0, 0):
-                    pieces = [(slice(0, PASS // 2), "spare"), (slice(PASS // 2, PASS), "score00")]
-                capped = sb.tile([P, PASS], F32, name=f"capped{j}{h}", tag="capped10" if (j, h) == (0, 1) else f"capped{j}{h}", align_bytes=64)
+                    banks = [scores(j, h, cols, tag)[:] for cols, tag in zip(halves, ("spare", "score00"))]
+                else:
+                    bank = scores(j, h, whole[0], f"score{j}{h}")
+                    banks = [bank[:, cols] for cols in pieces]
                 e_all[j, h] = sb.tile([P, PASS], F32, name=f"e{j}{h}")
-                for cols, tag in pieces:
+                capped = []
+                for cols, bank, tag in zip(pieces, banks, capped_tags[j, h]):
+                    capped.append(sb.tile([P, cols.stop - cols.start], F32, name=f"capped{j}{h}_{cols.start}", tag=tag, align_bytes=64))
                     nc.scalar.activation(
-                        dealt(capped, cols).rearrange("p u (k e) -> p u k e", e=2),
-                        scores(j, h, cols, tag)[:].rearrange("p (k u e) -> p u k e", u=2, e=2),
-                        ACT.Tanh,
-                        scale=1.0 / CAP,
+                        capped[-1][:].rearrange("p (u k e) -> p u k e", u=2, e=2), bank.rearrange("p (k u e) -> p u k e", u=2, e=2), ACT.Tanh, scale=1.0 / CAP
                     )
-                for cols, tag in pieces:
-                    nc.scalar.activation(dealt(e_all[j, h], cols), dealt(capped, cols), ACT.Exp, scale=CAP)
+                for cols, piece in zip(pieces, capped):
+                    nc.scalar.activation(dealt(e_all[j, h], cols), piece[:].rearrange("p (u x) -> p u x", u=2), ACT.Exp, scale=CAP)
 
         place_banks.append(spread(pos_cols[1], "pos1", "score00"))
         vs_turned = ps.tile([P, P + 2 * (N // P - 1)], F32, name="vs_turned", tag="score01")
         for c in reversed(range(N // P)):
-            nc.tensor.transpose(vs_turned[:, 2 * c : 2 * c + P], vs_slots[c // CHUNKS][:, c % CHUNKS * P : (c % CHUNKS + 1) * P], ident[:])
+            nc.tensor.transpose(vs_turned[:, 2 * c : 2 * c + P], vs_chunks[c], ident[:])
 
         v_turned = sb.tile([P, N], BF16, name="v_turned", align_bytes=64)
 
@@ -232,8 +240,6 @@ def tile_attend_soft_draft_cap_topkq256n1024t2048_kernel(tc, q_words, q_scales, 
                 nc.tensor.transpose(w_bank[:, u, :], w[:].bitcast(F32)[:, u * P : (u + 1) * P], ident[:])
             lay(w_bank[:], w_turned[j, g][:], nc.scalar.copy)
 
-        whole = [slice(0, PASS)]
-        halves = [slice(0, PASS // 2), slice(PASS // 2, PASS)]
         mask(0, 0)
         lift(0, 0)
         mask(1, 0)

@@ -28,7 +28,8 @@ SLOT_PASSES = N // PASS
 ROW_TILES = NQ // P
 CHUNKS = PASS // P
 LIVE = P - 1
-VS_SPLIT = 768
+VS_SPLIT = 512
+VS_LAST = 256
 
 
 def tile_attend_soft_draft_cap_topkq256n1024t2048_kernel(tc, q_words, q_scales, k_words, k_scales, vT, vs, pos, qpos, offs, out):
@@ -139,9 +140,8 @@ def tile_attend_soft_draft_cap_topkq256n1024t2048_kernel(tc, q_words, q_scales, 
         pos_slots = [gather_row(pos_pool, h, "pos") for h in range(SLOT_PASSES)]
         vs_first = sb.tile([P, VS_SPLIT], F32, name="vs_first")
         nc.scalar.activation(vs_first[:], vs_pool[:].indirect(offsets[:, : VS_SPLIT // LIST_ROWS]), ACT.Copy)
-        vs_last = sb.tile([P, N - VS_SPLIT], F32, name="vs_last", tag="kw_slots1", align_bytes=64)
-        nc.vector.tensor_copy(vs_last[:], vs_pool[:].indirect(offsets[:, VS_SPLIT // LIST_ROWS :]))
-        vs_chunks = [vs_first[:, c : c + P] for c in range(0, VS_SPLIT, P)] + [vs_last[:, c : c + P] for c in range(0, N - VS_SPLIT, P)]
+        vs_middle = sb.tile([P, N - VS_SPLIT - VS_LAST], F32, name="vs_middle", tag="kw_slots1", align_bytes=64)
+        nc.vector.tensor_copy(vs_middle[:], vs_pool[:].indirect(offsets[:, VS_SPLIT // LIST_ROWS : (N - VS_LAST) // LIST_ROWS]))
         pos_cols = [to_columns(pos_slots[h], f"pos{h}", f"score{h}1", move) for h, move in enumerate((nc.vector.tensor_copy, nc.scalar.copy))]
         place_banks = [spread(pos_cols[0], "pos0", "place0")]
 
@@ -194,9 +194,6 @@ def tile_attend_soft_draft_cap_topkq256n1024t2048_kernel(tc, q_words, q_scales, 
                     nc.scalar.activation(dealt(e_all[j, h], cols), piece[:].rearrange("p (u x) -> p u x", u=2), ACT.Exp, scale=CAP)
 
         place_banks.append(spread(pos_cols[1], "pos1", "score00"))
-        vs_turned = ps.tile([P, P + 2 * (N // P - 1)], F32, name="vs_turned", tag="score01")
-        for c in reversed(range(N // P)):
-            nc.tensor.transpose(vs_turned[:, 2 * c : 2 * c + P], vs_chunks[c], ident[:])
 
         v_turned = sb.tile([P, N], BF16, name="v_turned", align_bytes=64)
 
@@ -241,22 +238,28 @@ def tile_attend_soft_draft_cap_topkq256n1024t2048_kernel(tc, q_words, q_scales, 
             lay(w_bank[:], w_turned[j, g][:], nc.scalar.copy)
 
         mask(0, 0)
+        vs_last = sb.tile([P, VS_LAST], F32, name="vs_last", tag="capped_b", align_bytes=64)
+        nc.vector.tensor_copy(vs_last[:], vs_pool[:].indirect(offsets[:, (N - VS_LAST) // LIST_ROWS :]))
+        vs_chunks = [part[:, c : c + P] for part in (vs_first, vs_middle, vs_last) for c in range(0, part.shape[1], P)]
+        vs_turned = ps.tile([P, P + 2 * (N // P - 1)], F32, name="vs_turned", tag="score01")
+        for c in reversed(range(N // P)):
+            nc.tensor.transpose(vs_turned[:, 2 * c : 2 * c + P], vs_chunks[c], ident[:])
         lift(0, 0)
         mask(1, 0)
-        mask(0, 1)
         lift(1, 0)
+        mask(0, 1)
         vs_cols = sb.tile([P, N // P], F32, name="vs_cols", tag="masked00", align_bytes=64)
         nc.vector.tensor_copy(vs_cols[:], vs_turned[:, LIVE::2])
         scale_banks = [spread(vs_cols[:, h * CHUNKS : (h + 1) * CHUNKS], f"vs{h}", f"scale{h}") for h in range(SLOT_PASSES)]
-        lift(0, 1)
         mask(1, 1)
-        invert(slice(0, 1))
-        values(0, "capped11", "score11")
+        lift(0, 1)
         lift(1, 1)
+        invert(slice(0, 1))
+        invert(slice(1, 2))
+        values(0, "capped11", "score11")
         weigh(0, 0, whole)
         values(1, "masked01", "place0")
         weigh(0, 1, whole)
-        invert(slice(1, 2))
         weigh(1, 0, whole)
         weigh(1, 1, halves)
 

@@ -28,6 +28,7 @@ SLOT_PASSES = N // PASS
 ROW_TILES = NQ // P
 CHUNKS = PASS // P
 LIVE = P - 1
+ZERO_SPLIT = 1024
 VS_SPLIT = 512
 VS_LAST = 256
 
@@ -71,13 +72,14 @@ def tile_attend_soft_draft_cap_topkq256n1024t2048_kernel(tc, q_words, q_scales, 
 
         log_floor = sb.tile([P, 1], F32, name="log_floor")
         nc.vector.memset(log_floor[:], LOG_FLOOR)
+        zero_words(pos_pool[:LIVE, :ZERO_SPLIT])
         zero_words(ks_pool[: P - QUAD, :].bitcast(I32))
         k_scale = [sb.tile([P, D_PASSES * PASS], U8, name=f"k_scale{h}", align_bytes=64) for h in range(SLOT_PASSES)]
         for h in range(SLOT_PASSES):
             zero_words(k_scale[h][:].bitcast(I32))
         ident = sb.tile([P, P], F32, name="ident")
         make_identity(nc, ident[:])
-        nc.gpsimd.memset(pos_pool[:LIVE, :], 0.0)
+        nc.gpsimd.memset(pos_pool[:LIVE, ZERO_SPLIT:], 0.0)
         nc.gpsimd.memset(vs_pool[:LIVE, :], 0.0)
 
         floor = sb.tile([P, 1], F32, name="floor")

@@ -29,8 +29,7 @@ ROW_TILES = NQ // P
 CHUNKS = PASS // P
 LIVE = P - 1
 ZERO_SPLIT = 1024
-VS_SPLIT = 512
-VS_LAST = 256
+VS_SPLIT = 768
 
 
 def tile_attend_soft_draft_cap_topkq256n1024t2048_kernel(tc, q_words, q_scales, k_words, k_scales, vT, vs, pos, qpos, offs, out):
@@ -142,8 +141,8 @@ def tile_attend_soft_draft_cap_topkq256n1024t2048_kernel(tc, q_words, q_scales, 
         pos_slots = [gather_row(pos_pool, h, "pos") for h in range(SLOT_PASSES)]
         vs_first = sb.tile([P, VS_SPLIT], F32, name="vs_first")
         nc.scalar.activation(vs_first[:], vs_pool[:].indirect(offsets[:, : VS_SPLIT // LIST_ROWS]), ACT.Copy)
-        vs_middle = sb.tile([P, N - VS_SPLIT - VS_LAST], F32, name="vs_middle", tag="kw_slots1", align_bytes=64)
-        nc.vector.tensor_copy(vs_middle[:], vs_pool[:].indirect(offsets[:, VS_SPLIT // LIST_ROWS : (N - VS_LAST) // LIST_ROWS]))
+        vs_last = sb.tile([P, N - VS_SPLIT], F32, name="vs_last", tag="kw_slots1", align_bytes=64)
+        nc.vector.tensor_copy(vs_last[:], vs_pool[:].indirect(offsets[:, VS_SPLIT // LIST_ROWS :]))
         pos_cols = [to_columns(pos_slots[h], f"pos{h}", f"score{h}1", move) for h, move in enumerate((nc.vector.tensor_copy, nc.scalar.copy))]
         place_banks = [spread(pos_cols[0], "pos0", "place0")]
 
@@ -240,9 +239,7 @@ def tile_attend_soft_draft_cap_topkq256n1024t2048_kernel(tc, q_words, q_scales, 
             lay(w_bank[:], w_turned[j, g][:], nc.scalar.copy)
 
         mask(0, 0)
-        vs_last = sb.tile([P, VS_LAST], F32, name="vs_last", tag="capped_b", align_bytes=64)
-        nc.vector.tensor_copy(vs_last[:], vs_pool[:].indirect(offsets[:, (N - VS_LAST) // LIST_ROWS :]))
-        vs_chunks = [part[:, c : c + P] for part in (vs_first, vs_middle, vs_last) for c in range(0, part.shape[1], P)]
+        vs_chunks = [part[:, c : c + P] for part in (vs_first, vs_last) for c in range(0, part.shape[1], P)]
         vs_turned = ps.tile([P, P + 2 * (N // P - 1)], F32, name="vs_turned", tag="score01")
         for c in reversed(range(N // P)):
             nc.tensor.transpose(vs_turned[:, 2 * c : 2 * c + P], vs_chunks[c], ident[:])

@@ -5,7 +5,7 @@ from concourse.masks import make_identity
 
 N, T, D, DV, NQ = 1024, 2048, 1024, 128, 256
 CAP = 2.0
-LOG_FLOOR = -70.0
+LOG_PENALTY = 21.0
 FLOPS = 2 * NQ * N * (D + DV)
 
 F32 = mybir.dt.float32
@@ -21,15 +21,16 @@ ALU = mybir.AluOpType
 
 P = 128
 PASS = 512
+PACK = 4
 QUAD = 32
 LIST_ROWS = 16
 D_PASSES = D // PASS
 SLOT_PASSES = N // PASS
 ROW_TILES = NQ // P
 CHUNKS = PASS // P
+QUARTER = PASS // 2
 LIVE = P - 1
 ZERO_SPLIT = 1024
-VS_SPLIT = 768
 
 
 def tile_attend_soft_draft_cap_topkq256n1024t2048_kernel(tc, q_words, q_scales, k_words, k_scales, vT, vs, pos, qpos, offs, out):
@@ -41,252 +42,228 @@ def tile_attend_soft_draft_cap_topkq256n1024t2048_kernel(tc, q_words, q_scales, 
         q_scale = sb.tile([P, D_PASSES * NQ], U8, name="q_scale", align_bytes=64)
         nc.gpsimd.memset(q_scale[:].bitcast(I32), 0)
 
-        def load_query_scales(queue, quad):
-            queue.dma_start(
+        def load_query_scales(quad):
+            nc.sync.dma_start(
                 q_scale[QUAD * quad : QUAD * quad + 4, :].rearrange("p (o q) -> p o q", o=D_PASSES).bitcast(I32),
                 q_scales[0, :, 4 * quad : 4 * quad + 4, :].rearrange("o f q -> f o q").bitcast(I32),
             )
 
         offsets = sb.tile([P, N // LIST_ROWS], U16, name="offsets")
         nc.sync.dma_start(offsets[:], offs)
-        ks_pool = sb.tile([P, T], U8, name="ks_pool", align_bytes=64)
+        ks_pool = sb.tile([P, T], U8, name="ks_pool", tag="ks_pool", align_bytes=64)
         nc.sync.dma_start(ks_pool[P - QUAD :, :].bitcast(I32), k_scales.rearrange("o f t -> f o t").bitcast(I32))
         pos_pool = sb.tile([P, T], F32, name="pos_pool")
         nc.sync.dma_start(pos_pool[LIVE:, :], pos[0:1, :])
+        q_place = sb.tile([P, ROW_TILES], F32, name="q_place")
+        with nc.allow_non_contiguous_dma(reason="one place for each query row"):
+            nc.sync.dma_start(q_place[:], qpos[0].rearrange("(j p) o -> p (j o)", p=P))
         vs_pool = sb.tile([P, T], F32, name="vs_pool")
         nc.sync.dma_start(vs_pool[LIVE:, :], vs[0:1, :])
-        load_query_scales(nc.sync, 0)
-        load_query_scales(nc.sync, 1)
+        load_query_scales(0)
+        load_query_scales(1)
         kw_pool = sb.tile([P, T], I32, name="kw_pool", align_bytes=64)
         nc.sync.dma_start(kw_pool[:], k_words[0].rearrange("p t b -> p (t b)").bitcast(I32))
         q_code = sb.tile([P, D_PASSES, NQ], I32, name="q_code", align_bytes=64)
         nc.sync.dma_start(q_code[:], q_words[0].rearrange("o p q r -> p o (q r)").bitcast(I32))
-        load_query_scales(nc.sync, 2)
-        load_query_scales(nc.sync, 3)
+        load_query_scales(2)
+        load_query_scales(3)
 
         def zero_words(words):
             last = words.shape[1] - 1
             nc.vector.memset(words[:, :last], 0)
             nc.vector.memset(words[:, last:], 0)
 
-        log_floor = sb.tile([P, 1], F32, name="log_floor")
-        nc.vector.memset(log_floor[:], LOG_FLOOR)
+        log_penalty = sb.tile([P, 1], F32, name="log_penalty")
+        nc.vector.memset(log_penalty[:], LOG_PENALTY)
+        v_slots = sb.tile([P, N], BF16, name="v_slots", align_bytes=64)
+        inv_cap = v_slots[:, QUARTER:].bitcast(F32)[:, 0:1]
+        nc.vector.memset(inv_cap, -1.0 / CAP)
+        hidden = v_slots[:, 3 * QUARTER :].bitcast(F32)[:, 0:1]
+        nc.scalar.activation(hidden, log_penalty[:], ACT.Exp)
         zero_words(pos_pool[:LIVE, :ZERO_SPLIT])
         zero_words(ks_pool[: P - QUAD, :].bitcast(I32))
-        k_scale = [sb.tile([P, D_PASSES * PASS], U8, name=f"k_scale{h}", align_bytes=64) for h in range(SLOT_PASSES)]
-        for h in range(SLOT_PASSES):
-            zero_words(k_scale[h][:].bitcast(I32))
+        k_scale = sb.tile([P, D_PASSES * N], U8, name="k_scale", align_bytes=64)
+        zero_words(k_scale[:].bitcast(I32))
         ident = sb.tile([P, P], F32, name="ident")
         make_identity(nc, ident[:])
         nc.gpsimd.memset(pos_pool[:LIVE, ZERO_SPLIT:], 0.0)
         nc.gpsimd.memset(vs_pool[:LIVE, :], 0.0)
 
-        floor = sb.tile([P, 1], F32, name="floor")
-        nc.scalar.activation(floor[:], log_floor[:], ACT.Exp)
-        floor_sum = sb.tile([P, 1], F32, name="floor_sum")
-        nc.scalar.activation(floor_sum[:], floor[:], ACT.Copy, scale=float(N))
+        def entries(first, count):
+            return offsets[:, first // LIST_ROWS : (first + count) // LIST_ROWS]
 
-        def entries(h):
-            return offsets[:, h * PASS // LIST_ROWS : (h + 1) * PASS // LIST_ROWS]
-
-        for h in range(SLOT_PASSES):
-            ks_slots = sb.tile([P, PASS], U8, name=f"ks_slots{h}", tag=f"after_scale_moves{h}", align_bytes=64)
-            nc.vector.tensor_copy(ks_slots[:], ks_pool[:].indirect(entries(h)))
-            for quad in range(P // QUAD):
-                nc.sync.dma_start(
-                    k_scale[h][QUAD * quad : QUAD * quad + 4, :].bitcast(I32),
-                    ks_slots[P - QUAD + 8 * quad : P - QUAD + 8 * quad + 8, :].bitcast(I32),
-                )
-        q_place = sb.tile([P, ROW_TILES], F32, name="q_place", tag="after_scale_moves0", align_bytes=64)
-        with nc.allow_non_contiguous_dma(reason="one place for each query row"):
-            nc.sync.dma_start(q_place[:], qpos[0].rearrange("(j p) o -> p (j o)", p=P))
-        v_pool = sb.tile([P, T], F32, name="v_pool", tag="after_scale_moves1", align_bytes=64)
+        ks_slots = sb.tile([P, N], U8, name="ks_slots", tag="after_scale_moves", align_bytes=64)
+        nc.vector.tensor_copy(ks_slots[:], ks_pool[:].indirect(offsets[:]))
+        for quad in range(P // QUAD):
+            nc.sync.dma_start(
+                k_scale[QUAD * quad : QUAD * quad + 4, :].bitcast(I32),
+                ks_slots[P - QUAD + 8 * quad : P - QUAD + 8 * quad + 8, :].bitcast(I32),
+            )
+        v_pool = sb.tile([P, T], F32, name="v_pool", tag="ks_pool", align_bytes=64)
         nc.sync.dma_start(v_pool[:], vT)
+
+        q_bank = ps.tile([P, ROW_TILES, P], F32, name="q_bank", tag="early")
+        for j in range(ROW_TILES):
+            nc.tensor.transpose(q_bank[:, j, :], q_place[:, j : j + 1].to_broadcast([P, P]), ident[:])
+        q_spread = sb.tile([P, NQ], F32, name="q_spread", tag="q_spread", align_bytes=64)
+        nc.vector.tensor_copy(q_spread[:], q_bank[:].rearrange("p j q -> p (j q)"))
+
+        pos_banks = []
+        for h in range(SLOT_PASSES):
+            pos_slots = sb.tile([P, PASS], F32, name=f"pos_slots{h}", tag=f"pos_slots{h}", align_bytes=64)
+            nc.scalar.activation(pos_slots[:], pos_pool[:].indirect(entries(h * PASS, PASS)), ACT.Copy)
+            pos_banks.append(ps.tile([P, CHUNKS, P], F32, name=f"pos_bank{h}", tag=("score0", "late")[h]))
+            for c in range(CHUNKS):
+                nc.tensor.transpose(pos_banks[h][:, c, :], pos_slots[:, c * P : (c + 1) * P], ident[:])
+
+        vs_slots = sb.tile([P, N], F32, name="vs_slots")
+        nc.scalar.activation(vs_slots[:], vs_pool[:].indirect(offsets[:]), ACT.Copy)
+
+        sums = {(j, h): ps.tile([P, PASS], F32, name=f"sum{j}{h}") for j in range(ROW_TILES) for h in range(SLOT_PASSES)}
+        added = {key: [] for key in sums}
+
+        def add_turned(src, j, h, c):
+            added[j, h].append(c)
+            nc.tensor.matmul(
+                sums[j, h][:, c * P : (c + 1) * P],
+                lhsT=src[:, j * P : (j + 1) * P],
+                rhs=ident[:],
+                is_transpose=True,
+                start=(len(added[j, h]) == 1),
+                stop=(len(added[j, h]) == 2 * CHUNKS),
+            )
+
+        def penalties(h, cols_tag, tag):
+            pos_cols = sb.tile([P, CHUNKS], F32, name=f"pos_cols{h}", tag=cols_tag, align_bytes=64)
+            nc.vector.tensor_copy(pos_cols[:], pos_banks[h][:, :, LIVE])
+            penalty = sb.tile([P, CHUNKS, NQ], F32, name=f"penalty{h}", tag=tag, align_bytes=64)
+            for c in range(CHUNKS):
+                nc.vector.tensor_scalar(penalty[:, c, :], q_spread[:], pos_cols[:, c : c + 1], hidden, ALU.is_lt, ALU.mult)
+            return penalty
+
+        penalty0 = penalties(0, "pos_cols0", "penalty0")
+        for j in range(ROW_TILES):
+            for c in range(CHUNKS):
+                add_turned(penalty0[:, c, :], j, 0, c)
 
         k_code = []
         for h in range(SLOT_PASSES):
-            parted = sb.tile([P, D_PASSES, PASS], U16, name=f"k_code{h}", align_bytes=64)
             gathered = []
             for a in range(2):
-                kw_slots = sb.tile([P, PASS // 2], U32, name=f"kw_slots{h}{a}", tag=f"kw_slots{a}", align_bytes=64)
-                first = (2 * h + a) * PASS // 2 // LIST_ROWS
-                nc.vector.tensor_copy(kw_slots[:], kw_pool[:].bitcast(U32).indirect(offsets[:, first : first + PASS // 2 // LIST_ROWS]))
+                kw_slots = sb.tile([P, QUARTER], U32, name=f"kw_slots{h}{a}", tag=f"kw_slots{a}", align_bytes=64)
+                nc.vector.tensor_copy(kw_slots[:], kw_pool[:].bitcast(U32).indirect(entries((2 * h + a) * QUARTER, QUARTER)))
                 gathered.append(kw_slots)
             for a in range(2):
+                parted = sb.tile([P, D_PASSES, QUARTER], U16, name=f"k_code{h}{a}", tag=f"k_code{h}{a}", align_bytes=64)
                 nc.vector.tensor_copy(
-                    parted[:, :, a * PASS // 2 : (a + 1) * PASS // 2].rearrange("p o (b n) -> p b o n", b=2),
+                    parted[:].rearrange("p o (b n) -> p b o n", b=2),
                     gathered[a][:].bitcast(U16).rearrange("p (b n o) -> p b o n", b=2, o=D_PASSES),
                 )
-            k_code.append(parted)
+                k_code.append(parted)
 
-        def gather_row(pool, h, name):
-            slots = sb.tile([P, PASS], F32, name=f"{name}_slots{h}")
-            nc.scalar.activation(slots[:], pool[:].indirect(entries(h)), ACT.Copy)
-            return slots
+        penalty1 = penalties(1, "kw_slots0", "kw_slots1")
 
-        def to_columns(slots, name, tag, move):
-            bank = ps.tile([P, CHUNKS, P], F32, name=name + "_turned", tag=tag)
+        capped = []
+        for k in range(2 * SLOT_PASSES):
+            h, a = divmod(k, 2)
+            score = ps.tile([P, 2, NQ], F32, name=f"score{k}", tag=("score0", "score1", "early", "late")[k])
+            for i in range(2):
+                first = (2 * k + i) * P
+                for o in range(D_PASSES):
+                    nc.tensor.matmul_mx(
+                        out=score[:, i, :],
+                        lhsT=k_code[k][:, o, i * P : (i + 1) * P].bitcast(FP4X4),
+                        lhsT_scale=k_scale[:, o * N + first : o * N + first + P],
+                        rhs=q_code[:, o, :].bitcast(FP8X4),
+                        rhs_scale=q_scale[:, o * NQ : (o + 1) * NQ],
+                        start=(o == 0),
+                        stop=(o == D_PASSES - 1),
+                    )
+            capped.append(sb.tile([P, 2, NQ], F32, name=f"capped{k}", tag=f"capped{k}", align_bytes=64))
+            last = k == 2 * SLOT_PASSES - 1
+            for cols in [slice(0, P), slice(P, NQ)] if last else [slice(0, NQ)]:
+                nc.scalar.activation(capped[k][:, :, cols], score[:, :, cols], ACT.Tanh, scale=inv_cap)
+        for j in range(ROW_TILES):
             for c in range(CHUNKS):
-                nc.tensor.transpose(bank[:, c, :], slots[:, c * P : (c + 1) * P], ident[:])
-            cols = sb.tile([P, CHUNKS], F32, name=name + "_cols")
-            move(cols[:], bank[:, :, LIVE])
-            return cols
-
-        def spread(cols, name, tag):
-            bank = ps.tile([P, PASS], F32, name=name + "_bank", tag=tag)
+                add_turned(capped[c // 2][:, c % 2, :], j, 0, c)
+            for i in range(2):
+                add_turned(capped[2][:, i, :], j, 1, i)
             for c in range(CHUNKS):
-                nc.tensor.transpose(bank[:].rearrange("p (u c k e) -> p c k u e", u=2, c=CHUNKS, e=2)[:, c], cols[:, c : c + 1].to_broadcast([P, P]), ident[:])
-            return bank
+                add_turned(penalty1[:, c, :], j, 1, c)
+            for i in range(2):
+                add_turned(capped[3][:, i, :], j, 1, 2 + i)
 
-        pos_slots = [gather_row(pos_pool, h, "pos") for h in range(SLOT_PASSES)]
-        vs_first = sb.tile([P, VS_SPLIT], F32, name="vs_first")
-        nc.scalar.activation(vs_first[:], vs_pool[:].indirect(offsets[:, : VS_SPLIT // LIST_ROWS]), ACT.Copy)
-        vs_last = sb.tile([P, N - VS_SPLIT], F32, name="vs_last", tag="kw_slots1", align_bytes=64)
-        nc.vector.tensor_copy(vs_last[:], vs_pool[:].indirect(offsets[:, VS_SPLIT // LIST_ROWS :]))
-        pos_cols = [to_columns(pos_slots[h], f"pos{h}", f"score{h}1", move) for h, move in enumerate((nc.vector.tensor_copy, nc.scalar.copy))]
-        place_banks = [spread(pos_cols[0], "pos0", "place0")]
+        vs_cols = []
+        for g in range(SLOT_PASSES):
+            vs_cols.append(sb.tile([P, 1, PACK], F32, name=f"vs_cols{g}", tag=f"k_code0{g}", align_bytes=64))
+            nc.sync.dma_start(vs_cols[g][:, 0, :], vs_slots[LIVE:, g * PASS : (g + 1) * PASS].rearrange("o (p r) -> o p r", r=PACK))
 
-        def dealt(tile, cols):
-            return tile[:].rearrange("p (u x) -> p u x", u=2)[:, :, cols.start // 2 : cols.stop // 2]
+        nc.scalar.activation(v_slots[:, :QUARTER], v_pool[:].indirect(entries(0, QUARTER)), ACT.Copy)
+        nc.vector.tensor_copy(v_slots[:, 3 * QUARTER :], v_pool[:].indirect(entries(3 * QUARTER, QUARTER)))
+        nc.scalar.activation(v_slots[:, QUARTER : 3 * QUARTER], v_pool[:].indirect(entries(QUARTER, PASS)), ACT.Copy)
 
-        def lay(bank, dst, move):
-            move(dst.bitcast(F32).rearrange("p (c u) -> p c u", u=2), bank.rearrange("p u c -> p c u"))
+        least = sb.tile([P, ROW_TILES, SLOT_PASSES], F32, name="least")
+        lowered = {}
+        for j in range(ROW_TILES):
+            for h in range(SLOT_PASSES):
+                lowered[j, h] = sb.tile([P, PACK, P], F32, name=f"lowered{j}{h}", tag=f"lowered{j}{h}", align_bytes=64)
+                nc.vector.tensor_scalar(
+                    lowered[j, h][:], sums[j, h][:].rearrange("p (k r) -> p r k", r=PACK), CAP, least[:, j, 0:1] if h else None, ALU.mult, ALU.min, accum_out=least[:, j, h : h + 1]
+                )
 
-        def quantise(src, name, codes):
-            columns = src.shape[1] // 4
-            scales = sb.tile([P, columns], U8, name=name + "_scale", align_bytes=64)
+        v_turned = {}
+
+        def values(g, bank_tag, turned_tag):
+            v_turned[g] = sb.tile([P, PASS], BF16, name=f"v_turned{g}", tag=turned_tag, align_bytes=64)
+            v_bank = ps.tile([P, 2, DV], F32, name=f"v_bank{g}", tag=bank_tag)
+            for u in range(2):
+                nc.tensor.transpose(v_bank[:, u, :], v_slots[:, g * PASS : (g + 1) * PASS].bitcast(F32)[:, u::2], ident[:])
+            nc.scalar.copy(v_turned[g][:].bitcast(F32).rearrange("p (c u) -> p c u", u=2), v_bank[:].rearrange("p u c -> p c u"))
+
+        values(1, "sum00", "v_turned1")
+
+        p_sum = sb.tile([P, SLOT_PASSES, ROW_TILES], F32, name="p_sum")
+        p_tags = {(0, 0): "score0", (0, 1): "score1", (1, 0): "early", (1, 1): "late"}
+        w = {}
+        for j in range(ROW_TILES):
+            for g in range(SLOT_PASSES):
+                prob = sb.tile([P, PACK, P], F32, name=f"prob{j}{g}")
+                nc.scalar.activation(prob[:], lowered[j, g][:], ACT.Exp, scale=-1.0, bias=least[:, j, 1:2], accum_out=p_sum[:, g, j : j + 1])
+                p_bank = ps.tile([P, PACK, P], F32, name=f"p_bank{j}{g}", tag=p_tags[j, g])
+                for r in range(PACK):
+                    nc.tensor.transpose(p_bank[:, r, :], prob[:, r, :], ident[:])
+                w[j, g] = sb.tile([P, P, PACK], BF16, name=f"w{j}{g}", align_bytes=64)
+                nc.vector.tensor_tensor(w[j, g][:], p_bank[:].rearrange("p r q -> p q r"), vs_cols[g][:].to_broadcast([P, P, PACK]), ALU.mult)
+
+        values(0, "sum01", "lowered11")
+
+        row_sum = sb.tile([P, ROW_TILES], F32, name="row_sum")
+        nc.gpsimd.tensor_tensor(row_sum[:], p_sum[:, 0, :], p_sum[:, 1, :], ALU.add)
+        inv_sum = sb.tile([P, ROW_TILES], F32, name="inv_sum")
+        nc.vector.reciprocal(inv_sum[:], row_sum[:])
+
+
+        def quantise(src, name):
+            codes = sb.tile([P, P], U32, name=name + "_code", align_bytes=64)
+            scales = sb.tile([P, P], U8, name=name + "_scale", align_bytes=64)
             nc.vector.quantize_mx(out=codes[:].bitcast(FP8X4), scales=scales[:], in_=src)
             return codes, scales
 
-        def scores(j, h, cols, tag):
-            score = ps.tile([P, cols.stop - cols.start], F32, name=f"score{j}{h}_{cols.start}", tag=tag)
-            for o in range(D_PASSES):
-                nc.tensor.matmul_mx(
-                    out=score[:],
-                    lhsT=q_code[:, o, j * P : (j + 1) * P].bitcast(FP8X4),
-                    lhsT_scale=q_scale[:, o * NQ + j * P : o * NQ + (j + 1) * P],
-                    rhs=k_code[h][:, o, cols].bitcast(FP4X4),
-                    rhs_scale=k_scale[h][:, o * PASS + cols.start : o * PASS + cols.stop],
-                    start=(o == 0),
-                    stop=(o == D_PASSES - 1),
-                )
-            return score
-
-        whole = [slice(0, PASS)]
-        halves = [slice(0, PASS // 2), slice(PASS // 2, PASS)]
-        capped_tags = {(0, 0): ["capped_a", "capped_b"], (1, 0): ["capped_a", "capped_c"], (0, 1): ["capped_a"], (1, 1): ["capped11"]}
-        e_all = {}
-        for h in range(SLOT_PASSES):
-            for j in range(ROW_TILES):
-                pieces = whole if h else halves
-                if (j, h) == (0, 0):
-                    banks = [scores(j, h, cols, tag)[:] for cols, tag in zip(halves, ("spare", "score00"))]
-                else:
-                    bank = scores(j, h, whole[0], f"score{j}{h}")
-                    banks = [bank[:, cols] for cols in pieces]
-                e_all[j, h] = sb.tile([P, PASS], F32, name=f"e{j}{h}")
-                capped = []
-                for cols, bank, tag in zip(pieces, banks, capped_tags[j, h]):
-                    capped.append(sb.tile([P, cols.stop - cols.start], F32, name=f"capped{j}{h}_{cols.start}", tag=tag, align_bytes=64))
-                    nc.scalar.activation(
-                        capped[-1][:].rearrange("p (u k e) -> p u k e", u=2, e=2), bank.rearrange("p (k u e) -> p u k e", u=2, e=2), ACT.Tanh, scale=1.0 / CAP
-                    )
-                for cols, piece in zip(pieces, capped):
-                    nc.scalar.activation(dealt(e_all[j, h], cols), piece[:].rearrange("p (u x) -> p u x", u=2), ACT.Exp, scale=CAP)
-
-        place_banks.append(spread(pos_cols[1], "pos1", "score00"))
-
-        v_turned = sb.tile([P, N], BF16, name="v_turned", align_bytes=64)
-
-        def values(g, slots_tag, bank_tag):
-            v_slots = sb.tile([P, PASS], BF16, name=f"v_slots{g}", tag=slots_tag, align_bytes=64)
-            nc.scalar.activation(v_slots[:], v_pool[:].indirect(entries(g)), ACT.Copy)
-            v_bank = ps.tile([P, 2, DV], F32, name=f"v_bank{g}", tag=bank_tag)
-            for u in range(2):
-                nc.tensor.transpose(v_bank[:, u, :], v_slots[:].bitcast(F32)[:, u::2], ident[:])
-            lay(v_bank[:], v_turned[:, g * PASS : (g + 1) * PASS], nc.scalar.copy)
-
-        e_sum = sb.tile([P, SLOT_PASSES, ROW_TILES], F32, name="e_sum")
-        stats = sb.tile([P, ROW_TILES], F32, name="stats")
-        inv_stats = sb.tile([P, ROW_TILES], F32, name="inv_stats")
-        inv_top = inv_stats[:, :ROW_TILES]
-        masked, lifted, top, w_turned = {}, {}, {}, {}
-
-        def mask(j, h):
-            masked[j, h] = sb.tile([P, PASS], F32, name=f"masked{j}{h}", tag=f"masked{j}{h}", align_bytes=64)
-            nc.vector.scalar_tensor_tensor(
-                masked[j, h][:], place_banks[h][:], q_place[:, j : j + 1], e_all[j, h][:], ALU.is_le, ALU.mult, accum_out=e_sum[:, h, j : j + 1]
-            )
-
-        def lift(j, h):
-            lifted[j, h] = sb.tile([P, PASS], F32, name=f"lifted{j}{h}", tag=f"lifted{j}{h}", align_bytes=64)
-            top[j, h] = stats[:, j : j + 1] if h else sb.tile([P, 1], F32, name=f"top{j}")[:]
-            nc.vector.tensor_scalar(lifted[j, h][:], masked[j, h][:], floor[:], top[j, h - 1] if h else None, ALU.max, ALU.max, accum_out=top[j, h])
-
-        def invert(cols):
-            nc.vector.reciprocal(inv_stats[:, cols], stats[:, cols])
-
-        w_tags = {(0, 0): "score01", (0, 1): "score10", (1, 0): "spare", (1, 1): "score11"}
-
-        def weigh(j, g, pieces):
-            w = sb.tile([P, PASS], BF16, name=f"w{j}{g}", align_bytes=64)
-            for cols in pieces:
-                nc.vector.scalar_tensor_tensor(w[:, cols], lifted[j, g][:, cols], inv_top[:, j : j + 1], scale_banks[g][:, cols], ALU.mult, ALU.mult)
-            w_bank = ps.tile([P, 2, P], F32, name=f"w_bank{j}{g}", tag=w_tags[j, g])
-            w_turned[j, g] = sb.tile([P, PASS], BF16, name=f"w_turned{j}{g}", align_bytes=64)
-            for u in range(2):
-                nc.tensor.transpose(w_bank[:, u, :], w[:].bitcast(F32)[:, u * P : (u + 1) * P], ident[:])
-            lay(w_bank[:], w_turned[j, g][:], nc.scalar.copy)
-
-        mask(0, 0)
-        vs_chunks = [part[:, c : c + P] for part in (vs_first, vs_last) for c in range(0, part.shape[1], P)]
-        vs_turned = ps.tile([P, P + 2 * (N // P - 1)], F32, name="vs_turned", tag="score01")
-        for c in reversed(range(N // P)):
-            nc.tensor.transpose(vs_turned[:, 2 * c : 2 * c + P], vs_chunks[c], ident[:])
-        lift(0, 0)
-        mask(1, 0)
-        lift(1, 0)
-        mask(0, 1)
-        vs_cols = sb.tile([P, N // P], F32, name="vs_cols", tag="masked00", align_bytes=64)
-        nc.vector.tensor_copy(vs_cols[:], vs_turned[:, LIVE::2])
-        scale_banks = [spread(vs_cols[:, h * CHUNKS : (h + 1) * CHUNKS], f"vs{h}", f"scale{h}") for h in range(SLOT_PASSES)]
-        mask(1, 1)
-        lift(0, 1)
-        lift(1, 1)
-        invert(slice(0, 1))
-        invert(slice(1, 2))
-        values(0, "capped11", "score11")
-        weigh(0, 0, whole)
-        values(1, "masked01", "place0")
-        weigh(0, 1, whole)
-        weigh(1, 0, whole)
-        weigh(1, 1, halves)
-
-        half_sum = sb.tile([P, ROW_TILES], F32, name="half_sum")
-        nc.gpsimd.tensor_scalar(half_sum[:], e_sum[:, 0, :], floor_sum[:], 1.0, ALU.add, ALU.mult)
-        row_sum = sb.tile([P, ROW_TILES], F32, name="row_sum")
-        nc.gpsimd.tensor_tensor(row_sum[:], half_sum[:], e_sum[:, 1, :], ALU.add)
-        inv_sum = sb.tile([P, ROW_TILES], F32, name="inv_sum")
-        nc.vector.reciprocal(inv_sum[:], row_sum[:])
-        inv_row_sum = sb.tile([P, ROW_TILES], F32, name="inv_row_sum")
-        nc.gpsimd.tensor_tensor(inv_row_sum[:], inv_sum[:], stats[:], ALU.mult)
-
-        v_code, v_scale = quantise(v_turned[:], "v", sb.tile([P, N // 4], U32, name="v_code", tag="lifted11", align_bytes=64))
+        v_mx = [quantise(v_turned[g][:], f"v{g}") for g in range(SLOT_PASSES)]
         store_queues = [nc.sync, nc.scalar]
-        acc_tags = ["score00", "score10"]
         for j in range(ROW_TILES):
-            acc = ps.tile([P, DV], F32, name=f"acc{j}", tag=acc_tags[j])
+            acc = ps.tile([P, DV], F32, name=f"acc{j}", tag=f"sum1{j}")
             for g in range(SLOT_PASSES):
-                w_code, w_scale = quantise(w_turned[j, g][:], f"w{j}{g}", sb.tile([P, PASS // 4], U32, name=f"w{j}{g}_code", align_bytes=64))
+                w_code, w_scale = quantise(w[j, g][:].rearrange("p q r -> p (q r)"), f"w{j}{g}")
                 nc.tensor.matmul_mx(
                     out=acc[:],
                     lhsT=w_code[:].bitcast(FP8X4),
                     lhsT_scale=w_scale[:],
-                    rhs=v_code[:, g * DV : (g + 1) * DV].bitcast(FP8X4),
-                    rhs_scale=v_scale[:, g * DV : (g + 1) * DV],
+                    rhs=v_mx[g][0][:].bitcast(FP8X4),
+                    rhs_scale=v_mx[g][1][:],
                     start=(g == 0),
                     stop=(g == SLOT_PASSES - 1),
                 )
             result = sb.tile([P, DV], F32, name=f"result{j}")
-            nc.scalar.activation(result[:], acc[:], ACT.Copy, scale=inv_row_sum[:, j : j + 1])
+            nc.scalar.activation(result[:], acc[:], ACT.Copy, scale=inv_sum[:, j : j + 1])
             store_queues[j].dma_start(out[0, j * P : (j + 1) * P, :], result[:])

@@ -5,7 +5,8 @@ from concourse.masks import make_identity
 
 N, T, D, DV, NQ = 1024, 2048, 1024, 128, 256
 CAP = 2.0
-LOG_PENALTY = 21.0
+LOG_CEILING = 30.0
+PENALTY = 2.0**30
 FLOPS = 2 * NQ * N * (D + DV)
 
 F32 = mybir.dt.float32
@@ -54,7 +55,7 @@ def tile_attend_soft_draft_cap_topkq256n1024t2048_kernel(tc, q_words, q_scales, 
         nc.sync.dma_start(ks_pool[P - QUAD :, :].bitcast(I32), k_scales.rearrange("o f t -> f o t").bitcast(I32))
         pos_pool = sb.tile([P, T], F32, name="pos_pool")
         nc.sync.dma_start(pos_pool[LIVE:, :], pos[0:1, :])
-        q_place = sb.tile([P, ROW_TILES], F32, name="q_place")
+        q_place = sb.tile([P, ROW_TILES], F32, name="q_place", tag="pos_slots1", align_bytes=64)
         with nc.allow_non_contiguous_dma(reason="one place for each query row"):
             nc.sync.dma_start(q_place[:], qpos[0].rearrange("(j p) o -> p (j o)", p=P))
         vs_pool = sb.tile([P, T], F32, name="vs_pool")
@@ -73,13 +74,15 @@ def tile_attend_soft_draft_cap_topkq256n1024t2048_kernel(tc, q_words, q_scales, 
             nc.vector.memset(words[:, :last], 0)
             nc.vector.memset(words[:, last:], 0)
 
-        log_penalty = sb.tile([P, 1], F32, name="log_penalty")
-        nc.vector.memset(log_penalty[:], LOG_PENALTY)
+        log_ceiling = sb.tile([P, 1], F32, name="log_ceiling")
+        nc.vector.memset(log_ceiling[:], LOG_CEILING)
         v_slots = sb.tile([P, N], BF16, name="v_slots", align_bytes=64)
         inv_cap = v_slots[:, QUARTER:].bitcast(F32)[:, 0:1]
         nc.vector.memset(inv_cap, -1.0 / CAP)
         hidden = v_slots[:, 3 * QUARTER :].bitcast(F32)[:, 0:1]
-        nc.scalar.activation(hidden, log_penalty[:], ACT.Exp)
+        nc.vector.memset(hidden, PENALTY)
+        ceiling = sb.tile([P, 1], F32, name="ceiling")
+        nc.scalar.activation(ceiling[:], log_ceiling[:], ACT.Exp)
         zero_words(pos_pool[:LIVE, :ZERO_SPLIT])
         zero_words(ks_pool[: P - QUAD, :].bitcast(I32))
         k_scale = sb.tile([P, D_PASSES * N], U8, name="k_scale", align_bytes=64)
@@ -106,7 +109,7 @@ def tile_attend_soft_draft_cap_topkq256n1024t2048_kernel(tc, q_words, q_scales, 
         for j in range(ROW_TILES):
             nc.tensor.transpose(q_bank[:, j, :], q_place[:, j : j + 1].to_broadcast([P, P]), ident[:])
         q_spread = sb.tile([P, NQ], F32, name="q_spread", tag="q_spread", align_bytes=64)
-        nc.vector.tensor_copy(q_spread[:], q_bank[:].rearrange("p j q -> p (j q)"))
+        nc.scalar.copy(q_spread[:], q_bank[:].rearrange("p j q -> p (j q)"))
 
         pos_banks = []
         for h in range(SLOT_PASSES):
@@ -133,15 +136,18 @@ def tile_attend_soft_draft_cap_topkq256n1024t2048_kernel(tc, q_words, q_scales, 
                 stop=(len(added[j, h]) == 2 * CHUNKS),
             )
 
-        def penalties(h, cols_tag, tag):
-            pos_cols = sb.tile([P, CHUNKS], F32, name=f"pos_cols{h}", tag=cols_tag, align_bytes=64)
+        def place_columns(h, tag):
+            pos_cols = sb.tile([P, CHUNKS], F32, name=f"pos_cols{h}", tag=tag, align_bytes=64)
             nc.vector.tensor_copy(pos_cols[:], pos_banks[h][:, :, LIVE])
+            return pos_cols
+
+        def penalties(h, pos_cols, tag):
             penalty = sb.tile([P, CHUNKS, NQ], F32, name=f"penalty{h}", tag=tag, align_bytes=64)
             for c in range(CHUNKS):
-                nc.vector.tensor_scalar(penalty[:, c, :], q_spread[:], pos_cols[:, c : c + 1], hidden, ALU.is_lt, ALU.mult)
+                nc.vector.tensor_scalar(penalty[:, c, :], q_spread[:], pos_cols[:, c : c + 1], hidden if (h, c) == (1, CHUNKS - 1) else PENALTY, ALU.is_lt, ALU.mult)
             return penalty
 
-        penalty0 = penalties(0, "pos_cols0", "penalty0")
+        penalty0 = penalties(0, place_columns(0, "pos_cols0"), "penalty0")
         for j in range(ROW_TILES):
             for c in range(CHUNKS):
                 add_turned(penalty0[:, c, :], j, 0, c)
@@ -160,8 +166,10 @@ def tile_attend_soft_draft_cap_topkq256n1024t2048_kernel(tc, q_words, q_scales, 
                     gathered[a][:].bitcast(U16).rearrange("p (b n o) -> p b o n", b=2, o=D_PASSES),
                 )
                 k_code.append(parted)
+                if (h, a) == (1, 0):
+                    late_cols = place_columns(1, "kw_slots0")
 
-        penalty1 = penalties(1, "kw_slots0", "kw_slots1")
+        penalty1 = penalties(1, late_cols, "kw_slots1")
 
         capped = []
         for k in range(2 * SLOT_PASSES):
@@ -208,7 +216,7 @@ def tile_attend_soft_draft_cap_topkq256n1024t2048_kernel(tc, q_words, q_scales, 
             for h in range(SLOT_PASSES):
                 lowered[j, h] = sb.tile([P, PACK, P], F32, name=f"lowered{j}{h}", tag=f"lowered{j}{h}", align_bytes=64)
                 nc.vector.tensor_scalar(
-                    lowered[j, h][:], sums[j, h][:].rearrange("p (k r) -> p r k", r=PACK), CAP, least[:, j, 0:1] if h else None, ALU.mult, ALU.min, accum_out=least[:, j, h : h + 1]
+                    lowered[j, h][:], sums[j, h][:].rearrange("p (k r) -> p r k", r=PACK), CAP, least[:, j, 0:1] if h else ceiling[:], ALU.mult, ALU.min, accum_out=least[:, j, h : h + 1]
                 )
 
         v_turned = {}
@@ -222,13 +230,17 @@ def tile_attend_soft_draft_cap_topkq256n1024t2048_kernel(tc, q_words, q_scales, 
 
         values(1, "sum00", "v_turned1")
 
-        p_sum = sb.tile([P, SLOT_PASSES, ROW_TILES], F32, name="p_sum")
+        p_sum = sb.tile([P, SLOT_PASSES + 1, ROW_TILES], F32, name="p_sum")
         p_tags = {(0, 0): "score0", (0, 1): "score1", (1, 0): "early", (1, 1): "late"}
         w = {}
         for j in range(ROW_TILES):
             for g in range(SLOT_PASSES):
                 prob = sb.tile([P, PACK, P], F32, name=f"prob{j}{g}")
-                nc.scalar.activation(prob[:], lowered[j, g][:], ACT.Exp, scale=-1.0, bias=least[:, j, 1:2], accum_out=p_sum[:, g, j : j + 1])
+                if j + g == 2:
+                    for u in range(2):
+                        nc.scalar.activation(prob[:, 2 * u : 2 * u + 2, :], lowered[j, g][:, 2 * u : 2 * u + 2, :], ACT.Exp, scale=-1.0, bias=least[:, j, 1:2], accum_out=p_sum[:, g + u, j : j + 1])
+                else:
+                    nc.scalar.activation(prob[:], lowered[j, g][:], ACT.Exp, scale=-1.0, bias=least[:, j, 1:2], accum_out=p_sum[:, g, j : j + 1])
                 p_bank = ps.tile([P, PACK, P], F32, name=f"p_bank{j}{g}", tag=p_tags[j, g])
                 for r in range(PACK):
                     nc.tensor.transpose(p_bank[:, r, :], prob[:, r, :], ident[:])
@@ -239,6 +251,7 @@ def tile_attend_soft_draft_cap_topkq256n1024t2048_kernel(tc, q_words, q_scales, 
 
         row_sum = sb.tile([P, ROW_TILES], F32, name="row_sum")
         nc.gpsimd.tensor_tensor(row_sum[:], p_sum[:, 0, :], p_sum[:, 1, :], ALU.add)
+        nc.gpsimd.tensor_tensor(row_sum[:, 1:2], row_sum[:, 1:2], p_sum[:, 2, 1:2], ALU.add)
         inv_sum = sb.tile([P, ROW_TILES], F32, name="inv_sum")
         nc.vector.reciprocal(inv_sum[:], row_sum[:])
 

@@ -221,14 +221,14 @@ def tile_attend_soft_draft_cap_topkq256n1024t2048_kernel(tc, q_words, q_scales, 
 
         v_turned = {}
 
-        def values(g, bank_tag, turned_tag):
+        def values(g, bank_tag, turned_tag, copy_out):
             v_turned[g] = sb.tile([P, PASS], BF16, name=f"v_turned{g}", tag=turned_tag, align_bytes=64)
             v_bank = ps.tile([P, 2, DV], F32, name=f"v_bank{g}", tag=bank_tag)
             for u in range(2):
                 nc.tensor.transpose(v_bank[:, u, :], v_slots[:, g * PASS : (g + 1) * PASS].bitcast(F32)[:, u::2], ident[:])
-            nc.scalar.copy(v_turned[g][:].bitcast(F32).rearrange("p (c u) -> p c u", u=2), v_bank[:].rearrange("p u c -> p c u"))
+            copy_out(v_turned[g][:].bitcast(F32).rearrange("p (c u) -> p c u", u=2), v_bank[:].rearrange("p u c -> p c u"))
 
-        values(1, "sum00", "v_turned1")
+        values(1, "sum00", "v_turned1", nc.vector.tensor_copy)
 
         p_sum = sb.tile([P, SLOT_PASSES + 1, ROW_TILES], F32, name="p_sum")
         p_tags = {(0, 0): "score0", (0, 1): "score1", (1, 0): "early", (1, 1): "late"}
@@ -247,7 +247,7 @@ def tile_attend_soft_draft_cap_topkq256n1024t2048_kernel(tc, q_words, q_scales, 
                 w[j, g] = sb.tile([P, P, PACK], BF16, name=f"w{j}{g}", align_bytes=64)
                 nc.vector.tensor_tensor(w[j, g][:], p_bank[:].rearrange("p r q -> p q r"), vs_cols[g][:].to_broadcast([P, P, PACK]), ALU.mult)
 
-        values(0, "sum01", "lowered11")
+        values(0, "sum01", "lowered11", nc.scalar.copy)
 
         row_sum = sb.tile([P, ROW_TILES], F32, name="row_sum")
         nc.gpsimd.tensor_tensor(row_sum[:], p_sum[:, 0, :], p_sum[:, 1, :], ALU.add)

from contextlib import ExitStack

import concourse.mybir as mybir
from concourse.masks import make_identity

N, T, D, DV, NQ = 1024, 2048, 1024, 128, 256
CAP = 2.0
LOG_CEILING = 30.0
PENALTY = 2.0**30
FLOPS = 2 * NQ * N * (D + DV)

F32 = mybir.dt.float32
BF16 = mybir.dt.bfloat16
I32 = mybir.dt.int32
U32 = mybir.dt.uint32
U16 = mybir.dt.uint16
U8 = mybir.dt.uint8
FP8X4 = mybir.dt.float8_e4m3fn_x4
FP4X4 = mybir.dt.float4_e2m1fn_x4
ACT = mybir.ActivationFunctionType
ALU = mybir.AluOpType

P = 128
PASS = 512
PACK = 4
QUAD = 32
LIST_ROWS = 16
D_PASSES = D // PASS
SLOT_PASSES = N // PASS
ROW_TILES = NQ // P
CHUNKS = PASS // P
QUARTER = PASS // 2
LIVE = P - 1
ZERO_SPLIT = 1024


def tile_attend_soft_draft_cap_topkq256n1024t2048_kernel(tc, q_words, q_scales, k_words, k_scales, vT, vs, pos, qpos, offs, out):
    nc = tc.nc
    with ExitStack() as ctx:
        sb = ctx.enter_context(tc.tile_pool(name="sb", bufs=1))
        ps = ctx.enter_context(tc.psum_pool(name="ps", bufs=1))

        q_scale = sb.tile([P, D_PASSES * NQ], U8, name="q_scale", align_bytes=64)
        nc.gpsimd.memset(q_scale[:].bitcast(I32), 0)

        def load_query_scales(quad):
            nc.sync.dma_start(
                q_scale[QUAD * quad : QUAD * quad + 4, :].rearrange("p (o q) -> p o q", o=D_PASSES).bitcast(I32),
                q_scales[0, :, 4 * quad : 4 * quad + 4, :].rearrange("o f q -> f o q").bitcast(I32),
            )

        offsets = sb.tile([P, N // LIST_ROWS], U16, name="offsets")
        nc.sync.dma_start(offsets[:], offs)
        ks_pool = sb.tile([P, T], U8, name="ks_pool", tag="ks_pool", align_bytes=64)
        nc.sync.dma_start(ks_pool[P - QUAD :, :].bitcast(I32), k_scales.rearrange("o f t -> f o t").bitcast(I32))
        pos_pool = sb.tile([P, T], F32, name="pos_pool")
        nc.sync.dma_start(pos_pool[LIVE:, :], pos[0:1, :])
        q_place = sb.tile([P, ROW_TILES], F32, name="q_place", tag="pos_slots1", align_bytes=64)
        with nc.allow_non_contiguous_dma(reason="one place for each query row"):
            nc.sync.dma_start(q_place[:], qpos[0].rearrange("(j p) o -> p (j o)", p=P))
        vs_pool = sb.tile([P, T], F32, name="vs_pool")
        nc.sync.dma_start(vs_pool[LIVE:, :], vs[0:1, :])
        load_query_scales(0)
        load_query_scales(1)
        kw_pool = sb.tile([P, T], I32, name="kw_pool", align_bytes=64)
        nc.sync.dma_start(kw_pool[:], k_words[0].rearrange("p t b -> p (t b)").bitcast(I32))
        q_code = sb.tile([P, D_PASSES, NQ], I32, name="q_code", align_bytes=64)
        nc.sync.dma_start(q_code[:], q_words[0].rearrange("o p q r -> p o (q r)").bitcast(I32))
        load_query_scales(2)
        load_query_scales(3)

        def zero_words(words):
            last = words.shape[1] - 1
            nc.vector.memset(words[:, :last], 0)
            nc.vector.memset(words[:, last:], 0)

        log_ceiling = sb.tile([P, 1], F32, name="log_ceiling")
        nc.vector.memset(log_ceiling[:], LOG_CEILING)
        v_slots = sb.tile([P, N], BF16, name="v_slots", align_bytes=64)
        inv_cap = v_slots[:, QUARTER:].bitcast(F32)[:, 0:1]
        nc.vector.memset(inv_cap, -1.0 / CAP)
        hidden = v_slots[:, 3 * QUARTER :].bitcast(F32)[:, 0:1]
        nc.vector.memset(hidden, PENALTY)
        ceiling = sb.tile([P, 1], F32, name="ceiling")
        nc.scalar.activation(ceiling[:], log_ceiling[:], ACT.Exp)
        zero_words(pos_pool[:LIVE, :ZERO_SPLIT])
        zero_words(ks_pool[: P - QUAD, :].bitcast(I32))
        k_scale = sb.tile([P, D_PASSES * N], U8, name="k_scale", align_bytes=64)
        zero_words(k_scale[:].bitcast(I32))
        ident = sb.tile([P, P], F32, name="ident")
        make_identity(nc, ident[:])
        nc.gpsimd.memset(pos_pool[:LIVE, ZERO_SPLIT:], 0.0)
        nc.gpsimd.memset(vs_pool[:LIVE, :], 0.0)

        def entries(first, count):
            return offsets[:, first // LIST_ROWS : (first + count) // LIST_ROWS]

        ks_slots = sb.tile([P, N], U8, name="ks_slots", tag="after_scale_moves", align_bytes=64)
        nc.vector.tensor_copy(ks_slots[:], ks_pool[:].indirect(offsets[:]))
        for quad in range(P // QUAD):
            nc.sync.dma_start(
                k_scale[QUAD * quad : QUAD * quad + 4, :].bitcast(I32),
                ks_slots[P - QUAD + 8 * quad : P - QUAD + 8 * quad + 8, :].bitcast(I32),
            )
        v_pool = sb.tile([P, T], F32, name="v_pool", tag="ks_pool", align_bytes=64)
        nc.sync.dma_start(v_pool[:], vT)

        q_bank = ps.tile([P, ROW_TILES, P], F32, name="q_bank", tag="early")
        for j in range(ROW_TILES):
            nc.tensor.transpose(q_bank[:, j, :], q_place[:, j : j + 1].to_broadcast([P, P]), ident[:])
        q_spread = sb.tile([P, NQ], F32, name="q_spread", tag="q_spread", align_bytes=64)
        nc.scalar.copy(q_spread[:], q_bank[:].rearrange("p j q -> p (j q)"))

        pos_banks = []
        for h in range(SLOT_PASSES):
            pos_slots = sb.tile([P, PASS], F32, name=f"pos_slots{h}", tag=f"pos_slots{h}", align_bytes=64)
            nc.scalar.activation(pos_slots[:], pos_pool[:].indirect(entries(h * PASS, PASS)), ACT.Copy)
            pos_banks.append(ps.tile([P, CHUNKS, P], F32, name=f"pos_bank{h}", tag=("score0", "late")[h]))
            for c in range(CHUNKS):
                nc.tensor.transpose(pos_banks[h][:, c, :], pos_slots[:, c * P : (c + 1) * P], ident[:])

        vs_slots = sb.tile([P, N], F32, name="vs_slots")
        nc.scalar.activation(vs_slots[:], vs_pool[:].indirect(offsets[:]), ACT.Copy)

        sums = {(j, h): ps.tile([P, PASS], F32, name=f"sum{j}{h}") for j in range(ROW_TILES) for h in range(SLOT_PASSES)}
        added = {key: [] for key in sums}

        def add_turned(src, j, h, c):
            added[j, h].append(c)
            nc.tensor.matmul(
                sums[j, h][:, c * P : (c + 1) * P],
                lhsT=src[:, j * P : (j + 1) * P],
                rhs=ident[:],
                is_transpose=True,
                start=(len(added[j, h]) == 1),
                stop=(len(added[j, h]) == 2 * CHUNKS),
            )

        def place_columns(h, tag):
            pos_cols = sb.tile([P, CHUNKS], F32, name=f"pos_cols{h}", tag=tag, align_bytes=64)
            nc.vector.tensor_copy(pos_cols[:], pos_banks[h][:, :, LIVE])
            return pos_cols

        def penalties(h, pos_cols, tag):
            penalty = sb.tile([P, CHUNKS, NQ], F32, name=f"penalty{h}", tag=tag, align_bytes=64)
            for c in range(CHUNKS):
                nc.vector.tensor_scalar(penalty[:, c, :], q_spread[:], pos_cols[:, c : c + 1], hidden if (h, c) == (1, CHUNKS - 1) else PENALTY, ALU.is_lt, ALU.mult)
            return penalty

        penalty0 = penalties(0, place_columns(0, "pos_cols0"), "penalty0")
        for j in range(ROW_TILES):
            for c in range(CHUNKS):
                add_turned(penalty0[:, c, :], j, 0, c)

        k_code = []
        for h in range(SLOT_PASSES):
            gathered = []
            for a in range(2):
                kw_slots = sb.tile([P, QUARTER], U32, name=f"kw_slots{h}{a}", tag=f"kw_slots{a}", align_bytes=64)
                nc.vector.tensor_copy(kw_slots[:], kw_pool[:].bitcast(U32).indirect(entries((2 * h + a) * QUARTER, QUARTER)))
                gathered.append(kw_slots)
            for a in range(2):
                parted = sb.tile([P, D_PASSES, QUARTER], U16, name=f"k_code{h}{a}", tag=f"k_code{h}{a}", align_bytes=64)
                nc.vector.tensor_copy(
                    parted[:].rearrange("p o (b n) -> p b o n", b=2),
                    gathered[a][:].bitcast(U16).rearrange("p (b n o) -> p b o n", b=2, o=D_PASSES),
                )
                k_code.append(parted)
                if (h, a) == (1, 0):
                    late_cols = place_columns(1, "kw_slots0")

        penalty1 = penalties(1, late_cols, "kw_slots1")

        capped = []
        for k in range(2 * SLOT_PASSES):
            h, a = divmod(k, 2)
            score = ps.tile([P, 2, NQ], F32, name=f"score{k}", tag=("score0", "score1", "early", "late")[k])
            for i in range(2):
                first = (2 * k + i) * P
                for o in range(D_PASSES):
                    nc.tensor.matmul_mx(
                        out=score[:, i, :],
                        lhsT=k_code[k][:, o, i * P : (i + 1) * P].bitcast(FP4X4),
                        lhsT_scale=k_scale[:, o * N + first : o * N + first + P],
                        rhs=q_code[:, o, :].bitcast(FP8X4),
                        rhs_scale=q_scale[:, o * NQ : (o + 1) * NQ],
                        start=(o == 0),
                        stop=(o == D_PASSES - 1),
                    )
            capped.append(sb.tile([P, 2, NQ], F32, name=f"capped{k}", tag=f"capped{k}", align_bytes=64))
            last = k == 2 * SLOT_PASSES - 1
            for cols in [slice(0, P), slice(P, NQ)] if last else [slice(0, NQ)]:
                nc.scalar.activation(capped[k][:, :, cols], score[:, :, cols], ACT.Tanh, scale=inv_cap)
        for j in range(ROW_TILES):
            for c in range(CHUNKS):
                add_turned(capped[c // 2][:, c % 2, :], j, 0, c)
            for i in range(2):
                add_turned(capped[2][:, i, :], j, 1, i)
            for c in range(CHUNKS):
                add_turned(penalty1[:, c, :], j, 1, c)
            for i in range(2):
                add_turned(capped[3][:, i, :], j, 1, 2 + i)

        vs_cols = []
        for g in range(SLOT_PASSES):
            vs_cols.append(sb.tile([P, 1, PACK], F32, name=f"vs_cols{g}", tag=f"k_code0{g}", align_bytes=64))
            nc.sync.dma_start(vs_cols[g][:, 0, :], vs_slots[LIVE:, g * PASS : (g + 1) * PASS].rearrange("o (p r) -> o p r", r=PACK))

        nc.scalar.activation(v_slots[:, :QUARTER], v_pool[:].indirect(entries(0, QUARTER)), ACT.Copy)
        nc.vector.tensor_copy(v_slots[:, 3 * QUARTER :], v_pool[:].indirect(entries(3 * QUARTER, QUARTER)))
        nc.scalar.activation(v_slots[:, QUARTER : 3 * QUARTER], v_pool[:].indirect(entries(QUARTER, PASS)), ACT.Copy)

        least = sb.tile([P, ROW_TILES, SLOT_PASSES], F32, name="least")
        lowered = {}
        for j in range(ROW_TILES):
            for h in range(SLOT_PASSES):
                lowered[j, h] = sb.tile([P, PACK, P], F32, name=f"lowered{j}{h}", tag=f"lowered{j}{h}", align_bytes=64)
                nc.vector.tensor_scalar(
                    lowered[j, h][:], sums[j, h][:].rearrange("p (k r) -> p r k", r=PACK), CAP, least[:, j, 0:1] if h else ceiling[:], ALU.mult, ALU.min, accum_out=least[:, j, h : h + 1]
                )

        v_turned = {}

        def values(g, bank_tag, turned_tag, copy_out):
            v_turned[g] = sb.tile([P, PASS], BF16, name=f"v_turned{g}", tag=turned_tag, align_bytes=64)
            v_bank = ps.tile([P, 2, DV], F32, name=f"v_bank{g}", tag=bank_tag)
            for u in range(2):
                nc.tensor.transpose(v_bank[:, u, :], v_slots[:, g * PASS : (g + 1) * PASS].bitcast(F32)[:, u::2], ident[:])
            copy_out(v_turned[g][:].bitcast(F32).rearrange("p (c u) -> p c u", u=2), v_bank[:].rearrange("p u c -> p c u"))

        values(1, "sum00", "v_turned1", nc.vector.tensor_copy)

        p_sum = sb.tile([P, SLOT_PASSES + 1, ROW_TILES], F32, name="p_sum")
        p_tags = {(0, 0): "score0", (0, 1): "score1", (1, 0): "early", (1, 1): "late"}
        w = {}
        for j in range(ROW_TILES):
            for g in range(SLOT_PASSES):
                prob = sb.tile([P, PACK, P], F32, name=f"prob{j}{g}")
                if j + g == 2:
                    for u in range(2):
                        nc.scalar.activation(prob[:, 2 * u : 2 * u + 2, :], lowered[j, g][:, 2 * u : 2 * u + 2, :], ACT.Exp, scale=-1.0, bias=least[:, j, 1:2], accum_out=p_sum[:, g + u, j : j + 1])
                else:
                    nc.scalar.activation(prob[:], lowered[j, g][:], ACT.Exp, scale=-1.0, bias=least[:, j, 1:2], accum_out=p_sum[:, g, j : j + 1])
                p_bank = ps.tile([P, PACK, P], F32, name=f"p_bank{j}{g}", tag=p_tags[j, g])
                for r in range(PACK):
                    nc.tensor.transpose(p_bank[:, r, :], prob[:, r, :], ident[:])
                w[j, g] = sb.tile([P, P, PACK], BF16, name=f"w{j}{g}", align_bytes=64)
                nc.vector.tensor_tensor(w[j, g][:], p_bank[:].rearrange("p r q -> p q r"), vs_cols[g][:].to_broadcast([P, P, PACK]), ALU.mult)

        values(0, "sum01", "lowered11", nc.scalar.copy)

        row_sum = sb.tile([P, ROW_TILES], F32, name="row_sum")
        nc.gpsimd.tensor_tensor(row_sum[:], p_sum[:, 0, :], p_sum[:, 1, :], ALU.add)
        nc.gpsimd.tensor_tensor(row_sum[:, 1:2], row_sum[:, 1:2], p_sum[:, 2, 1:2], ALU.add)
        inv_sum = sb.tile([P, ROW_TILES], F32, name="inv_sum")
        nc.vector.reciprocal(inv_sum[:], row_sum[:])


        def quantise(src, name):
            codes = sb.tile([P, P], U32, name=name + "_code", align_bytes=64)
            scales = sb.tile([P, P], U8, name=name + "_scale", align_bytes=64)
            nc.vector.quantize_mx(out=codes[:].bitcast(FP8X4), scales=scales[:], in_=src)
            return codes, scales

        v_mx = [quantise(v_turned[g][:], f"v{g}") for g in range(SLOT_PASSES)]
        store_queues = [nc.sync, nc.scalar]
        for j in range(ROW_TILES):
            acc = ps.tile([P, DV], F32, name=f"acc{j}", tag=f"sum1{j}")
            for g in range(SLOT_PASSES):
                w_code, w_scale = quantise(w[j, g][:].rearrange("p q r -> p (q r)"), f"w{j}{g}")
                nc.tensor.matmul_mx(
                    out=acc[:],
                    lhsT=w_code[:].bitcast(FP8X4),
                    lhsT_scale=w_scale[:],
                    rhs=v_mx[g][0][:].bitcast(FP8X4),
                    rhs_scale=v_mx[g][1][:],
                    start=(g == 0),
                    stop=(g == SLOT_PASSES - 1),
                )
            result = sb.tile([P, DV], F32, name=f"result{j}")
            nc.scalar.activation(result[:], acc[:], ACT.Copy, scale=inv_sum[:, j : j + 1])
            store_queues[j].dma_start(out[0, j * P : (j + 1) * P, :], result[:])
